import numpy as np
import ml_dtypes


def mxq(x, axis, fmt="e4m3"):
    dtype, down = {"e4m3": (ml_dtypes.float8_e4m3fn, 7), "e5m2": (ml_dtypes.float8_e5m2, 14)}[fmt]
    v = np.moveaxis(np.asarray(x, np.float32).astype(ml_dtypes.bfloat16).astype(np.float64), axis, -1)
    blocks = v.reshape(v.shape[:-1] + (-1, 32))
    amax = np.abs(blocks).max(-1, keepdims=True)
    byte = np.maximum(np.where(amax > 0, np.frexp(amax)[1] - 1 + 127, 0) - down, 1)
    scale = np.exp2(byte - 127.0)
    codes = (blocks / scale).astype(np.float32).astype(dtype).astype(np.float64)
    return np.moveaxis((codes * scale).reshape(v.shape), -1, axis)


WIDE = False


def mx_kscale(k):
    if not WIDE:
        return np.ones(k)
    levels = np.array([24, -24, 12, -12, 0])
    if k % 512:
        return np.exp2(np.random.permutation(np.resize(levels, k // 32))).repeat(32)
    a = np.empty((k // 512, 16))
    for p in range(k // 512):
        a[p, :8] = np.random.permutation(np.resize(levels, 8))
        for g in range(8):
            far = levels[np.abs(levels - a[p, g]) >= 10]
            a[p, g + 8] = far[np.random.randint(len(far))]
    return np.exp2(a.ravel()).repeat(32)


def f64(x):
    return np.asarray(x).astype(np.float64)


def striped(idx):
    return np.tile(idx.reshape(-1, 16).T, (8, 1)).astype(np.uint16)


def unstriped(offs):
    return offs[:16].T.reshape(-1).astype(np.int64)


E2M1 = np.array([0.0, 0.5, 1.0, 1.5, 2.0, 3.0, 4.0, 6.0, -0.0, -0.5, -1.0, -1.5, -2.0, -3.0, -4.0, -6.0])


def pack_weight(w, fmt):
    k, n = w.shape
    w = f64(np.asarray(w, np.float32).astype(ml_dtypes.bfloat16)).reshape(k // 32, 32, n)
    amax = np.abs(w).max(1)
    if fmt == "e4m3":
        byte = np.frexp(amax)[1] - 1 + 127 - 7
    else:
        mant, ex = np.frexp(amax / 6.0)
        byte = np.where(mant > 0.5, ex, ex - 1) + 127
    byte = np.clip(np.where(amax > 0, byte, 1), 1, 254)
    scaled = (w * np.exp2(127.0 - byte)[:, None, :]).reshape(k, n).astype(np.float32)
    by_word = np.ascontiguousarray(scaled.reshape(k // 512, 128, 4, n).transpose(0, 1, 3, 2))
    if fmt == "e4m3":
        words = by_word.astype(ml_dtypes.float8_e4m3fn).view(np.uint8)
    else:
        c = by_word.astype(ml_dtypes.float4_e2m1fn).view(np.uint8) & 0xF
        words = (c[..., 0::2] | (c[..., 1::2] << 4)).reshape(k // 512, 128, 2 * n)
    return np.ascontiguousarray(words), np.ascontiguousarray(byte.astype(np.uint8).reshape(k // 512, 16, n))


def unpack_weight(words, scales, fmt):
    g, _, n = scales.shape
    words = np.ascontiguousarray(words).reshape(g, 128, n, -1)
    if fmt == "e4m3":
        vals = words.view(ml_dtypes.float8_e4m3fn).astype(np.float64)
    else:
        nib = np.empty((g, 128, n, 4), np.uint8)
        nib[..., 0::2] = words & 0xF
        nib[..., 1::2] = words >> 4
        vals = E2M1[nib]
    vals = vals * np.repeat(np.exp2(scales.astype(np.float64) - 127.0), 8, axis=1)[..., None]
    return vals.transpose(0, 1, 3, 2).reshape(g * 512, n)


def pack_table4(v):
    words, scales = pack_weight(v, "e2m1")
    g, t = words.shape[0] // 2, v.shape[1]
    return np.ascontiguousarray(words.reshape(g, 2, 128, t, 2).transpose(0, 2, 3, 1, 4).reshape(g, 128, t, 4)), scales


def unpack_table4(words, scales):
    g, _, t, _ = words.shape
    return unpack_weight(words.reshape(g, 128, t, 2, 2).transpose(0, 3, 1, 2, 4).reshape(2 * g, 128, 2 * t), scales, "e2m1")


def planes(y):
    n, m = y.shape
    v = y.astype(np.float32).astype(ml_dtypes.bfloat16).astype(np.float64).reshape(n // 32, 32, m)
    top = np.abs(v).max(1)
    byte = np.clip(np.where(top > 0, np.frexp(top)[1] - 1 + 127 - 7, 1), 1, 254)
    codes = (v * np.exp2(127.0 - byte)[:, None, :]).reshape(n, m).astype(np.float32).astype(ml_dtypes.float8_e4m3fn).view(np.uint8)
    words = codes.reshape(n // 512, 128, 4, m).transpose(0, 1, 3, 2)
    return np.ascontiguousarray(words), np.ascontiguousarray(byte.astype(np.uint8).reshape(n // 512, 16, m))


def sigm(f):
    return 1.0 / (1.0 + np.exp(-np.maximum(f, -700.0)))


K, N, T, J = 1024, 512, 2048, 1024


def setup_inputs():
    n = np.random.standard_normal
    s = mx_kscale(K)[:, None]
    p_tab = pack_table4(n((K, T)) * s)
    p_wa = pack_weight(n((K, N)) / np.sqrt(2 * K) / s, "e2m1")
    p_wb = pack_weight(n((K, N)) / np.sqrt(2 * K) / s, "e4m3")
    return {
        "tab_words": p_tab[0],
        "tab_scales": p_tab[1],
        "wa_words": p_wa[0],
        "wa_scales": p_wa[1],
        "wb_words": p_wb[0],
        "wb_scales": p_wb[1],
        "wc": (n((K, N)) / np.sqrt(K) / s).astype(np.float32),
        "wgo": np.tile(np.random.uniform(0.5, 2.0, J), (128, 1)).astype(np.float32),
        "offs": striped(np.random.permutation(T)[:J]),
        "offs2": striped(np.random.permutation(T)[:J]),
    }


def reference(tab_words, tab_scales, wa_words, wa_scales, wb_words, wb_scales, wc, wgo, offs, offs2):
    idx = unstriped(offs)
    idx2 = unstriped(offs2)
    tab_ = unpack_table4(tab_words, tab_scales)[:, idx]
    tabb_ = unpack_table4(tab_words, tab_scales)[:, idx2]
    wa_ = unpack_weight(wa_words, wa_scales, "e2m1")
    wb_ = unpack_weight(wb_words, wb_scales, "e4m3")
    za = wa_.T @ tabb_ + wb_.T @ tab_
    eta = sigm(za)
    wc_ = mxq(f64(wc), 0, "e4m3")
    ms = wc_.T @ tab_
    out = np.zeros((N, T))
    out[:, idx2] = f64(wgo)[0] * (np.maximum(eta * ms, 0.0))
    return (out,) + planes(out)

@@ -1,0 +1,189 @@
+from contextlib import ExitStack
+
+import concourse.mybir as mybir
+
+K, N, T, J = 1024, 512, 2048, 1024
+FLOPS = 3 * 2 * K * N * J
+
+F32 = mybir.dt.float32
+BF16 = mybir.dt.bfloat16
+I32 = mybir.dt.int32
+U32 = mybir.dt.uint32
+U16 = mybir.dt.uint16
+U8 = mybir.dt.uint8
+FP8X4 = mybir.dt.float8_e4m3fn_x4
+FP4X4 = mybir.dt.float4_e2m1fn_x4
+ALU = mybir.AluOpType
+ACT = mybir.ActivationFunctionType
+
+P = 128
+PACK = 4
+PASSES = K // (P * PACK)
+HALF = 512
+HALVES = J // HALF
+CHUNK = 512
+CHUNKS = T // CHUNK
+SHIFT_ROWS = 112
+
+
+def tile_list_rgg_reluP_kernel(
+    tc, tab_words, tab_scales, wa_words, wa_scales, wb_words, wb_scales, wc, wgo, offs, offs2, out_0, out_1, out_2
+):
+    nc = tc.nc
+    with ExitStack() as ctx:
+        keep = ctx.enter_context(tc.tile_pool(name="keep", bufs=1))
+        ring = ctx.enter_context(tc.tile_pool(name="ring", bufs=3))
+        psum = ctx.enter_context(tc.psum_pool(name="psum", bufs=4))
+
+        def held(name, shape, dtype, tag=None):
+            return keep.tile(shape, dtype, name=name, tag=tag or name, align_bytes=64)
+
+        src_list = keep.tile([P, J // 16], U16, name="src_list")
+        dst_list = keep.tile([P, J // 16], U16, name="dst_list")
+        tab_s = held("tab_s", [P, T], U8)
+        w_s_raw = held("w_s_raw", [P, 2 * PASSES, N], U8)
+        nc.vector.memset(tab_s[:].bitcast(I32), 0)
+        nc.gpsimd.memset(w_s_raw[:].rearrange("p a n -> p (a n)").bitcast(I32), 0)
+        pages = [held("page%d" % t, [P, T], F32) for t in range(2)]
+        for t in range(2):
+            nc.vector.memset(pages[t][:].bitcast(I32), 0)
+
+        nc.sync.dma_start(src_list[:], offs)
+        nc.sync.dma_start(dst_list[:], offs2)
+        for q in range(4):
+            nc.sync.dma_start(tab_s[32 * q : 32 * q + 8, :].bitcast(I32), tab_scales[:, 4 * q : 4 * q + 4, :].bitcast(I32))
+        wa_raw = held("wa_raw", [P, PASSES, 2 * N], U8)
+        nc.sync.dma_start(wa_raw[:].bitcast(I32), wa_words.rearrange("a p b -> p a b").bitcast(I32))
+        wc_raw = [held("wc_raw%d" % a, [P, PACK, N], F32) for a in range(PASSES)]
+        wc_rows = wc.rearrange("(a p i) n -> a p i n", p=P, i=PACK)
+        nc.sync.dma_start(wc_raw[0][:], wc_rows[0])
+        tab_w = held("tab_w", [P, T], I32)
+        nc.sync.dma_start(tab_w[:], tab_words[0].rearrange("p t b -> p (t b)").bitcast(I32))
+        for w, scales in enumerate((wa_scales, wb_scales)):
+            for q in range(4):
+                nc.gpsimd.dma_start(
+                    w_s_raw[32 * q : 32 * q + 4, PASSES * w : PASSES * (w + 1), :].bitcast(I32),
+                    scales[:, 4 * q : 4 * q + 4, :].rearrange("a r n -> r a n").bitcast(I32),
+                )
+        nc.sync.dma_start(wc_raw[1][:], wc_rows[1])
+        wb_raw = held("wb_raw", [P, PASSES, N], I32)
+        nc.sync.dma_start(wb_raw[:], wb_words.rearrange("a p n b -> p a (n b)").bitcast(I32))
+        gain = held("gain", [P, J], F32)
+        nc.sync.dma_start(gain[:], wgo)
+
+        lists = (src_list, dst_list)
+        picked_s = []
+        for l in range(2):
+            both = held("picked_s%d" % l, [P, J], U8)
+            nc.vector.tensor_copy(both[:], tab_s[:].indirect(lists[l][:]))
+            second = held("shifted_s%d" % l, [P, J], U8)
+            nc.gpsimd.dma_start(second[0:SHIFT_ROWS, :].bitcast(I32), both[4 : 4 + SHIFT_ROWS, :].bitcast(I32))
+            picked_s.append((both, second))
+
+        parted = {}
+        after = {(0, 1): "wb_raw", (1, 1): "wc_grouped1"}
+
+        def pick_words(h):
+            for l in range(2):
+                words = held("picked_w%d_%d" % (l, h), [P, HALF], I32, tag=after.get((l, h)))
+                cols = slice(h * HALF // 16, (h + 1) * HALF // 16)
+                nc.vector.tensor_copy(words[:].bitcast(U32), tab_w[:].bitcast(U32).indirect(lists[l][:, cols]))
+                parted[l, h] = (words, held("parted%d_%d" % (l, h), [P, PASSES, 2 * HALF], U8))
+            for l in range(2):
+                words, apart = parted[l, h]
+                nc.vector.tensor_copy(
+                    apart[:].bitcast(U16),
+                    words[:].bitcast(U16).rearrange("p (j a) -> p a j", a=PASSES),
+                )
+
+        wc_codes = held("wc_codes", [P, PASSES, N], U32)
+        wc_s = held("wc_s", [P, PASSES, N], U8)
+
+        def quantise_wc(a):
+            grouped = held("wc_grouped%d" % a, [P, N * PACK], BF16)
+            nc.scalar.copy(
+                grouped[:].rearrange("p (t m i) -> p m t i", t=PACK, i=PACK),
+                wc_raw[a][:].rearrange("p i (m t) -> p m t i", t=PACK),
+            )
+            nc.vector.quantize_mx(out=wc_codes[:, a, :].bitcast(FP8X4), scales=wc_s[:, a, :], in_=grouped[:])
+
+        pick_words(0)
+        quantise_wc(0)
+        w_s = held("w_s", [P, 2 * PASSES, N], U8)
+        nc.vector.tensor_copy(
+            w_s[:].rearrange("p a (t o i) -> p a o t i", t=PACK, i=16),
+            w_s_raw[:].rearrange("p a (o i t) -> p a o t i", t=PACK, i=16),
+        )
+        wb_codes = held("wb_codes", [P, PASSES, N], I32)
+        nc.vector.tensor_copy(
+            wb_codes[:].rearrange("p a (t o i) -> p a o t i", t=PACK, i=4),
+            wb_raw[:].rearrange("p a (o i t) -> p a o t i", t=PACK, i=4),
+        )
+        wa_codes = held("wa_codes", [P, PASSES, 2 * N], U8)
+        nc.vector.tensor_copy(
+            wa_codes[:].bitcast(U16).rearrange("p a (t o i) -> p a o t i", t=PACK, i=8),
+            wa_raw[:].bitcast(U16).rearrange("p a (o i t) -> p a o t i", t=PACK, i=8),
+        )
+        quantise_wc(1)
+        pick_words(1)
+        for t, tag in ((2, "wb_raw"), (3, "wc_grouped1")):
+            pages.append(held("page%d" % t, [P, T], F32, tag=tag))
+            nc.gpsimd.memset(pages[t][:], 0.0)
+
+        def table_operand(l, h, a):
+            cols = slice(h * HALF, (h + 1) * HALF)
+            return parted[l, h][1][:, a, :].bitcast(FP4X4), picked_s[l][a][:, cols]
+
+        rounded = [held("rounded%d" % c, [P, CHUNK, PACK], BF16) for c in range(CHUNKS)]
+        out_rows = out_0.rearrange("(p t) c -> p t c", t=PACK)
+
+        for t in range(PACK):
+            m = slice(t * P, (t + 1) * P)
+            for h in range(HALVES):
+                za = psum.tile([P, HALF], F32, name="za")
+                ms = psum.tile([P, HALF], F32, name="ms")
+                for a in range(PASSES):
+                    v, v_s = table_operand(0, h, a)
+                    nc.tensor.matmul_mx(za[:], wb_codes[:, a, m].bitcast(FP8X4), w_s[:, PASSES + a, m], v, v_s, start=(a == 0), stop=False)
+                for a in range(PASSES):
+                    v, v_s = table_operand(1, h, a)
+                    wa_cols = wa_codes[:, a, 2 * t * P : 2 * (t + 1) * P]
+                    nc.tensor.matmul_mx(za[:], wa_cols.bitcast(FP4X4), w_s[:, a, m], v, v_s, start=False, stop=(a == PASSES - 1))
+                for a in range(PASSES):
+                    v, v_s = table_operand(0, h, a)
+                    nc.tensor.matmul_mx(ms[:], wc_codes[:, a, m].bitcast(FP8X4), wc_s[:, a, m], v, v_s, start=(a == 0), stop=(a == PASSES - 1))
+                eta = held("eta%d_%d" % (t, h), [P, HALF], F32)
+                nc.scalar.activation(eta[:], za[:], ACT.Sigmoid)
+                message = ring.tile([P, HALF], F32, name="message")
+                nc.vector.scalar_tensor_tensor(message[:], ms[:], 0.0, eta[:], ALU.max, ALU.mult)
+                cols = slice(h * HALF // 16, (h + 1) * HALF // 16)
+                nc.vector.tensor_tensor(
+                    pages[t][:].indirect(dst_list[:, cols]), message[:], gain[:, h * HALF : (h + 1) * HALF], ALU.mult
+                )
+            nc.sync.dma_start(out_rows[:, t, :], pages[t][:])
+        for t in range(PACK - 1):
+            for c in range(CHUNKS):
+                rows = pages[t][:, c * CHUNK : (c + 1) * CHUNK]
+                if t == PACK - 2 and c % 2 == 0:
+                    nc.scalar.copy(rounded[c][:, :, t : t + 2], rows.unsqueeze(2).to_broadcast([P, CHUNK, 2]))
+                else:
+                    nc.scalar.copy(rounded[c][:, :, t], rows)
+
+        y_s = held("y_s", [P, T], U8)
+        out_words = out_1[0].rearrange("p t b -> p (t b)").bitcast(I32)
+        last = PACK - 1
+        for c in range(CHUNKS):
+            cols = slice(c * CHUNK, (c + 1) * CHUNK)
+            if c % 2 == 0:
+                nc.vector.tensor_copy(rounded[c][:, :, last], pages[last][:, cols])
+            else:
+                nc.scalar.copy(rounded[c][:, :, last], pages[last][:, cols])
+        for c in (0, 1, 2, 3):
+            cols = slice(c * CHUNK, (c + 1) * CHUNK)
+            y_codes = held("y_codes%d" % c, [P, CHUNK], I32)
+            nc.vector.quantize_mx(
+                out=y_codes[:].bitcast(FP8X4), scales=y_s[:, cols], in_=rounded[c][:].rearrange("p c t -> p (c t)")
+            )
+            nc.sync.dma_start(out_words[:, cols], y_codes[:])
+        for q in range(4):
+            nc.scalar.dma_start(out_2[0, 4 * q : 4 * q + 4, :].bitcast(I32), y_s[32 * q : 32 * q + 4, :].bitcast(I32))

@@ -40,13 +40,21 @@ def tile_list_rgg_reluP_kernel(
 
         src_list = keep.tile([P, J // 16], U16, name="src_list")
         dst_list = keep.tile([P, J // 16], U16, name="dst_list")
+        lists = (src_list, dst_list)
         tab_s = held("tab_s", [P, T], U8)
         w_s_raw = held("w_s_raw", [P, 2 * PASSES, N], U8)
         nc.vector.memset(tab_s[:].bitcast(I32), 0)
-        nc.gpsimd.memset(w_s_raw[:].rearrange("p a n -> p (a n)").bitcast(I32), 0)
+        nc.vector.memset(w_s_raw[:].rearrange("p a n -> p (a n)").bitcast(I32), 0)
         pages = [held("page%d" % t, [P, T], F32) for t in range(2)]
         for t in range(2):
             nc.vector.memset(pages[t][:].bitcast(I32), 0)
+        warm_in = held("warm_in", [P, 1], F32)
+        warm_out = held("warm_out", [P, 1], F32)
+        nc.vector.memset(warm_in[:], 0.0)
+        nc.scalar.activation(warm_out[:], warm_in[:], ACT.Sigmoid)
+        for t, tag in ((2, "warm_in"), (3, "warm_out")):
+            pages.append(held("page%d" % t, [P, T], F32, tag=tag))
+            nc.gpsimd.memset(pages[t][:], 0.0)
 
         nc.sync.dma_start(src_list[:], offs)
         nc.sync.dma_start(dst_list[:], offs2)
@@ -54,46 +62,52 @@ def tile_list_rgg_reluP_kernel(
             nc.sync.dma_start(tab_s[32 * q : 32 * q + 8, :].bitcast(I32), tab_scales[:, 4 * q : 4 * q + 4, :].bitcast(I32))
         wa_raw = held("wa_raw", [P, PASSES, 2 * N], U8)
         nc.sync.dma_start(wa_raw[:].bitcast(I32), wa_words.rearrange("a p b -> p a b").bitcast(I32))
+        tab_w = held("tab_w", [P, T], I32)
+        nc.sync.dma_start(tab_w[:], tab_words[0].rearrange("p t b -> p (t b)").bitcast(I32))
         wc_raw = [held("wc_raw%d" % a, [P, PACK, N], F32) for a in range(PASSES)]
         wc_rows = wc.rearrange("(a p i) n -> a p i n", p=P, i=PACK)
         nc.sync.dma_start(wc_raw[0][:], wc_rows[0])
-        tab_w = held("tab_w", [P, T], I32)
-        nc.sync.dma_start(tab_w[:], tab_words[0].rearrange("p t b -> p (t b)").bitcast(I32))
-        for w, scales in enumerate((wa_scales, wb_scales)):
-            for q in range(4):
-                nc.gpsimd.dma_start(
-                    w_s_raw[32 * q : 32 * q + 4, PASSES * w : PASSES * (w + 1), :].bitcast(I32),
-                    scales[:, 4 * q : 4 * q + 4, :].rearrange("a r n -> r a n").bitcast(I32),
-                )
+
+        def load_weight_scales(i):
+            w, q = divmod(i, 4)
+            nc.sync.dma_start(
+                w_s_raw[32 * q : 32 * q + 4, PASSES * w : PASSES * (w + 1), :].bitcast(I32),
+                (wa_scales, wb_scales)[w][:, 4 * q : 4 * q + 4, :].rearrange("a r n -> r a n").bitcast(I32),
+            )
+
+        for i in range(6):
+            load_weight_scales(i)
         nc.sync.dma_start(wc_raw[1][:], wc_rows[1])
+        for i in range(6, 8):
+            load_weight_scales(i)
         wb_raw = held("wb_raw", [P, PASSES, N], I32)
         nc.sync.dma_start(wb_raw[:], wb_words.rearrange("a p n b -> p a (n b)").bitcast(I32))
-        gain = held("gain", [P, J], F32)
-        nc.sync.dma_start(gain[:], wgo)
 
-        lists = (src_list, dst_list)
-        picked_s = []
-        for l in range(2):
-            both = held("picked_s%d" % l, [P, J], U8)
-            nc.vector.tensor_copy(both[:], tab_s[:].indirect(lists[l][:]))
-            second = held("shifted_s%d" % l, [P, J], U8)
-            nc.gpsimd.dma_start(second[0:SHIFT_ROWS, :].bitcast(I32), both[4 : 4 + SHIFT_ROWS, :].bitcast(I32))
-            picked_s.append((both, second))
-
+        picked_s = {}
         parted = {}
-        after = {(0, 1): "wb_raw", (1, 1): "wc_grouped1"}
 
-        def pick_words(h):
+        def list_half(l, h):
+            return lists[l][:, h * HALF // 16 : (h + 1) * HALF // 16]
+
+        def pick_scales(h, tag):
+            both = held("picked_s%d" % h, [P, 2 * HALF], U8, tag=tag)
             for l in range(2):
-                words = held("picked_w%d_%d" % (l, h), [P, HALF], I32, tag=after.get((l, h)))
-                cols = slice(h * HALF // 16, (h + 1) * HALF // 16)
-                nc.vector.tensor_copy(words[:].bitcast(U32), tab_w[:].bitcast(U32).indirect(lists[l][:, cols]))
-                parted[l, h] = (words, held("parted%d_%d" % (l, h), [P, PASSES, 2 * HALF], U8))
+                nc.vector.tensor_copy(both[:, l * HALF : (l + 1) * HALF], tab_s[:].indirect(list_half(l, h)))
+            second = held("shifted_s%d" % h, [P, 2 * HALF], U8)
+            nc.sync.dma_start(second[0:SHIFT_ROWS, :].bitcast(I32), both[4 : 4 + SHIFT_ROWS, :].bitcast(I32))
+            picked_s[h] = (both, second)
+
+        def pick_words(h, tag):
+            words = held("picked_w%d" % h, [P, 2 * HALF], I32, tag=tag)
             for l in range(2):
-                words, apart = parted[l, h]
                 nc.vector.tensor_copy(
-                    apart[:].bitcast(U16),
-                    words[:].bitcast(U16).rearrange("p (j a) -> p a j", a=PASSES),
+                    words[:, l * HALF : (l + 1) * HALF].bitcast(U32), tab_w[:].bitcast(U32).indirect(list_half(l, h))
+                )
+            for l in range(2):
+                parted[l, h] = held("parted%d_%d" % (l, h), [P, PASSES, 2 * HALF], U8)
+                nc.vector.tensor_copy(
+                    parted[l, h][:].bitcast(U16),
+                    words[:, l * HALF : (l + 1) * HALF].bitcast(U16).rearrange("p (j a) -> p a j", a=PASSES),
                 )
 
         wc_codes = held("wc_codes", [P, PASSES, N], U32)
@@ -107,7 +121,15 @@ def tile_list_rgg_reluP_kernel(
             )
             nc.vector.quantize_mx(out=wc_codes[:, a, :].bitcast(FP8X4), scales=wc_s[:, a, :], in_=grouped[:])
 
-        pick_words(0)
+        pick_scales(0, None)
+        gain = held("gain", [P, J], F32)
+        nc.sync.dma_start(gain[:], wgo)
+        pick_words(0, None)
+        wa_codes = held("wa_codes", [P, PASSES, 2 * N], U8)
+        nc.vector.tensor_copy(
+            wa_codes[:].bitcast(U16).rearrange("p a (t o i) -> p a o t i", t=PACK, i=8),
+            wa_raw[:].bitcast(U16).rearrange("p a (o i t) -> p a o t i", t=PACK, i=8),
+        )
         quantise_wc(0)
         w_s = held("w_s", [P, 2 * PASSES, N], U8)
         nc.vector.tensor_copy(
@@ -119,70 +141,84 @@ def tile_list_rgg_reluP_kernel(
             wb_codes[:].rearrange("p a (t o i) -> p a o t i", t=PACK, i=4),
             wb_raw[:].rearrange("p a (o i t) -> p a o t i", t=PACK, i=4),
         )
-        wa_codes = held("wa_codes", [P, PASSES, 2 * N], U8)
-        nc.vector.tensor_copy(
-            wa_codes[:].bitcast(U16).rearrange("p a (t o i) -> p a o t i", t=PACK, i=8),
-            wa_raw[:].bitcast(U16).rearrange("p a (o i t) -> p a o t i", t=PACK, i=8),
-        )
         quantise_wc(1)
-        pick_words(1)
-        for t, tag in ((2, "wb_raw"), (3, "wc_grouped1")):
-            pages.append(held("page%d" % t, [P, T], F32, tag=tag))
-            nc.gpsimd.memset(pages[t][:], 0.0)
+        pick_scales(1, "wc_grouped1")
+        pick_words(1, "tab_s")
 
         def table_operand(l, h, a):
-            cols = slice(h * HALF, (h + 1) * HALF)
-            return parted[l, h][1][:, a, :].bitcast(FP4X4), picked_s[l][a][:, cols]
+            return parted[l, h][:, a, :].bitcast(FP4X4), picked_s[h][a][:, l * HALF : (l + 1) * HALF]
 
-        rounded = [held("rounded%d" % c, [P, CHUNK, PACK], BF16) for c in range(CHUNKS)]
         out_rows = out_0.rearrange("(p t) c -> p t c", t=PACK)
+        messages = [held("message%d" % t, [P, J], F32) for t in range(PACK)]
 
-        for t in range(PACK):
+        def make_messages(t, h):
             m = slice(t * P, (t + 1) * P)
+            za = psum.tile([P, HALF], F32, name="za")
+            ms = psum.tile([P, HALF], F32, name="ms")
+            for a in range(PASSES):
+                v, v_s = table_operand(1, h, a)
+                wa_cols = wa_codes[:, a, 2 * t * P : 2 * (t + 1) * P]
+                nc.tensor.matmul_mx(za[:], wa_cols.bitcast(FP4X4), w_s[:, a, m], v, v_s, start=(a == 0), stop=False)
+            for a in range(PASSES):
+                v, v_s = table_operand(0, h, a)
+                nc.tensor.matmul_mx(za[:], wb_codes[:, a, m].bitcast(FP8X4), w_s[:, PASSES + a, m], v, v_s, start=False, stop=(a == PASSES - 1))
+            for a in range(PASSES):
+                v, v_s = table_operand(0, h, a)
+                nc.tensor.matmul_mx(ms[:], wc_codes[:, a, m].bitcast(FP8X4), wc_s[:, a, m], v, v_s, start=(a == 0), stop=(a == PASSES - 1))
+            eta = held("eta%d_%d" % (t, h), [P, HALF], F32)
+            nc.scalar.activation(eta[:], za[:], ACT.Sigmoid)
+            positive = held("positive%d_%d" % (t, h), [P, HALF], F32)
+            nc.scalar.activation(positive[:], ms[:], ACT.Relu)
+            gated = ring.tile([P, HALF], F32, name="gated")
+            edges = slice(h * HALF, (h + 1) * HALF)
+            nc.gpsimd.tensor_tensor(gated[:], eta[:], gain[:, edges], ALU.mult)
+            nc.gpsimd.tensor_tensor(messages[t][:, edges], gated[:], positive[:], ALU.mult)
+
+        for h in range(HALVES):
+            for t in range(2):
+                make_messages(t, h)
+                nc.vector.tensor_copy(pages[t][:].indirect(list_half(1, h)), messages[t][:, h * HALF : (h + 1) * HALF])
+        for t in range(2, PACK):
             for h in range(HALVES):
-                za = psum.tile([P, HALF], F32, name="za")
-                ms = psum.tile([P, HALF], F32, name="ms")
-                for a in range(PASSES):
-                    v, v_s = table_operand(0, h, a)
-                    nc.tensor.matmul_mx(za[:], wb_codes[:, a, m].bitcast(FP8X4), w_s[:, PASSES + a, m], v, v_s, start=(a == 0), stop=False)
-                for a in range(PASSES):
-                    v, v_s = table_operand(1, h, a)
-                    wa_cols = wa_codes[:, a, 2 * t * P : 2 * (t + 1) * P]
-                    nc.tensor.matmul_mx(za[:], wa_cols.bitcast(FP4X4), w_s[:, a, m], v, v_s, start=False, stop=(a == PASSES - 1))
-                for a in range(PASSES):
-                    v, v_s = table_operand(0, h, a)
-                    nc.tensor.matmul_mx(ms[:], wc_codes[:, a, m].bitcast(FP8X4), wc_s[:, a, m], v, v_s, start=(a == 0), stop=(a == PASSES - 1))
-                eta = held("eta%d_%d" % (t, h), [P, HALF], F32)
-                nc.scalar.activation(eta[:], za[:], ACT.Sigmoid)
-                message = ring.tile([P, HALF], F32, name="message")
-                nc.vector.scalar_tensor_tensor(message[:], ms[:], 0.0, eta[:], ALU.max, ALU.mult)
-                cols = slice(h * HALF // 16, (h + 1) * HALF // 16)
-                nc.vector.tensor_tensor(
-                    pages[t][:].indirect(dst_list[:, cols]), message[:], gain[:, h * HALF : (h + 1) * HALF], ALU.mult
-                )
+                make_messages(t, h)
+            nc.vector.tensor_copy(pages[t][:].indirect(dst_list[:]), messages[t][:])
+        for t in range(PACK):
             nc.sync.dma_start(out_rows[:, t, :], pages[t][:])
+
+        gate_operands = ("parted1_1", "wa_codes", "wb_codes", "parted0_1")
+        pairs = [held("pairs%d" % c, [P, 2, CHUNK, 2], BF16, tag=gate_operands[c]) for c in range(CHUNKS)]
+        rounded = [held("rounded%d" % c, [P, CHUNK * PACK], BF16) for c in range(CHUNKS)]
         for t in range(PACK - 1):
             for c in range(CHUNKS):
                 rows = pages[t][:, c * CHUNK : (c + 1) * CHUNK]
                 if t == PACK - 2 and c % 2 == 0:
-                    nc.scalar.copy(rounded[c][:, :, t : t + 2], rows.unsqueeze(2).to_broadcast([P, CHUNK, 2]))
+                    nc.scalar.copy(pairs[c][:, 1, :, :], rows.unsqueeze(2).to_broadcast([P, CHUNK, 2]))
                 else:
-                    nc.scalar.copy(rounded[c][:, :, t], rows)
+                    nc.scalar.copy(pairs[c][:, t // 2, :, t % 2], rows)
 
         y_s = held("y_s", [P, T], U8)
         out_words = out_1[0].rearrange("p t b -> p (t b)").bitcast(I32)
         last = PACK - 1
-        for c in range(CHUNKS):
-            cols = slice(c * CHUNK, (c + 1) * CHUNK)
-            if c % 2 == 0:
-                nc.vector.tensor_copy(rounded[c][:, :, last], pages[last][:, cols])
-            else:
-                nc.scalar.copy(rounded[c][:, :, last], pages[last][:, cols])
-        for c in (0, 1, 2, 3):
+
+        def round_last(copy, c):
+            copy(pairs[c][:, 1, :, 1], pages[last][:, c * CHUNK : (c + 1) * CHUNK])
+
+        def weave(copy, word, c):
+            woven = rounded[c][:].bitcast(word).rearrange("p (c u) -> p c u", u=2)
+            copy(woven, pairs[c][:].rearrange("p u c e -> p u (c e)").bitcast(word).rearrange("p u c -> p c u"))
+
+        for c in (0, 2):
+            round_last(nc.vector.tensor_copy, c)
+        for c in (0, 2):
+            weave(nc.vector.tensor_copy, I32, c)
+        for c in (1, 3):
+            round_last(nc.scalar.copy, c)
+            weave(nc.scalar.copy, U32, c)
+        for c in (0, 2, 1, 3):
             cols = slice(c * CHUNK, (c + 1) * CHUNK)
             y_codes = held("y_codes%d" % c, [P, CHUNK], I32)
             nc.vector.quantize_mx(
-                out=y_codes[:].bitcast(FP8X4), scales=y_s[:, cols], in_=rounded[c][:].rearrange("p c t -> p (c t)")
+                out=y_codes[:].bitcast(FP8X4), scales=y_s[:, cols], in_=rounded[c][:]
             )
             nc.sync.dma_start(out_words[:, cols], y_codes[:])
         for q in range(4):

@@ -32,17 +32,19 @@ def tile_list_rgg_reluP_kernel(
     nc = tc.nc
     with ExitStack() as ctx:
         keep = ctx.enter_context(tc.tile_pool(name="keep", bufs=1))
-        ring = ctx.enter_context(tc.tile_pool(name="ring", bufs=3))
         psum = ctx.enter_context(tc.psum_pool(name="psum", bufs=4))
 
         def held(name, shape, dtype, tag=None):
             return keep.tile(shape, dtype, name=name, tag=tag or name, align_bytes=64)
 
+        def scale_rows(scales, r):
+            return scales.rearrange("a (q r) n -> r q a n", r=4)[r].bitcast(I32)
+
         src_list = keep.tile([P, J // 16], U16, name="src_list")
         dst_list = keep.tile([P, J // 16], U16, name="dst_list")
         lists = (src_list, dst_list)
         tab_s = held("tab_s", [P, T], U8)
-        w_s_raw = held("w_s_raw", [P, 2 * PASSES, N], U8)
+        w_s_raw = held("w_s_raw", [P, 2, N], U8)
         nc.vector.memset(tab_s[:].bitcast(I32), 0)
         nc.vector.memset(w_s_raw[:].rearrange("p a n -> p (a n)").bitcast(I32), 0)
         pages = [held("page%d" % t, [P, T], F32) for t in range(2)]
@@ -52,34 +54,28 @@ def tile_list_rgg_reluP_kernel(
         warm_out = held("warm_out", [P, 1], F32)
         nc.vector.memset(warm_in[:], 0.0)
         nc.scalar.activation(warm_out[:], warm_in[:], ACT.Sigmoid)
-        for t, tag in ((2, "warm_in"), (3, "warm_out")):
-            pages.append(held("page%d" % t, [P, T], F32, tag=tag))
-            nc.gpsimd.memset(pages[t][:], 0.0)
 
         nc.sync.dma_start(src_list[:], offs)
         nc.sync.dma_start(dst_list[:], offs2)
-        for q in range(4):
-            nc.sync.dma_start(tab_s[32 * q : 32 * q + 8, :].bitcast(I32), tab_scales[:, 4 * q : 4 * q + 4, :].bitcast(I32))
+        for r in range(4):
+            nc.sync.dma_start(tab_s[r:P:16, :].bitcast(I32), scale_rows(tab_scales, r))
         wa_raw = held("wa_raw", [P, PASSES, 2 * N], U8)
         nc.sync.dma_start(wa_raw[:].bitcast(I32), wa_words.rearrange("a p b -> p a b").bitcast(I32))
         tab_w = held("tab_w", [P, T], I32)
         nc.sync.dma_start(tab_w[:], tab_words[0].rearrange("p t b -> p (t b)").bitcast(I32))
         wc_raw = [held("wc_raw%d" % a, [P, PACK, N], F32) for a in range(PASSES)]
         wc_rows = wc.rearrange("(a p i) n -> a p i n", p=P, i=PACK)
-        nc.sync.dma_start(wc_raw[0][:], wc_rows[0])
 
         def load_weight_scales(i):
-            w, q = divmod(i, 4)
-            nc.sync.dma_start(
-                w_s_raw[32 * q : 32 * q + 4, PASSES * w : PASSES * (w + 1), :].bitcast(I32),
-                (wa_scales, wb_scales)[w][:, 4 * q : 4 * q + 4, :].rearrange("a r n -> r a n").bitcast(I32),
-            )
+            w, r = divmod(i, 4)
+            nc.sync.dma_start(w_s_raw[r:P:16, w, :].bitcast(I32), scale_rows((wa_scales, wb_scales)[w], r))
 
         for i in range(6):
             load_weight_scales(i)
-        nc.sync.dma_start(wc_raw[1][:], wc_rows[1])
+        nc.sync.dma_start(wc_raw[0][:], wc_rows[0])
         for i in range(6, 8):
             load_weight_scales(i)
+        nc.sync.dma_start(wc_raw[1][:], wc_rows[1])
         wb_raw = held("wb_raw", [P, PASSES, N], I32)
         nc.sync.dma_start(wb_raw[:], wb_words.rearrange("a p n b -> p a (n b)").bitcast(I32))
 
@@ -94,7 +90,7 @@ def tile_list_rgg_reluP_kernel(
             for l in range(2):
                 nc.vector.tensor_copy(both[:, l * HALF : (l + 1) * HALF], tab_s[:].indirect(list_half(l, h)))
             second = held("shifted_s%d" % h, [P, 2 * HALF], U8)
-            nc.sync.dma_start(second[0:SHIFT_ROWS, :].bitcast(I32), both[4 : 4 + SHIFT_ROWS, :].bitcast(I32))
+            nc.sync.dma_start(second[0:SHIFT_ROWS, :].bitcast(I32), both[16 : 16 + SHIFT_ROWS, :].bitcast(I32))
             picked_s[h] = (both, second)
 
         def pick_words(h, tag):
@@ -103,50 +99,61 @@ def tile_list_rgg_reluP_kernel(
                 nc.vector.tensor_copy(
                     words[:, l * HALF : (l + 1) * HALF].bitcast(U32), tab_w[:].bitcast(U32).indirect(list_half(l, h))
                 )
+            return words
+
+        def part_words(h, words, tag):
+            parted[h] = held("parted%d" % h, [P, 2, PASSES, 2 * HALF], U8, tag=tag)
             for l in range(2):
-                parted[l, h] = held("parted%d_%d" % (l, h), [P, PASSES, 2 * HALF], U8)
                 nc.vector.tensor_copy(
-                    parted[l, h][:].bitcast(U16),
+                    parted[h][:, l].bitcast(U16),
                     words[:, l * HALF : (l + 1) * HALF].bitcast(U16).rearrange("p (j a) -> p a j", a=PASSES),
                 )
 
         wc_codes = held("wc_codes", [P, PASSES, N], U32)
         wc_s = held("wc_s", [P, PASSES, N], U8)
 
-        def quantise_wc(a):
-            grouped = held("wc_grouped%d" % a, [P, N * PACK], BF16)
+        grouped = held("wc_grouped", [P, PASSES, N * PACK], BF16)
+        for a in range(PASSES):
             nc.scalar.copy(
-                grouped[:].rearrange("p (t m i) -> p m t i", t=PACK, i=PACK),
+                grouped[:, a, :].rearrange("p (t m i) -> p m t i", t=PACK, i=PACK),
                 wc_raw[a][:].rearrange("p i (m t) -> p m t i", t=PACK),
             )
-            nc.vector.quantize_mx(out=wc_codes[:, a, :].bitcast(FP8X4), scales=wc_s[:, a, :], in_=grouped[:])
 
         pick_scales(0, None)
-        gain = held("gain", [P, J], F32)
-        nc.sync.dma_start(gain[:], wgo)
-        pick_words(0, None)
+        part_words(0, pick_words(0, None), None)
         wa_codes = held("wa_codes", [P, PASSES, 2 * N], U8)
         nc.vector.tensor_copy(
             wa_codes[:].bitcast(U16).rearrange("p a (t o i) -> p a o t i", t=PACK, i=8),
             wa_raw[:].bitcast(U16).rearrange("p a (o i t) -> p a o t i", t=PACK, i=8),
         )
-        quantise_wc(0)
-        w_s = held("w_s", [P, 2 * PASSES, N], U8)
+        pages.append(held("page2", [P, T], F32, tag="wa_raw"))
+        nc.gpsimd.memset(pages[2][:], 0.0)
+        w_s = held("w_s", [P, 2, N], U8)
         nc.vector.tensor_copy(
             w_s[:].rearrange("p a (t o i) -> p a o t i", t=PACK, i=16),
             w_s_raw[:].rearrange("p a (o i t) -> p a o t i", t=PACK, i=16),
         )
+        w_s_second = held("w_s_second", [P, 2, N], U8)
+        nc.sync.dma_start(w_s_second[0:SHIFT_ROWS].bitcast(I32), w_s[16 : 16 + SHIFT_ROWS].bitcast(I32))
+        w_planes = (w_s, w_s_second)
+        gain = held("gain", [P, J], F32)
+        nc.sync.dma_start(gain[:], wgo)
+        later_words = pick_words(1, "w_s_raw")
         wb_codes = held("wb_codes", [P, PASSES, N], I32)
         nc.vector.tensor_copy(
             wb_codes[:].rearrange("p a (t o i) -> p a o t i", t=PACK, i=4),
             wb_raw[:].rearrange("p a (o i t) -> p a o t i", t=PACK, i=4),
         )
-        quantise_wc(1)
-        pick_scales(1, "wc_grouped1")
-        pick_words(1, "tab_s")
+        part_words(1, later_words, "wb_raw")
+        nc.vector.quantize_mx(
+            out=wc_codes[:].rearrange("p a n -> p (a n)").bitcast(FP8X4),
+            scales=wc_s[:].rearrange("p a n -> p (a n)"),
+            in_=grouped[:].rearrange("p a n -> p (a n)"),
+        )
+        pick_scales(1, "wc_grouped")
 
         def table_operand(l, h, a):
-            return parted[l, h][:, a, :].bitcast(FP4X4), picked_s[h][a][:, l * HALF : (l + 1) * HALF]
+            return parted[h][:, l, a, :].bitcast(FP4X4), picked_s[h][a][:, l * HALF : (l + 1) * HALF]
 
         out_rows = out_0.rearrange("(p t) c -> p t c", t=PACK)
         messages = [held("message%d" % t, [P, J], F32) for t in range(PACK)]
@@ -158,10 +165,10 @@ def tile_list_rgg_reluP_kernel(
             for a in range(PASSES):
                 v, v_s = table_operand(1, h, a)
                 wa_cols = wa_codes[:, a, 2 * t * P : 2 * (t + 1) * P]
-                nc.tensor.matmul_mx(za[:], wa_cols.bitcast(FP4X4), w_s[:, a, m], v, v_s, start=(a == 0), stop=False)
+                nc.tensor.matmul_mx(za[:], wa_cols.bitcast(FP4X4), w_planes[a][:, 0, m], v, v_s, start=(a == 0), stop=False)
             for a in range(PASSES):
                 v, v_s = table_operand(0, h, a)
-                nc.tensor.matmul_mx(za[:], wb_codes[:, a, m].bitcast(FP8X4), w_s[:, PASSES + a, m], v, v_s, start=False, stop=(a == PASSES - 1))
+                nc.tensor.matmul_mx(za[:], wb_codes[:, a, m].bitcast(FP8X4), w_planes[a][:, 1, m], v, v_s, start=False, stop=(a == PASSES - 1))
             for a in range(PASSES):
                 v, v_s = table_operand(0, h, a)
                 nc.tensor.matmul_mx(ms[:], wc_codes[:, a, m].bitcast(FP8X4), wc_s[:, a, m], v, v_s, start=(a == 0), stop=(a == PASSES - 1))
@@ -169,23 +176,27 @@ def tile_list_rgg_reluP_kernel(
             nc.scalar.activation(eta[:], za[:], ACT.Sigmoid)
             positive = held("positive%d_%d" % (t, h), [P, HALF], F32)
             nc.scalar.activation(positive[:], ms[:], ACT.Relu)
-            gated = ring.tile([P, HALF], F32, name="gated")
+            gated = held("gated", [P, HALF], F32)
             edges = slice(h * HALF, (h + 1) * HALF)
             nc.gpsimd.tensor_tensor(gated[:], eta[:], gain[:, edges], ALU.mult)
             nc.gpsimd.tensor_tensor(messages[t][:, edges], gated[:], positive[:], ALU.mult)
 
+        def place(t, h):
+            make_messages(t, h)
+            nc.vector.tensor_copy(pages[t][:].indirect(list_half(1, h)), messages[t][:, h * HALF : (h + 1) * HALF])
+
         for h in range(HALVES):
-            for t in range(2):
-                make_messages(t, h)
-                nc.vector.tensor_copy(pages[t][:].indirect(list_half(1, h)), messages[t][:, h * HALF : (h + 1) * HALF])
-        for t in range(2, PACK):
-            for h in range(HALVES):
-                make_messages(t, h)
-            nc.vector.tensor_copy(pages[t][:].indirect(dst_list[:]), messages[t][:])
+            for t in range(PACK - 1):
+                if (t, h) == (2, 1):
+                    pages.append(held("page3", [P, T], F32, tag="positive1_1"))
+                    nc.gpsimd.memset(pages[3][:], 0.0)
+                place(t, h)
+        for h in range(HALVES):
+            place(PACK - 1, h)
         for t in range(PACK):
             nc.sync.dma_start(out_rows[:, t, :], pages[t][:])
 
-        gate_operands = ("parted1_1", "wa_codes", "wb_codes", "parted0_1")
+        gate_operands = ("wb_raw", "wa_codes", "wb_codes", "w_s_second")
         pairs = [held("pairs%d" % c, [P, 2, CHUNK, 2], BF16, tag=gate_operands[c]) for c in range(CHUNKS)]
         rounded = [held("rounded%d" % c, [P, CHUNK * PACK], BF16) for c in range(CHUNKS)]
         for t in range(PACK - 1):

@@ -19,11 +19,20 @@ ACT = mybir.ActivationFunctionType
 P = 128
 PACK = 4
 PASSES = K // (P * PACK)
+QUADRANT = 32
+SCALE_ROWS = 4
+PASS_GAP = 16
+PER_COLUMN = 16
+LINE = 16
 HALF = 512
 HALVES = J // HALF
 CHUNK = 512
 CHUNKS = T // CHUNK
-SHIFT_ROWS = 112
+VECTOR_CHUNKS = (0, 2)
+SCALAR_CHUNKS = (1, 3)
+SOURCE, TARGET = 0, 1
+WA, WB = 0, 1
+LAST = PACK - 1
 
 
 def tile_list_rgg_reluP_kernel(
@@ -32,205 +41,228 @@ def tile_list_rgg_reluP_kernel(
     nc = tc.nc
     with ExitStack() as ctx:
         keep = ctx.enter_context(tc.tile_pool(name="keep", bufs=1))
+        overlay = ctx.enter_context(tc.tile_pool(name="overlay", bufs=1))
         psum = ctx.enter_context(tc.psum_pool(name="psum", bufs=4))
 
         def held(name, shape, dtype, tag=None):
             return keep.tile(shape, dtype, name=name, tag=tag or name, align_bytes=64)
 
         def scale_rows(scales, r):
-            return scales.rearrange("a (q r) n -> r q a n", r=4)[r].bitcast(I32)
+            return scales.rearrange("a (q r) n -> r q a n", r=SCALE_ROWS)[r].bitcast(I32)
 
-        src_list = keep.tile([P, J // 16], U16, name="src_list")
-        dst_list = keep.tile([P, J // 16], U16, name="dst_list")
-        lists = (src_list, dst_list)
+        def lift_second_pass(second, both):
+            nc.sync.dma_start(second[0 : P - PASS_GAP].bitcast(I32), both[PASS_GAP:P].bitcast(I32))
+
+        def deal_columns(dealt, raw, element_bytes):
+            i = LINE // element_bytes
+            nc.vector.tensor_copy(
+                dealt.rearrange("p a (t o i) -> p a o t i", t=PACK, i=i),
+                raw.rearrange("p a (o i t) -> p a o t i", t=PACK, i=i),
+            )
+
+        lists = [keep.tile([P, J // PER_COLUMN], U16, name=name) for name in ("source_list", "target_list")]
         tab_s = held("tab_s", [P, T], U8)
         w_s_raw = held("w_s_raw", [P, 2, N], U8)
         nc.vector.memset(tab_s[:].bitcast(I32), 0)
-        nc.vector.memset(w_s_raw[:].rearrange("p a n -> p (a n)").bitcast(I32), 0)
-        pages = [held("page%d" % t, [P, T], F32) for t in range(2)]
-        for t in range(2):
-            nc.vector.memset(pages[t][:].bitcast(I32), 0)
+        nc.vector.memset(w_s_raw[:].rearrange("p w n -> p (w n)").bitcast(I32), 0)
+        pages = [held("page0", [P, T], F32)]
+        nc.vector.memset(pages[0][:].bitcast(I32), 0)
         warm_in = held("warm_in", [P, 1], F32)
         warm_out = held("warm_out", [P, 1], F32)
         nc.vector.memset(warm_in[:], 0.0)
         nc.scalar.activation(warm_out[:], warm_in[:], ACT.Sigmoid)
+        for t, tag in ((1, "warm_in"), (2, "warm_out")):
+            pages.append(held("page%d" % t, [P, T], F32, tag=tag))
+            nc.gpsimd.memset(pages[t][:], 0.0)
 
-        nc.sync.dma_start(src_list[:], offs)
-        nc.sync.dma_start(dst_list[:], offs2)
-        for r in range(4):
-            nc.sync.dma_start(tab_s[r:P:16, :].bitcast(I32), scale_rows(tab_scales, r))
-        wa_raw = held("wa_raw", [P, PASSES, 2 * N], U8)
-        nc.sync.dma_start(wa_raw[:].bitcast(I32), wa_words.rearrange("a p b -> p a b").bitcast(I32))
+        wc_rows = wc.rearrange("(a p i) n -> a p i n", p=P, i=PACK)
+        wc_grouped = overlay.tile([P, PASSES, N * PACK], BF16, name="wc_grouped", offset=0, align_bytes=64)
+
+        def load_weight_scales(index):
+            w, r = divmod(index, SCALE_ROWS)
+            nc.sync.dma_start(w_s_raw[r:P:PASS_GAP, w, :].bitcast(I32), scale_rows((wa_scales, wb_scales)[w], r))
+
+        def load_and_round_wc(a, n0, n1, name):
+            raw = held(name, [P, PACK, n1 - n0], F32)
+            nc.sync.dma_start(raw[:], wc_rows[a][:, :, n0:n1])
+            nc.scalar.copy(
+                wc_grouped[:, a, :].rearrange("p (t m i) -> p m t i", t=PACK, i=PACK)[:, n0 // PACK : n1 // PACK],
+                raw[:].rearrange("p i (m t) -> p m t i", t=PACK),
+            )
+
+        nc.sync.dma_start(lists[SOURCE][:], offs)
+        for r in range(SCALE_ROWS):
+            nc.sync.dma_start(tab_s[r:P:PASS_GAP, :].bitcast(I32), scale_rows(tab_scales, r))
+        nc.sync.dma_start(lists[TARGET][:], offs2)
+        load_weight_scales(0)
         tab_w = held("tab_w", [P, T], I32)
         nc.sync.dma_start(tab_w[:], tab_words[0].rearrange("p t b -> p (t b)").bitcast(I32))
-        wc_raw = [held("wc_raw%d" % a, [P, PACK, N], F32) for a in range(PASSES)]
-        wc_rows = wc.rearrange("(a p i) n -> a p i n", p=P, i=PACK)
-
-        def load_weight_scales(i):
-            w, r = divmod(i, 4)
-            nc.sync.dma_start(w_s_raw[r:P:16, w, :].bitcast(I32), scale_rows((wa_scales, wb_scales)[w], r))
-
-        for i in range(6):
-            load_weight_scales(i)
-        nc.sync.dma_start(wc_raw[0][:], wc_rows[0])
-        for i in range(6, 8):
-            load_weight_scales(i)
-        nc.sync.dma_start(wc_raw[1][:], wc_rows[1])
-        wb_raw = held("wb_raw", [P, PASSES, N], I32)
-        nc.sync.dma_start(wb_raw[:], wb_words.rearrange("a p n b -> p a (n b)").bitcast(I32))
+        for index in range(1, 2 * SCALE_ROWS - 1):
+            load_weight_scales(index)
+        load_and_round_wc(0, 0, N, "wc_raw_first")
+        load_weight_scales(2 * SCALE_ROWS - 1)
+        wa_raw = held("wa_raw", [P, PASSES, 2 * N], U8)
+        nc.sync.dma_start(wa_raw[:].bitcast(I32), wa_words.rearrange("a p b -> p a b").bitcast(I32))
 
         picked_s = {}
         parted = {}
 
-        def list_half(l, h):
-            return lists[l][:, h * HALF // 16 : (h + 1) * HALF // 16]
+        def half(h):
+            return slice(h * HALF, (h + 1) * HALF)
 
-        def pick_scales(h, tag):
-            both = held("picked_s%d" % h, [P, 2 * HALF], U8, tag=tag)
-            for l in range(2):
-                nc.vector.tensor_copy(both[:, l * HALF : (l + 1) * HALF], tab_s[:].indirect(list_half(l, h)))
-            second = held("shifted_s%d" % h, [P, 2 * HALF], U8)
-            nc.sync.dma_start(second[0:SHIFT_ROWS, :].bitcast(I32), both[16 : 16 + SHIFT_ROWS, :].bitcast(I32))
+        def slot(which):
+            return slice(which * HALF, (which + 1) * HALF)
+
+        def list_half(which, h):
+            return lists[which][:, h * HALF // PER_COLUMN : (h + 1) * HALF // PER_COLUMN]
+
+        def pick_scales(h, both):
+            for which in (SOURCE, TARGET):
+                nc.vector.tensor_copy(both[:, slot(which)], tab_s[:].indirect(list_half(which, h)))
+            second = held("picked_s_second%d" % h, [P, 2 * HALF], U8)
+            lift_second_pass(second, both)
             picked_s[h] = (both, second)
 
-        def pick_words(h, tag):
+        def pick_words(h, tag=None):
             words = held("picked_w%d" % h, [P, 2 * HALF], I32, tag=tag)
-            for l in range(2):
-                nc.vector.tensor_copy(
-                    words[:, l * HALF : (l + 1) * HALF].bitcast(U32), tab_w[:].bitcast(U32).indirect(list_half(l, h))
-                )
+            for which in (SOURCE, TARGET):
+                nc.vector.tensor_copy(words[:, slot(which)].bitcast(U32), tab_w[:].bitcast(U32).indirect(list_half(which, h)))
             return words
 
-        def part_words(h, words, tag):
+        def part_words(h, words, tag=None):
             parted[h] = held("parted%d" % h, [P, 2, PASSES, 2 * HALF], U8, tag=tag)
-            for l in range(2):
+            for which in (SOURCE, TARGET):
                 nc.vector.tensor_copy(
-                    parted[h][:, l].bitcast(U16),
-                    words[:, l * HALF : (l + 1) * HALF].bitcast(U16).rearrange("p (j a) -> p a j", a=PASSES),
+                    parted[h][:, which].bitcast(U16),
+                    words[:, slot(which)].bitcast(U16).rearrange("p (j a) -> p a j", a=PASSES),
                 )
 
-        wc_codes = held("wc_codes", [P, PASSES, N], U32)
-        wc_s = held("wc_s", [P, PASSES, N], U8)
+        pick_scales(0, held("picked_s0", [P, 2 * HALF], U8))
+        wb_raw = held("wb_raw", [P, PASSES, N], I32)
+        nc.sync.dma_start(wb_raw[:], wb_words.rearrange("a p n b -> p a (n b)").bitcast(I32))
+        load_and_round_wc(1, 0, N // 2, "wc_raw_second")
+        part_words(0, pick_words(0))
 
-        grouped = held("wc_grouped", [P, PASSES, N * PACK], BF16)
-        for a in range(PASSES):
-            nc.scalar.copy(
-                grouped[:, a, :].rearrange("p (t m i) -> p m t i", t=PACK, i=PACK),
-                wc_raw[a][:].rearrange("p i (m t) -> p m t i", t=PACK),
-            )
-
-        pick_scales(0, None)
-        part_words(0, pick_words(0, None), None)
-        wa_codes = held("wa_codes", [P, PASSES, 2 * N], U8)
-        nc.vector.tensor_copy(
-            wa_codes[:].bitcast(U16).rearrange("p a (t o i) -> p a o t i", t=PACK, i=8),
-            wa_raw[:].bitcast(U16).rearrange("p a (o i t) -> p a o t i", t=PACK, i=8),
-        )
-        pages.append(held("page2", [P, T], F32, tag="wa_raw"))
-        nc.gpsimd.memset(pages[2][:], 0.0)
         w_s = held("w_s", [P, 2, N], U8)
-        nc.vector.tensor_copy(
-            w_s[:].rearrange("p a (t o i) -> p a o t i", t=PACK, i=16),
-            w_s_raw[:].rearrange("p a (o i t) -> p a o t i", t=PACK, i=16),
-        )
+        deal_columns(w_s[:], w_s_raw[:], 1)
         w_s_second = held("w_s_second", [P, 2, N], U8)
-        nc.sync.dma_start(w_s_second[0:SHIFT_ROWS].bitcast(I32), w_s[16 : 16 + SHIFT_ROWS].bitcast(I32))
+        lift_second_pass(w_s_second, w_s)
         w_planes = (w_s, w_s_second)
+        load_and_round_wc(1, N // 2, N, "wc_raw_last")
         gain = held("gain", [P, J], F32)
         nc.sync.dma_start(gain[:], wgo)
-        later_words = pick_words(1, "w_s_raw")
+        wa_codes = held("wa_codes", [P, PASSES, 2 * N], U8)
+        deal_columns(wa_codes[:].bitcast(U16), wa_raw[:].bitcast(U16), 2)
+
+        later_words = pick_words(1, tag="w_s_raw")
         wb_codes = held("wb_codes", [P, PASSES, N], I32)
-        nc.vector.tensor_copy(
-            wb_codes[:].rearrange("p a (t o i) -> p a o t i", t=PACK, i=4),
-            wb_raw[:].rearrange("p a (o i t) -> p a o t i", t=PACK, i=4),
-        )
-        part_words(1, later_words, "wb_raw")
+        deal_columns(wb_codes[:], wb_raw[:], 4)
+        part_words(1, later_words, tag="wb_raw")
+        wc_codes = held("wc_codes", [P, PASSES, N], U32)
+        wc_s = held("wc_s", [P, PASSES, N], U8)
         nc.vector.quantize_mx(
             out=wc_codes[:].rearrange("p a n -> p (a n)").bitcast(FP8X4),
             scales=wc_s[:].rearrange("p a n -> p (a n)"),
-            in_=grouped[:].rearrange("p a n -> p (a n)"),
+            in_=wc_grouped[:].rearrange("p a n -> p (a n)"),
         )
-        pick_scales(1, "wc_grouped")
+        pick_scales(1, overlay.tile([P, 2 * HALF], U8, name="picked_s1", offset=0, align_bytes=64))
 
-        def table_operand(l, h, a):
-            return parted[h][:, l, a, :].bitcast(FP4X4), picked_s[h][a][:, l * HALF : (l + 1) * HALF]
-
-        out_rows = out_0.rearrange("(p t) c -> p t c", t=PACK)
         messages = [held("message%d" % t, [P, J], F32) for t in range(PACK)]
 
-        def make_messages(t, h):
+        def table_operand(which, h, a):
+            return parted[h][:, which, a, :].bitcast(FP4X4), picked_s[h][a][:, slot(which)]
+
+        def multiply(t, h):
             m = slice(t * P, (t + 1) * P)
             za = psum.tile([P, HALF], F32, name="za")
             ms = psum.tile([P, HALF], F32, name="ms")
             for a in range(PASSES):
-                v, v_s = table_operand(1, h, a)
-                wa_cols = wa_codes[:, a, 2 * t * P : 2 * (t + 1) * P]
-                nc.tensor.matmul_mx(za[:], wa_cols.bitcast(FP4X4), w_planes[a][:, 0, m], v, v_s, start=(a == 0), stop=False)
+                v, v_s = table_operand(TARGET, h, a)
+                wa_cols = wa_codes[:, a, 2 * t * P : 2 * (t + 1) * P].bitcast(FP4X4)
+                nc.tensor.matmul_mx(za[:], wa_cols, w_planes[a][:, WA, m], v, v_s, start=(a == 0), stop=False)
             for a in range(PASSES):
-                v, v_s = table_operand(0, h, a)
-                nc.tensor.matmul_mx(za[:], wb_codes[:, a, m].bitcast(FP8X4), w_planes[a][:, 1, m], v, v_s, start=False, stop=(a == PASSES - 1))
+                v, v_s = table_operand(SOURCE, h, a)
+                wb_cols = wb_codes[:, a, m].bitcast(FP8X4)
+                nc.tensor.matmul_mx(za[:], wb_cols, w_planes[a][:, WB, m], v, v_s, start=False, stop=(a == PASSES - 1))
             for a in range(PASSES):
-                v, v_s = table_operand(0, h, a)
-                nc.tensor.matmul_mx(ms[:], wc_codes[:, a, m].bitcast(FP8X4), wc_s[:, a, m], v, v_s, start=(a == 0), stop=(a == PASSES - 1))
+                v, v_s = table_operand(SOURCE, h, a)
+                wc_cols = wc_codes[:, a, m].bitcast(FP8X4)
+                nc.tensor.matmul_mx(ms[:], wc_cols, wc_s[:, a, m], v, v_s, start=(a == 0), stop=(a == PASSES - 1))
+            return za, ms
+
+        def scatter(t, h):
+            nc.vector.tensor_copy(pages[t][:].indirect(list_half(TARGET, h)), messages[t][:, half(h)])
+
+        def place_first():
+            za, ms = multiply(0, 0)
+            eta = held("eta0_0", [P, HALF], F32, tag="wc_raw_last")
+            nc.scalar.activation(eta[:], za[:], ACT.Sigmoid)
+            gated = overlay.tile([P, HALF], F32, name="first_gated", offset=2 * HALF, align_bytes=64)
+            nc.gpsimd.tensor_tensor(gated[:], eta[:], gain[:, half(0)], ALU.mult)
+            nc.vector.scalar_tensor_tensor(messages[0][:, half(0)], ms[:], 0.0, gated[:], ALU.max, ALU.mult)
+            scatter(0, 0)
+
+        def place(t, h):
+            za, ms = multiply(t, h)
             eta = held("eta%d_%d" % (t, h), [P, HALF], F32)
             nc.scalar.activation(eta[:], za[:], ACT.Sigmoid)
             positive = held("positive%d_%d" % (t, h), [P, HALF], F32)
             nc.scalar.activation(positive[:], ms[:], ACT.Relu)
             gated = held("gated", [P, HALF], F32)
-            edges = slice(h * HALF, (h + 1) * HALF)
-            nc.gpsimd.tensor_tensor(gated[:], eta[:], gain[:, edges], ALU.mult)
-            nc.gpsimd.tensor_tensor(messages[t][:, edges], gated[:], positive[:], ALU.mult)
+            nc.gpsimd.tensor_tensor(gated[:], eta[:], gain[:, half(h)], ALU.mult)
+            nc.gpsimd.tensor_tensor(messages[t][:, half(h)], gated[:], positive[:], ALU.mult)
+            scatter(t, h)
 
-        def place(t, h):
-            make_messages(t, h)
-            nc.vector.tensor_copy(pages[t][:].indirect(list_half(1, h)), messages[t][:, h * HALF : (h + 1) * HALF])
-
+        place_first()
+        for t in range(1, LAST):
+            place(t, 0)
+        for t in range(LAST - 1):
+            place(t, 1)
+        pages.append(held("page%d" % LAST, [P, T], F32, tag="positive%d_1" % (LAST - 2)))
+        nc.gpsimd.memset(pages[LAST][:], 0.0)
+        place(LAST - 1, 1)
         for h in range(HALVES):
-            for t in range(PACK - 1):
-                if (t, h) == (2, 1):
-                    pages.append(held("page3", [P, T], F32, tag="positive1_1"))
-                    nc.gpsimd.memset(pages[3][:], 0.0)
-                place(t, h)
-        for h in range(HALVES):
-            place(PACK - 1, h)
+            place(LAST, h)
+        out_rows = out_0.rearrange("(p t) c -> p t c", t=PACK)
         for t in range(PACK):
             nc.sync.dma_start(out_rows[:, t, :], pages[t][:])
 
-        gate_operands = ("wb_raw", "wa_codes", "wb_codes", "w_s_second")
-        pairs = [held("pairs%d" % c, [P, 2, CHUNK, 2], BF16, tag=gate_operands[c]) for c in range(CHUNKS)]
+        za_operands = ("wb_raw", "wa_codes", "wb_codes", "w_s_second")
+        pairs = [held("pairs%d" % c, [P, 2, CHUNK, 2], BF16, tag=za_operands[c]) for c in range(CHUNKS)]
         rounded = [held("rounded%d" % c, [P, CHUNK * PACK], BF16) for c in range(CHUNKS)]
-        for t in range(PACK - 1):
-            for c in range(CHUNKS):
-                rows = pages[t][:, c * CHUNK : (c + 1) * CHUNK]
-                if t == PACK - 2 and c % 2 == 0:
-                    nc.scalar.copy(pairs[c][:, 1, :, :], rows.unsqueeze(2).to_broadcast([P, CHUNK, 2]))
-                else:
-                    nc.scalar.copy(pairs[c][:, t // 2, :, t % 2], rows)
 
-        y_s = held("y_s", [P, T], U8)
-        out_words = out_1[0].rearrange("p t b -> p (t b)").bitcast(I32)
-        last = PACK - 1
+        def chunk(c):
+            return slice(c * CHUNK, (c + 1) * CHUNK)
+
+        for t in range(LAST):
+            for c in range(CHUNKS):
+                values = pages[t][:, chunk(c)]
+                if t == LAST - 1 and c in VECTOR_CHUNKS:
+                    nc.scalar.copy(pairs[c][:, 1, :, :], values.unsqueeze(2).to_broadcast([P, CHUNK, 2]))
+                else:
+                    nc.scalar.copy(pairs[c][:, t // 2, :, t % 2], values)
 
         def round_last(copy, c):
-            copy(pairs[c][:, 1, :, 1], pages[last][:, c * CHUNK : (c + 1) * CHUNK])
+            copy(pairs[c][:, 1, :, 1], pages[LAST][:, chunk(c)])
 
         def weave(copy, word, c):
             woven = rounded[c][:].bitcast(word).rearrange("p (c u) -> p c u", u=2)
             copy(woven, pairs[c][:].rearrange("p u c e -> p u (c e)").bitcast(word).rearrange("p u c -> p c u"))
 
-        for c in (0, 2):
+        for c in VECTOR_CHUNKS:
             round_last(nc.vector.tensor_copy, c)
-        for c in (0, 2):
+        for c in VECTOR_CHUNKS:
             weave(nc.vector.tensor_copy, I32, c)
-        for c in (1, 3):
+        for c in SCALAR_CHUNKS:
             round_last(nc.scalar.copy, c)
             weave(nc.scalar.copy, U32, c)
-        for c in (0, 2, 1, 3):
-            cols = slice(c * CHUNK, (c + 1) * CHUNK)
+
+        y_s = held("y_s", [P, T], U8)
+        out_words = out_1[0].rearrange("p t b -> p (t b)").bitcast(I32)
+        for c in VECTOR_CHUNKS + SCALAR_CHUNKS:
             y_codes = held("y_codes%d" % c, [P, CHUNK], I32)
-            nc.vector.quantize_mx(
-                out=y_codes[:].bitcast(FP8X4), scales=y_s[:, cols], in_=rounded[c][:]
-            )
-            nc.sync.dma_start(out_words[:, cols], y_codes[:])
-        for q in range(4):
-            nc.scalar.dma_start(out_2[0, 4 * q : 4 * q + 4, :].bitcast(I32), y_s[32 * q : 32 * q + 4, :].bitcast(I32))
+            nc.vector.quantize_mx(out=y_codes[:].bitcast(FP8X4), scales=y_s[:, chunk(c)], in_=rounded[c][:])
+            nc.sync.dma_start(out_words[:, chunk(c)], y_codes[:])
+        for q in range(P // QUADRANT):
+            rows = y_s[QUADRANT * q : QUADRANT * q + SCALE_ROWS, :]
+            nc.scalar.dma_start(out_2[0, SCALE_ROWS * q : SCALE_ROWS * (q + 1), :].bitcast(I32), rows.bitcast(I32))

@@ -62,25 +62,29 @@ def tile_list_rgg_reluP_kernel(
 
         lists = [keep.tile([P, J // PER_COLUMN], U16, name=name) for name in ("source_list", "target_list")]
         tab_s = held("tab_s", [P, T], U8)
-        w_s_raw = held("w_s_raw", [P, 2, N], U8)
+        operands_at = 5 * 4 * T
+        operand_bytes = 4 * PASSES * N
+        parted_at = (operands_at, operands_at + 2 * operand_bytes)
+        wb_codes_at, wc_codes_at = operands_at + operand_bytes, operands_at + 3 * operand_bytes
+        w_s_raw = overlay.tile([P, 2, N], U8, name="w_s_raw", offset=wb_codes_at - N, align_bytes=64)
         nc.vector.memset(tab_s[:].bitcast(I32), 0)
         nc.vector.memset(w_s_raw[:].rearrange("p w n -> p (w n)").bitcast(I32), 0)
         pages = [held("page0", [P, T], F32)]
         nc.vector.memset(pages[0][:].bitcast(I32), 0)
-        warm_in = held("warm_in", [P, 1], F32)
-        warm_out = held("warm_out", [P, 1], F32)
-        nc.vector.memset(warm_in[:], 0.0)
-        nc.scalar.activation(warm_out[:], warm_in[:], ACT.Sigmoid)
-        for t, tag in ((1, "warm_in"), (2, "warm_out")):
-            pages.append(held("page%d" % t, [P, T], F32, tag=tag))
-            nc.gpsimd.memset(pages[t][:], 0.0)
+        page_bytes = 4 * T
+        words_at, grouped_at, pages_at = 0, page_bytes, 2 * page_bytes
+        wa_raw_at = pages_at + page_bytes - 2 * N
+
+        def placed(name, shape, dtype, offset):
+            return overlay.tile(shape, dtype, name=name, offset=offset, align_bytes=64)
 
         wc_rows = wc.rearrange("(a p i) n -> a p i n", p=P, i=PACK)
-        wc_grouped = overlay.tile([P, PASSES, N * PACK], BF16, name="wc_grouped", offset=0, align_bytes=64)
+        wc_grouped = placed("wc_grouped", [P, PASSES, N * PACK], BF16, grouped_at)
 
-        def load_weight_scales(index):
-            w, r = divmod(index, SCALE_ROWS)
-            nc.sync.dma_start(w_s_raw[r:P:PASS_GAP, w, :].bitcast(I32), scale_rows((wa_scales, wb_scales)[w], r))
+        def load_weight_scales(first, last):
+            for index in range(first, last):
+                w, r = divmod(index, SCALE_ROWS)
+                nc.sync.dma_start(w_s_raw[r:P:PASS_GAP, w, :].bitcast(I32), scale_rows((wa_scales, wb_scales)[w], r))
 
         def load_and_round_wc(a, n0, n1, name):
             raw = held(name, [P, PACK, n1 - n0], F32)
@@ -91,18 +95,32 @@ def tile_list_rgg_reluP_kernel(
             )
 
         nc.sync.dma_start(lists[SOURCE][:], offs)
+        nc.sync.dma_start(lists[TARGET][:], offs2)
+        wa_raw = placed("wa_raw", [P, PASSES, 2 * N], U8, wa_raw_at)
+        nc.sync.dma_start(wa_raw[:].bitcast(I32), wa_words.rearrange("a p b -> p a b").bitcast(I32))
         for r in range(SCALE_ROWS):
             nc.sync.dma_start(tab_s[r:P:PASS_GAP, :].bitcast(I32), scale_rows(tab_scales, r))
-        nc.sync.dma_start(lists[TARGET][:], offs2)
-        load_weight_scales(0)
         tab_w = held("tab_w", [P, T], I32)
         nc.sync.dma_start(tab_w[:], tab_words[0].rearrange("p t b -> p (t b)").bitcast(I32))
-        for index in range(1, 2 * SCALE_ROWS - 1):
-            load_weight_scales(index)
-        load_and_round_wc(0, 0, N, "wc_raw_first")
-        load_weight_scales(2 * SCALE_ROWS - 1)
-        wa_raw = held("wa_raw", [P, PASSES, 2 * N], U8)
-        nc.sync.dma_start(wa_raw[:].bitcast(I32), wa_words.rearrange("a p b -> p a b").bitcast(I32))
+
+        wa_codes = held("wa_codes", [P, PASSES, 2 * N], U8)
+        deal_columns(wa_codes[:].bitcast(U16), wa_raw[:].bitcast(U16), 2)
+        warm_in = placed("warm_in", [P, 1], F32, pages_at + page_bytes)
+        warm_out = placed("warm_out", [P, 1], F32, pages_at + 2 * page_bytes)
+        nc.vector.memset(warm_in[:], 0.0)
+        nc.scalar.activation(warm_out[:], warm_in[:], ACT.Sigmoid)
+        for t in range(1, PACK):
+            pages.append(placed("page%d" % t, [P, T], F32, pages_at + (t - 1) * page_bytes))
+            nc.gpsimd.memset(pages[t][:], 0.0)
+
+        load_and_round_wc(0, 0, N // 2, "wc_raw0")
+        load_and_round_wc(0, N // 2, N, "wc_raw1")
+        load_weight_scales(0, 5)
+        load_and_round_wc(1, 0, N // 2, "wc_raw2")
+        load_and_round_wc(1, N // 2, N, "wc_raw_last")
+        load_weight_scales(5, 2 * SCALE_ROWS)
+        wb_raw = placed("wb_raw", [P, PASSES, N], I32, wc_codes_at - operand_bytes // 2)
+        nc.sync.dma_start(wb_raw[:], wb_words.rearrange("a p n b -> p a (n b)").bitcast(I32))
 
         picked_s = {}
         parted = {}
@@ -119,53 +137,41 @@ def tile_list_rgg_reluP_kernel(
         def pick_scales(h, both):
             for which in (SOURCE, TARGET):
                 nc.vector.tensor_copy(both[:, slot(which)], tab_s[:].indirect(list_half(which, h)))
-            second = held("picked_s_second%d" % h, [P, 2 * HALF], U8)
+            second = placed("picked_s_second%d" % h, [P, 2 * HALF], U8, operands_at + (6 - 2 * h) * operand_bytes)
             lift_second_pass(second, both)
             picked_s[h] = (both, second)
 
-        def pick_words(h, tag=None):
-            words = held("picked_w%d" % h, [P, 2 * HALF], I32, tag=tag)
-            for which in (SOURCE, TARGET):
-                nc.vector.tensor_copy(words[:, slot(which)].bitcast(U32), tab_w[:].bitcast(U32).indirect(list_half(which, h)))
-            return words
-
-        def part_words(h, words, tag=None):
-            parted[h] = held("parted%d" % h, [P, 2, PASSES, 2 * HALF], U8, tag=tag)
-            for which in (SOURCE, TARGET):
-                nc.vector.tensor_copy(
-                    parted[h][:, which].bitcast(U16),
-                    words[:, slot(which)].bitcast(U16).rearrange("p (j a) -> p a j", a=PASSES),
-                )
+        def part_words(h):
+            parted[h] = placed("parted%d" % h, [P, 2, PASSES, 2 * HALF], U8, parted_at[h])
+            nc.vector.tensor_copy(
+                parted[h][:].bitcast(U16),
+                words[:, :, half(h)].bitcast(U16).rearrange("p w (j a) -> p w a j", a=PASSES),
+            )
 
         pick_scales(0, held("picked_s0", [P, 2 * HALF], U8))
-        wb_raw = held("wb_raw", [P, PASSES, N], I32)
-        nc.sync.dma_start(wb_raw[:], wb_words.rearrange("a p n b -> p a (n b)").bitcast(I32))
-        load_and_round_wc(1, 0, N // 2, "wc_raw_second")
-        part_words(0, pick_words(0))
+        words = placed("picked_w", [P, 2, J], I32, words_at)
+        for which in (SOURCE, TARGET):
+            nc.vector.tensor_copy(words[:, which, :].bitcast(U32), tab_w[:].bitcast(U32).indirect(lists[which][:]))
+        gain = held("gain", [P, J], F32)
+        nc.sync.dma_start(gain[:], wgo)
 
         w_s = held("w_s", [P, 2, N], U8)
         deal_columns(w_s[:], w_s_raw[:], 1)
         w_s_second = held("w_s_second", [P, 2, N], U8)
         lift_second_pass(w_s_second, w_s)
         w_planes = (w_s, w_s_second)
-        load_and_round_wc(1, N // 2, N, "wc_raw_last")
-        gain = held("gain", [P, J], F32)
-        nc.sync.dma_start(gain[:], wgo)
-        wa_codes = held("wa_codes", [P, PASSES, 2 * N], U8)
-        deal_columns(wa_codes[:].bitcast(U16), wa_raw[:].bitcast(U16), 2)
-
-        later_words = pick_words(1, tag="w_s_raw")
-        wb_codes = held("wb_codes", [P, PASSES, N], I32)
+        part_words(0)
+        wb_codes = placed("wb_codes", [P, PASSES, N], I32, wb_codes_at)
         deal_columns(wb_codes[:], wb_raw[:], 4)
-        part_words(1, later_words, tag="wb_raw")
-        wc_codes = held("wc_codes", [P, PASSES, N], U32)
+        part_words(1)
+        wc_codes = placed("wc_codes", [P, PASSES, N], U32, wc_codes_at)
         wc_s = held("wc_s", [P, PASSES, N], U8)
         nc.vector.quantize_mx(
             out=wc_codes[:].rearrange("p a n -> p (a n)").bitcast(FP8X4),
             scales=wc_s[:].rearrange("p a n -> p (a n)"),
             in_=wc_grouped[:].rearrange("p a n -> p (a n)"),
         )
-        pick_scales(1, overlay.tile([P, 2 * HALF], U8, name="picked_s1", offset=0, align_bytes=64))
+        pick_scales(1, placed("picked_s1", [P, 2 * HALF], U8, grouped_at - HALF))
 
         messages = [held("message%d" % t, [P, J], F32) for t in range(PACK)]
 
@@ -180,7 +186,6 @@ def tile_list_rgg_reluP_kernel(
                 v, v_s = table_operand(TARGET, h, a)
                 wa_cols = wa_codes[:, a, 2 * t * P : 2 * (t + 1) * P].bitcast(FP4X4)
                 nc.tensor.matmul_mx(za[:], wa_cols, w_planes[a][:, WA, m], v, v_s, start=(a == 0), stop=False)
-            for a in range(PASSES):
                 v, v_s = table_operand(SOURCE, h, a)
                 wb_cols = wb_codes[:, a, m].bitcast(FP8X4)
                 nc.tensor.matmul_mx(za[:], wb_cols, w_planes[a][:, WB, m], v, v_s, start=False, stop=(a == PASSES - 1))
@@ -197,7 +202,7 @@ def tile_list_rgg_reluP_kernel(
             za, ms = multiply(0, 0)
             eta = held("eta0_0", [P, HALF], F32, tag="wc_raw_last")
             nc.scalar.activation(eta[:], za[:], ACT.Sigmoid)
-            gated = overlay.tile([P, HALF], F32, name="first_gated", offset=2 * HALF, align_bytes=64)
+            gated = placed("first_gated", [P, HALF], F32, grouped_at + 2 * HALF)
             nc.gpsimd.tensor_tensor(gated[:], eta[:], gain[:, half(0)], ALU.mult)
             nc.vector.scalar_tensor_tensor(messages[0][:, half(0)], ms[:], 0.0, gated[:], ALU.max, ALU.mult)
             scatter(0, 0)
@@ -213,22 +218,29 @@ def tile_list_rgg_reluP_kernel(
             nc.gpsimd.tensor_tensor(messages[t][:, half(h)], gated[:], positive[:], ALU.mult)
             scatter(t, h)
 
+        def place_whole(t):
+            eta = held("eta_whole", [P, J], F32)
+            positive = held("positive_whole", [P, J], F32)
+            for h in range(HALVES):
+                za, ms = multiply(t, h)
+                nc.scalar.activation(eta[:, half(h)], za[:], ACT.Sigmoid)
+                nc.scalar.activation(positive[:, half(h)], ms[:], ACT.Relu)
+            gated = held("gated_whole", [P, J], F32, tag="gated")
+            nc.gpsimd.tensor_tensor(gated[:], eta[:], gain[:], ALU.mult)
+            nc.gpsimd.tensor_tensor(messages[t][:], gated[:], positive[:], ALU.mult)
+            nc.vector.tensor_copy(pages[t][:].indirect(lists[TARGET][:]), messages[t][:])
+
         place_first()
         for t in range(1, LAST):
             place(t, 0)
-        for t in range(LAST - 1):
+        for t in range(LAST):
             place(t, 1)
-        pages.append(held("page%d" % LAST, [P, T], F32, tag="positive%d_1" % (LAST - 2)))
-        nc.gpsimd.memset(pages[LAST][:], 0.0)
-        place(LAST - 1, 1)
-        for h in range(HALVES):
-            place(LAST, h)
+        place_whole(LAST)
         out_rows = out_0.rearrange("(p t) c -> p t c", t=PACK)
         for t in range(PACK):
             nc.sync.dma_start(out_rows[:, t, :], pages[t][:])
 
-        za_operands = ("wb_raw", "wa_codes", "wb_codes", "w_s_second")
-        pairs = [held("pairs%d" % c, [P, 2, CHUNK, 2], BF16, tag=za_operands[c]) for c in range(CHUNKS)]
+        pairs = [placed("pairs%d" % c, [P, 2, CHUNK, 2], BF16, wb_codes_at + HALF + c * operand_bytes) for c in range(CHUNKS)]
         rounded = [held("rounded%d" % c, [P, CHUNK * PACK], BF16) for c in range(CHUNKS)]
 
         def chunk(c):

@@ -26,10 +26,8 @@ PER_COLUMN = 16
 LINE = 16
 HALF = 512
 HALVES = J // HALF
-CHUNK = 512
-CHUNKS = T // CHUNK
-VECTOR_CHUNKS = (0, 2)
-SCALAR_CHUNKS = (1, 3)
+QUANTISED = ((0, 512), (512, 1024), (1024, 1536), (1536, 1792), (1792, 2048))
+VECTOR_COLUMNS = 768
 SOURCE, TARGET = 0, 1
 WA, WB = 0, 1
 LAST = PACK - 1
@@ -42,7 +40,7 @@ def tile_list_rgg_reluP_kernel(
     with ExitStack() as ctx:
         keep = ctx.enter_context(tc.tile_pool(name="keep", bufs=1))
         overlay = ctx.enter_context(tc.tile_pool(name="overlay", bufs=1))
-        psum = ctx.enter_context(tc.psum_pool(name="psum", bufs=4))
+        psum = ctx.enter_context(tc.psum_pool(name="psum", bufs=1))
 
         def held(name, shape, dtype, tag=None):
             return keep.tile(shape, dtype, name=name, tag=tag or name, align_bytes=64)
@@ -62,21 +60,25 @@ def tile_list_rgg_reluP_kernel(
 
         lists = [keep.tile([P, J // PER_COLUMN], U16, name=name) for name in ("source_list", "target_list")]
         tab_s = held("tab_s", [P, T], U8)
-        operands_at = 5 * 4 * T
-        operand_bytes = 4 * PASSES * N
-        parted_at = (operands_at, operands_at + 2 * operand_bytes)
-        wb_codes_at, wc_codes_at = operands_at + operand_bytes, operands_at + 3 * operand_bytes
-        w_s_raw = overlay.tile([P, 2, N], U8, name="w_s_raw", offset=wb_codes_at - N, align_bytes=64)
-        nc.vector.memset(tab_s[:].bitcast(I32), 0)
-        nc.vector.memset(w_s_raw[:].rearrange("p w n -> p (w n)").bitcast(I32), 0)
-        pages = [held("page0", [P, T], F32)]
-        nc.vector.memset(pages[0][:].bitcast(I32), 0)
         page_bytes = 4 * T
-        words_at, grouped_at, pages_at = 0, page_bytes, 2 * page_bytes
-        wa_raw_at = pages_at + page_bytes - 2 * N
+        operand_bytes = 4 * PASSES * N
+        grouped_at, codes_at, pages_at = 0, page_bytes, 2 * page_bytes
+        words_at = pages_at + 2 * page_bytes
+        parted_at = words_at + operand_bytes
 
         def placed(name, shape, dtype, offset):
             return overlay.tile(shape, dtype, name=name, offset=offset, align_bytes=64)
+
+        w_s_raw = placed("w_s_raw", [P, 2, N], U8, parted_at + operand_bytes - N)
+        nc.vector.memset(tab_s[:].bitcast(I32), 0)
+        nc.vector.memset(w_s_raw[:].rearrange("p w n -> p (w n)").bitcast(I32), 0)
+        warm_in = held("warm_in", [P, 1], F32)
+        warm_out = held("warm_out", [P, 1], F32)
+        nc.vector.memset(warm_in[:], 0.0)
+        nc.scalar.activation(warm_out[:], warm_in[:], ACT.Sigmoid)
+        pages = [held("page%d" % t, [P, T], F32) for t in range(2)]
+        for page in pages:
+            nc.vector.memset(page[:].bitcast(I32), 0)
 
         wc_rows = wc.rearrange("(a p i) n -> a p i n", p=P, i=PACK)
         wc_grouped = placed("wc_grouped", [P, PASSES, N * PACK], BF16, grouped_at)
@@ -96,8 +98,10 @@ def tile_list_rgg_reluP_kernel(
 
         nc.sync.dma_start(lists[SOURCE][:], offs)
         nc.sync.dma_start(lists[TARGET][:], offs2)
-        wa_raw = placed("wa_raw", [P, PASSES, 2 * N], U8, wa_raw_at)
+        wa_raw = held("wa_raw", [P, PASSES, 2 * N], U8)
         nc.sync.dma_start(wa_raw[:].bitcast(I32), wa_words.rearrange("a p b -> p a b").bitcast(I32))
+        wb_raw = placed("wb_raw", [P, PASSES, N], I32, pages_at + page_bytes - operand_bytes // 2)
+        nc.sync.dma_start(wb_raw[:], wb_words.rearrange("a p n b -> p a (n b)").bitcast(I32))
         for r in range(SCALE_ROWS):
             nc.sync.dma_start(tab_s[r:P:PASS_GAP, :].bitcast(I32), scale_rows(tab_scales, r))
         tab_w = held("tab_w", [P, T], I32)
@@ -105,22 +109,18 @@ def tile_list_rgg_reluP_kernel(
 
         wa_codes = held("wa_codes", [P, PASSES, 2 * N], U8)
         deal_columns(wa_codes[:].bitcast(U16), wa_raw[:].bitcast(U16), 2)
-        warm_in = placed("warm_in", [P, 1], F32, pages_at + page_bytes)
-        warm_out = placed("warm_out", [P, 1], F32, pages_at + 2 * page_bytes)
-        nc.vector.memset(warm_in[:], 0.0)
-        nc.scalar.activation(warm_out[:], warm_in[:], ACT.Sigmoid)
-        for t in range(1, PACK):
-            pages.append(placed("page%d" % t, [P, T], F32, pages_at + (t - 1) * page_bytes))
+        wb_codes = held("wb_codes", [P, PASSES, N], I32)
+        deal_columns(wb_codes[:], wb_raw[:], 4)
+        for t in range(2, PACK):
+            pages.append(placed("page%d" % t, [P, T], F32, pages_at + (t - 2) * page_bytes))
             nc.gpsimd.memset(pages[t][:], 0.0)
 
         load_and_round_wc(0, 0, N // 2, "wc_raw0")
+        load_weight_scales(0, 6)
         load_and_round_wc(0, N // 2, N, "wc_raw1")
-        load_weight_scales(0, 5)
+        load_weight_scales(6, 2 * SCALE_ROWS)
         load_and_round_wc(1, 0, N // 2, "wc_raw2")
         load_and_round_wc(1, N // 2, N, "wc_raw_last")
-        load_weight_scales(5, 2 * SCALE_ROWS)
-        wb_raw = placed("wb_raw", [P, PASSES, N], I32, wc_codes_at - operand_bytes // 2)
-        nc.sync.dma_start(wb_raw[:], wb_words.rearrange("a p n b -> p a (n b)").bitcast(I32))
 
         picked_s = {}
         parted = {}
@@ -137,21 +137,26 @@ def tile_list_rgg_reluP_kernel(
         def pick_scales(h, both):
             for which in (SOURCE, TARGET):
                 nc.vector.tensor_copy(both[:, slot(which)], tab_s[:].indirect(list_half(which, h)))
-            second = placed("picked_s_second%d" % h, [P, 2 * HALF], U8, operands_at + (6 - 2 * h) * operand_bytes)
+            second = held("picked_s_second%d" % h, [P, 2 * HALF], U8)
             lift_second_pass(second, both)
             picked_s[h] = (both, second)
 
-        def part_words(h):
-            parted[h] = placed("parted%d" % h, [P, 2, PASSES, 2 * HALF], U8, parted_at[h])
+        def pick_words(name, offsets, count, offset):
+            words = placed(name, [P, count], I32, offset)
+            nc.vector.tensor_copy(words[:].bitcast(U32), tab_w[:].bitcast(U32).indirect(offsets))
+            return words
+
+        def part_words(name, words, halves, offset):
+            runs = placed(name, [P, halves, PASSES, 2 * HALF], U8, offset)
             nc.vector.tensor_copy(
-                parted[h][:].bitcast(U16),
-                words[:, :, half(h)].bitcast(U16).rearrange("p w (j a) -> p w a j", a=PASSES),
+                runs[:].bitcast(U16),
+                words[:].bitcast(U16).rearrange("p (h j a) -> p h a j", h=halves, a=PASSES),
             )
+            return [runs[:, h] for h in range(halves)]
 
         pick_scales(0, held("picked_s0", [P, 2 * HALF], U8))
-        words = placed("picked_w", [P, 2, J], I32, words_at)
-        for which in (SOURCE, TARGET):
-            nc.vector.tensor_copy(words[:, which, :].bitcast(U32), tab_w[:].bitcast(U32).indirect(lists[which][:]))
+        source_words = pick_words("source_words", lists[SOURCE][:], J, words_at)
+        target_words = pick_words("target_words0", list_half(TARGET, 0), HALF, codes_at)
         gain = held("gain", [P, J], F32)
         nc.sync.dma_start(gain[:], wgo)
 
@@ -160,121 +165,124 @@ def tile_list_rgg_reluP_kernel(
         w_s_second = held("w_s_second", [P, 2, N], U8)
         lift_second_pass(w_s_second, w_s)
         w_planes = (w_s, w_s_second)
-        part_words(0)
-        wb_codes = placed("wb_codes", [P, PASSES, N], I32, wb_codes_at)
-        deal_columns(wb_codes[:], wb_raw[:], 4)
-        part_words(1)
-        wc_codes = placed("wc_codes", [P, PASSES, N], U32, wc_codes_at)
+        parted[SOURCE] = part_words("source_parted", source_words, HALVES, parted_at)
+        parted[TARGET] = part_words("target_parted0", target_words, 1, parted_at + operand_bytes)
+        target_words = pick_words("target_words1", list_half(TARGET, 1), HALF, words_at)
+        wc_codes = placed("wc_codes", [P, PASSES, N], U32, codes_at)
         wc_s = held("wc_s", [P, PASSES, N], U8)
         nc.vector.quantize_mx(
             out=wc_codes[:].rearrange("p a n -> p (a n)").bitcast(FP8X4),
             scales=wc_s[:].rearrange("p a n -> p (a n)"),
             in_=wc_grouped[:].rearrange("p a n -> p (a n)"),
         )
-        pick_scales(1, placed("picked_s1", [P, 2 * HALF], U8, grouped_at - HALF))
+        parted[TARGET].extend(part_words("target_parted1", target_words, 1, grouped_at))
+        pick_scales(1, placed("picked_s1", [P, 2 * HALF], U8, words_at))
 
         messages = [held("message%d" % t, [P, J], F32) for t in range(PACK)]
 
         def table_operand(which, h, a):
-            return parted[h][:, which, a, :].bitcast(FP4X4), picked_s[h][a][:, slot(which)]
+            return parted[which][h][:, a, :].bitcast(FP4X4), picked_s[h][a][:, slot(which)]
 
-        def multiply(t, h):
+        def bank(index, count=1):
+            return psum.tile([P, count * HALF], F32, name="bank%d_%d" % (index, count), offset=index * 4 * HALF)[:, 0:HALF]
+
+        def multiply(t, h, za, ms):
             m = slice(t * P, (t + 1) * P)
-            za = psum.tile([P, HALF], F32, name="za")
-            ms = psum.tile([P, HALF], F32, name="ms")
-            for a in range(PASSES):
+
+            def gate_pass(a):
                 v, v_s = table_operand(TARGET, h, a)
                 wa_cols = wa_codes[:, a, 2 * t * P : 2 * (t + 1) * P].bitcast(FP4X4)
-                nc.tensor.matmul_mx(za[:], wa_cols, w_planes[a][:, WA, m], v, v_s, start=(a == 0), stop=False)
+                nc.tensor.matmul_mx(za, wa_cols, w_planes[a][:, WA, m], v, v_s, start=(a == 0), stop=False)
                 v, v_s = table_operand(SOURCE, h, a)
                 wb_cols = wb_codes[:, a, m].bitcast(FP8X4)
-                nc.tensor.matmul_mx(za[:], wb_cols, w_planes[a][:, WB, m], v, v_s, start=False, stop=(a == PASSES - 1))
-            for a in range(PASSES):
+                nc.tensor.matmul_mx(za, wb_cols, w_planes[a][:, WB, m], v, v_s, start=False, stop=(a == PASSES - 1))
+
+            def message_pass(a):
                 v, v_s = table_operand(SOURCE, h, a)
                 wc_cols = wc_codes[:, a, m].bitcast(FP8X4)
-                nc.tensor.matmul_mx(ms[:], wc_cols, wc_s[:, a, m], v, v_s, start=(a == 0), stop=(a == PASSES - 1))
-            return za, ms
+                nc.tensor.matmul_mx(ms, wc_cols, wc_s[:, a, m], v, v_s, start=(a == 0), stop=(a == PASSES - 1))
 
-        def scatter(t, h):
-            nc.vector.tensor_copy(pages[t][:].indirect(list_half(TARGET, h)), messages[t][:, half(h)])
+            if h == 0:
+                steps = (gate_pass, 0), (gate_pass, 1), (message_pass, 0), (message_pass, 1)
+            else:
+                steps = (gate_pass, 0), (message_pass, 0), (message_pass, 1), (gate_pass, 1)
+            for step, a in steps:
+                step(a)
 
-        def place_first():
-            za, ms = multiply(0, 0)
-            eta = held("eta0_0", [P, HALF], F32, tag="wc_raw_last")
-            nc.scalar.activation(eta[:], za[:], ACT.Sigmoid)
-            gated = placed("first_gated", [P, HALF], F32, grouped_at + 2 * HALF)
-            nc.gpsimd.tensor_tensor(gated[:], eta[:], gain[:, half(0)], ALU.mult)
-            nc.vector.scalar_tensor_tensor(messages[0][:, half(0)], ms[:], 0.0, gated[:], ALU.max, ALU.mult)
-            scatter(0, 0)
+        etas = [held("eta%d" % t, [P, J], F32) for t in range(PACK)]
+        positives = [held("positive%d" % t, [P, J], F32) for t in range(PACK)]
 
-        def place(t, h):
-            za, ms = multiply(t, h)
-            eta = held("eta%d_%d" % (t, h), [P, HALF], F32)
-            nc.scalar.activation(eta[:], za[:], ACT.Sigmoid)
-            positive = held("positive%d_%d" % (t, h), [P, HALF], F32)
-            nc.scalar.activation(positive[:], ms[:], ACT.Relu)
-            gated = held("gated", [P, HALF], F32)
-            nc.gpsimd.tensor_tensor(gated[:], eta[:], gain[:, half(h)], ALU.mult)
-            nc.gpsimd.tensor_tensor(messages[t][:, half(h)], gated[:], positive[:], ALU.mult)
-            scatter(t, h)
+        def empty(t, h):
+            za, ms = bank(banks.pop(0)), bank(banks.pop(0))
+            multiply(t, h, za, ms)
+            if h == 0:
+                nc.scalar.activation(etas[t][:, half(h)], za, ACT.Sigmoid)
+            nc.scalar.activation(positives[t][:, half(h)], ms, ACT.Relu)
+            if h == 1:
+                nc.scalar.activation(etas[t][:, half(h)], za, ACT.Sigmoid)
 
-        def place_whole(t):
-            eta = held("eta_whole", [P, J], F32)
-            positive = held("positive_whole", [P, J], F32)
-            for h in range(HALVES):
-                za, ms = multiply(t, h)
-                nc.scalar.activation(eta[:, half(h)], za[:], ACT.Sigmoid)
-                nc.scalar.activation(positive[:, half(h)], ms[:], ACT.Relu)
-            gated = held("gated_whole", [P, J], F32, tag="gated")
-            nc.gpsimd.tensor_tensor(gated[:], eta[:], gain[:], ALU.mult)
-            nc.gpsimd.tensor_tensor(messages[t][:], gated[:], positive[:], ALU.mult)
-            nc.vector.tensor_copy(pages[t][:].indirect(lists[TARGET][:]), messages[t][:])
+        def place(t, cols, offsets):
+            weighted = held("weighted", [P, cols.stop - cols.start], F32)
+            nc.gpsimd.tensor_tensor(weighted[:], positives[t][:, cols], gain[:, cols], ALU.mult)
+            nc.gpsimd.tensor_tensor(messages[t][:, cols], weighted[:], etas[t][:, cols], ALU.mult)
+            nc.vector.tensor_copy(pages[t][:].indirect(offsets), messages[t][:, cols])
 
-        place_first()
+        za, ms = bank(0, 4), bank(4)
+        banks = [0, 1, 2, 3, 5, 6, 7, 0, 1, 2, 3, 4, 5, 6]
+        multiply(0, 0, za, ms)
+        eta = held("first_eta", [P, HALF], F32, tag="wc_raw_last")
+        nc.scalar.activation(eta[:], za, ACT.Sigmoid)
+        gated = placed("first_gated", [P, HALF], F32, words_at + 2 * HALF)
+        nc.gpsimd.tensor_tensor(gated[:], eta[:], gain[:, half(0)], ALU.mult)
+        nc.vector.scalar_tensor_tensor(messages[0][:, half(0)], ms, 0.0, gated[:], ALU.max, ALU.mult)
+        nc.vector.tensor_copy(pages[0][:].indirect(list_half(TARGET, 0)), messages[0][:, half(0)])
+
         for t in range(1, LAST):
-            place(t, 0)
+            empty(t, 0)
         for t in range(LAST):
-            place(t, 1)
-        place_whole(LAST)
+            empty(t, 1)
+        for h in range(HALVES):
+            empty(LAST, h)
+        for t, h in ((1, 0), (0, 1), (1, 1), (2, 0), (2, 1)):
+            place(t, half(h), list_half(TARGET, h))
+        place(LAST, slice(0, J), lists[TARGET][:])
         out_rows = out_0.rearrange("(p t) c -> p t c", t=PACK)
         for t in range(PACK):
             nc.sync.dma_start(out_rows[:, t, :], pages[t][:])
 
-        pairs = [placed("pairs%d" % c, [P, 2, CHUNK, 2], BF16, wb_codes_at + HALF + c * operand_bytes) for c in range(CHUNKS)]
-        rounded = [held("rounded%d" % c, [P, CHUNK * PACK], BF16) for c in range(CHUNKS)]
+        low_pair = placed("low_pair", [P, T, 2], BF16, codes_at)
+        rounded = [held("rounded%d" % c, [P, c1 - c0, PACK], BF16) for c, (c0, c1) in enumerate(QUANTISED)]
 
-        def chunk(c):
-            return slice(c * CHUNK, (c + 1) * CHUNK)
+        def pieces(first, last):
+            found = []
+            for c, (c0, c1) in enumerate(QUANTISED):
+                lo, hi = max(first, c0), min(last, c1)
+                if lo < hi:
+                    found.append((rounded[c][:, lo - c0 : hi - c0, :], slice(lo, hi)))
+            return found
 
-        for t in range(LAST):
-            for c in range(CHUNKS):
-                values = pages[t][:, chunk(c)]
-                if t == LAST - 1 and c in VECTOR_CHUNKS:
-                    nc.scalar.copy(pairs[c][:, 1, :, :], values.unsqueeze(2).to_broadcast([P, CHUNK, 2]))
-                else:
-                    nc.scalar.copy(pairs[c][:, t // 2, :, t % 2], values)
-
-        def round_last(copy, c):
-            copy(pairs[c][:, 1, :, 1], pages[LAST][:, chunk(c)])
-
-        def weave(copy, word, c):
-            woven = rounded[c][:].bitcast(word).rearrange("p (c u) -> p c u", u=2)
-            copy(woven, pairs[c][:].rearrange("p u c e -> p u (c e)").bitcast(word).rearrange("p u c -> p c u"))
-
-        for c in VECTOR_CHUNKS:
-            round_last(nc.vector.tensor_copy, c)
-        for c in VECTOR_CHUNKS:
-            weave(nc.vector.tensor_copy, I32, c)
-        for c in SCALAR_CHUNKS:
-            round_last(nc.scalar.copy, c)
-            weave(nc.scalar.copy, U32, c)
+        for t in range(2):
+            nc.scalar.copy(low_pair[:, :, t], pages[t][:])
+        low_words = low_pair[:].rearrange("p c e -> p (c e)").bitcast(U32)
+        for view, cols in pieces(0, T):
+            both_words = view.rearrange("p c t -> p (c t)").bitcast(U32).rearrange("p (c u) -> p c u", u=2)
+            nc.scalar.copy(both_words, low_words[:, cols].unsqueeze(2).to_broadcast([P, cols.stop - cols.start, 2]))
+        for view, cols in pieces(0, VECTOR_COLUMNS):
+            twice = pages[2][:, cols].unsqueeze(2).to_broadcast([P, cols.stop - cols.start, 2])
+            nc.gpsimd.tensor_scalar(view[:, :, 2:PACK], twice, 1.0, -0.0, ALU.mult, ALU.add)
+        for view, cols in pieces(VECTOR_COLUMNS, T):
+            nc.scalar.copy(view[:, :, 2], pages[2][:, cols])
+        for view, cols in pieces(0, VECTOR_COLUMNS):
+            nc.vector.tensor_copy(view[:, :, LAST], pages[LAST][:, cols])
+        for view, cols in pieces(VECTOR_COLUMNS, T):
+            nc.scalar.copy(view[:, :, LAST], pages[LAST][:, cols])
 
         y_s = held("y_s", [P, T], U8)
         out_words = out_1[0].rearrange("p t b -> p (t b)").bitcast(I32)
-        for c in VECTOR_CHUNKS + SCALAR_CHUNKS:
-            y_codes = held("y_codes%d" % c, [P, CHUNK], I32)
-            nc.vector.quantize_mx(out=y_codes[:].bitcast(FP8X4), scales=y_s[:, chunk(c)], in_=rounded[c][:])
-            nc.sync.dma_start(out_words[:, chunk(c)], y_codes[:])
+        for c, (c0, c1) in enumerate(QUANTISED):
+            y_codes = held("y_codes%d" % c, [P, c1 - c0], I32)
+            nc.vector.quantize_mx(out=y_codes[:].bitcast(FP8X4), scales=y_s[:, c0:c1], in_=rounded[c][:].rearrange("p c t -> p (c t)"))
+            nc.sync.dma_start(out_words[:, c0:c1], y_codes[:])
         for q in range(P // QUADRANT):
             rows = y_s[QUADRANT * q : QUADRANT * q + SCALE_ROWS, :]
             nc.scalar.dma_start(out_2[0, SCALE_ROWS * q : SCALE_ROWS * (q + 1), :].bitcast(I32), rows.bitcast(I32))

@@ -62,23 +62,30 @@ def tile_list_rgg_reluP_kernel(
         tab_s = held("tab_s", [P, T], U8)
         page_bytes = 4 * T
         operand_bytes = 4 * PASSES * N
-        grouped_at, codes_at, pages_at = 0, page_bytes, 2 * page_bytes
-        words_at = pages_at + 2 * page_bytes
-        parted_at = words_at + operand_bytes
+        words_at, grouped_at, pages_at = 0, page_bytes, 2 * page_bytes
+        parted0_at = pages_at + 2 * page_bytes
+        wa_codes_at = parted0_at + operand_bytes
+        wb_codes_at = wa_codes_at + operand_bytes
+        parted1_at = wb_codes_at + operand_bytes
+        wc_codes_at = parted1_at + operand_bytes
 
-        def placed(name, shape, dtype, offset):
-            return overlay.tile(shape, dtype, name=name, offset=offset, align_bytes=64)
+        def placed(name, shape, dtype, offset, align=64):
+            return overlay.tile(shape, dtype, name=name, offset=offset, align_bytes=align)
 
-        w_s_raw = placed("w_s_raw", [P, 2, N], U8, parted_at + operand_bytes - N)
+        w_s_raw = placed("w_s_raw", [P, 2, N], U8, wa_codes_at - N)
         nc.vector.memset(tab_s[:].bitcast(I32), 0)
         nc.vector.memset(w_s_raw[:].rearrange("p w n -> p (w n)").bitcast(I32), 0)
-        warm_in = held("warm_in", [P, 1], F32)
-        warm_out = held("warm_out", [P, 1], F32)
+        pages = [held("page%d" % t, [P, T], F32) for t in range(2)]
+        nc.vector.memset(pages[0][:].bitcast(I32), 0)
+        nc.vector.memset(pages[1][:, 0 : T // 2].bitcast(I32), 0)
+        nc.gpsimd.memset(pages[1][:, T // 2 - 8 : T], 0.0)
+        warm_in = placed("warm_in", [P, 9], F32, pages_at + page_bytes - 32, align=32)
+        warm_out = held("warm_out", [P, 9], F32)
         nc.vector.memset(warm_in[:], 0.0)
         nc.scalar.activation(warm_out[:], warm_in[:], ACT.Sigmoid)
-        pages = [held("page%d" % t, [P, T], F32) for t in range(2)]
-        for page in pages:
-            nc.vector.memset(page[:].bitcast(I32), 0)
+        for t in range(2, PACK):
+            pages.append(placed("page%d" % t, [P, T], F32, pages_at + (t - 2) * page_bytes))
+            nc.gpsimd.memset(pages[t][:], 0.0)
 
         wc_rows = wc.rearrange("(a p i) n -> a p i n", p=P, i=PACK)
         wc_grouped = placed("wc_grouped", [P, PASSES, N * PACK], BF16, grouped_at)
@@ -97,28 +104,19 @@ def tile_list_rgg_reluP_kernel(
             )
 
         nc.sync.dma_start(lists[SOURCE][:], offs)
-        nc.sync.dma_start(lists[TARGET][:], offs2)
-        wa_raw = held("wa_raw", [P, PASSES, 2 * N], U8)
-        nc.sync.dma_start(wa_raw[:].bitcast(I32), wa_words.rearrange("a p b -> p a b").bitcast(I32))
-        wb_raw = placed("wb_raw", [P, PASSES, N], I32, pages_at + page_bytes - operand_bytes // 2)
-        nc.sync.dma_start(wb_raw[:], wb_words.rearrange("a p n b -> p a (n b)").bitcast(I32))
         for r in range(SCALE_ROWS):
             nc.sync.dma_start(tab_s[r:P:PASS_GAP, :].bitcast(I32), scale_rows(tab_scales, r))
+        nc.sync.dma_start(lists[TARGET][:], offs2)
         tab_w = held("tab_w", [P, T], I32)
         nc.sync.dma_start(tab_w[:], tab_words[0].rearrange("p t b -> p (t b)").bitcast(I32))
-
-        wa_codes = held("wa_codes", [P, PASSES, 2 * N], U8)
-        deal_columns(wa_codes[:].bitcast(U16), wa_raw[:].bitcast(U16), 2)
-        wb_codes = held("wb_codes", [P, PASSES, N], I32)
-        deal_columns(wb_codes[:], wb_raw[:], 4)
-        for t in range(2, PACK):
-            pages.append(placed("page%d" % t, [P, T], F32, pages_at + (t - 2) * page_bytes))
-            nc.gpsimd.memset(pages[t][:], 0.0)
-
+        wa_raw = placed("wa_raw", [P, PASSES, 2 * N], U8, parted1_at - 2 * N)
+        nc.sync.dma_start(wa_raw[:].bitcast(I32), wa_words.rearrange("a p b -> p a b").bitcast(I32))
+        wb_raw = placed("wb_raw", [P, PASSES, N], I32, wc_codes_at)
+        nc.sync.dma_start(wb_raw[:], wb_words.rearrange("a p n b -> p a (n b)").bitcast(I32))
+        load_weight_scales(0, SCALE_ROWS)
         load_and_round_wc(0, 0, N // 2, "wc_raw0")
-        load_weight_scales(0, 6)
         load_and_round_wc(0, N // 2, N, "wc_raw1")
-        load_weight_scales(6, 2 * SCALE_ROWS)
+        load_weight_scales(SCALE_ROWS, 2 * SCALE_ROWS)
         load_and_round_wc(1, 0, N // 2, "wc_raw2")
         load_and_round_wc(1, N // 2, N, "wc_raw_last")
 
@@ -141,22 +139,17 @@ def tile_list_rgg_reluP_kernel(
             lift_second_pass(second, both)
             picked_s[h] = (both, second)
 
-        def pick_words(name, offsets, count, offset):
-            words = placed(name, [P, count], I32, offset)
-            nc.vector.tensor_copy(words[:].bitcast(U32), tab_w[:].bitcast(U32).indirect(offsets))
-            return words
-
-        def part_words(name, words, halves, offset):
-            runs = placed(name, [P, halves, PASSES, 2 * HALF], U8, offset)
+        def part_words(h, offset):
+            parted[h] = placed("parted%d" % h, [P, 2, PASSES, 2 * HALF], U8, offset)
             nc.vector.tensor_copy(
-                runs[:].bitcast(U16),
-                words[:].bitcast(U16).rearrange("p (h j a) -> p h a j", h=halves, a=PASSES),
+                parted[h][:].bitcast(U16),
+                words[:, :, half(h)].bitcast(U16).rearrange("p w (j a) -> p w a j", a=PASSES),
             )
-            return [runs[:, h] for h in range(halves)]
 
         pick_scales(0, held("picked_s0", [P, 2 * HALF], U8))
-        source_words = pick_words("source_words", lists[SOURCE][:], J, words_at)
-        target_words = pick_words("target_words0", list_half(TARGET, 0), HALF, codes_at)
+        words = placed("picked_w", [P, 2, J], I32, words_at)
+        for which in (SOURCE, TARGET):
+            nc.vector.tensor_copy(words[:, which, :].bitcast(U32), tab_w[:].bitcast(U32).indirect(lists[which][:]))
         gain = held("gain", [P, J], F32)
         nc.sync.dma_start(gain[:], wgo)
 
@@ -165,23 +158,25 @@ def tile_list_rgg_reluP_kernel(
         w_s_second = held("w_s_second", [P, 2, N], U8)
         lift_second_pass(w_s_second, w_s)
         w_planes = (w_s, w_s_second)
-        parted[SOURCE] = part_words("source_parted", source_words, HALVES, parted_at)
-        parted[TARGET] = part_words("target_parted0", target_words, 1, parted_at + operand_bytes)
-        target_words = pick_words("target_words1", list_half(TARGET, 1), HALF, words_at)
-        wc_codes = placed("wc_codes", [P, PASSES, N], U32, codes_at)
+        part_words(0, parted0_at)
+        wa_codes = placed("wa_codes", [P, PASSES, 2 * N], U8, wa_codes_at)
+        deal_columns(wa_codes[:].bitcast(U16), wa_raw[:].bitcast(U16), 2)
+        wb_codes = placed("wb_codes", [P, PASSES, N], I32, wb_codes_at)
+        deal_columns(wb_codes[:], wb_raw[:], 4)
+        part_words(1, parted1_at)
+        wc_codes = placed("wc_codes", [P, PASSES, N], U32, wc_codes_at)
         wc_s = held("wc_s", [P, PASSES, N], U8)
         nc.vector.quantize_mx(
             out=wc_codes[:].rearrange("p a n -> p (a n)").bitcast(FP8X4),
             scales=wc_s[:].rearrange("p a n -> p (a n)"),
             in_=wc_grouped[:].rearrange("p a n -> p (a n)"),
         )
-        parted[TARGET].extend(part_words("target_parted1", target_words, 1, grouped_at))
-        pick_scales(1, placed("picked_s1", [P, 2 * HALF], U8, words_at))
+        pick_scales(1, placed("picked_s1", [P, 2 * HALF], U8, grouped_at - HALF))
 
         messages = [held("message%d" % t, [P, J], F32) for t in range(PACK)]
 
         def table_operand(which, h, a):
-            return parted[which][h][:, a, :].bitcast(FP4X4), picked_s[h][a][:, slot(which)]
+            return parted[h][:, which, a, :].bitcast(FP4X4), picked_s[h][a][:, slot(which)]
 
         def bank(index, count=1):
             return psum.tile([P, count * HALF], F32, name="bank%d_%d" % (index, count), offset=index * 4 * HALF)[:, 0:HALF]
@@ -227,12 +222,12 @@ def tile_list_rgg_reluP_kernel(
             nc.gpsimd.tensor_tensor(messages[t][:, cols], weighted[:], etas[t][:, cols], ALU.mult)
             nc.vector.tensor_copy(pages[t][:].indirect(offsets), messages[t][:, cols])
 
-        za, ms = bank(0, 4), bank(4)
-        banks = [0, 1, 2, 3, 5, 6, 7, 0, 1, 2, 3, 4, 5, 6]
+        za, ms = bank(0, 7), bank(7)
+        banks = [b % 7 for b in range(14)]
         multiply(0, 0, za, ms)
         eta = held("first_eta", [P, HALF], F32, tag="wc_raw_last")
         nc.scalar.activation(eta[:], za, ACT.Sigmoid)
-        gated = placed("first_gated", [P, HALF], F32, words_at + 2 * HALF)
+        gated = placed("first_gated", [P, HALF], F32, grouped_at + 2 * HALF)
         nc.gpsimd.tensor_tensor(gated[:], eta[:], gain[:, half(0)], ALU.mult)
         nc.vector.scalar_tensor_tensor(messages[0][:, half(0)], ms, 0.0, gated[:], ALU.max, ALU.mult)
         nc.vector.tensor_copy(pages[0][:].indirect(list_half(TARGET, 0)), messages[0][:, half(0)])
@@ -250,7 +245,7 @@ def tile_list_rgg_reluP_kernel(
         for t in range(PACK):
             nc.sync.dma_start(out_rows[:, t, :], pages[t][:])
 
-        low_pair = placed("low_pair", [P, T, 2], BF16, codes_at)
+        low_pair = placed("low_pair", [P, T, 2], BF16, wc_codes_at)
         rounded = [held("rounded%d" % c, [P, c1 - c0, PACK], BF16) for c, (c0, c1) in enumerate(QUANTISED)]
 
         def pieces(first, last):
@@ -285,4 +280,4 @@ def tile_list_rgg_reluP_kernel(
             nc.sync.dma_start(out_words[:, c0:c1], y_codes[:])
         for q in range(P // QUADRANT):
             rows = y_s[QUADRANT * q : QUADRANT * q + SCALE_ROWS, :]
-            nc.scalar.dma_start(out_2[0, SCALE_ROWS * q : SCALE_ROWS * (q + 1), :].bitcast(I32), rows.bitcast(I32))
+            (nc.scalar, nc.sync)[q % 2].dma_start(out_2[0, SCALE_ROWS * q : SCALE_ROWS * (q + 1), :].bitcast(I32), rows.bitcast(I32))

@@ -51,9 +51,9 @@ def tile_list_rgg_reluP_kernel(
         def lift_second_pass(second, both):
             nc.sync.dma_start(second[0 : P - PASS_GAP].bitcast(I32), both[PASS_GAP:P].bitcast(I32))
 
-        def deal_columns(dealt, raw, element_bytes):
+        def deal_columns(engine, dealt, raw, element_bytes):
             i = LINE // element_bytes
-            nc.vector.tensor_copy(
+            engine.tensor_copy(
                 dealt.rearrange("p a (t o i) -> p a o t i", t=PACK, i=i),
                 raw.rearrange("p a (o i t) -> p a o t i", t=PACK, i=i),
             )
@@ -62,30 +62,28 @@ def tile_list_rgg_reluP_kernel(
         tab_s = held("tab_s", [P, T], U8)
         page_bytes = 4 * T
         operand_bytes = 4 * PASSES * N
-        words_at, grouped_at, pages_at = 0, page_bytes, 2 * page_bytes
-        parted0_at = pages_at + 2 * page_bytes
-        wa_codes_at = parted0_at + operand_bytes
-        wb_codes_at = wa_codes_at + operand_bytes
-        parted1_at = wb_codes_at + operand_bytes
-        wc_codes_at = parted1_at + operand_bytes
+        grouped_at, page2_at = page_bytes, 2 * page_bytes
+        wa_codes_at = page2_at + page_bytes
+        parted0_at = wa_codes_at + operand_bytes
+        wc_codes_at = parted0_at + 2 * operand_bytes
 
         def placed(name, shape, dtype, offset, align=64):
             return overlay.tile(shape, dtype, name=name, offset=offset, align_bytes=align)
 
-        w_s_raw = placed("w_s_raw", [P, 2, N], U8, wa_codes_at - N)
+        w_s_raw = placed("w_s_raw", [P, 6, N], U8, parted0_at + operand_bytes // 2 - N)[:, 0:2, :]
         nc.vector.memset(tab_s[:].bitcast(I32), 0)
-        nc.vector.memset(w_s_raw[:].rearrange("p w n -> p (w n)").bitcast(I32), 0)
+        nc.vector.memset(w_s_raw.rearrange("p w n -> p (w n)").bitcast(I32), 0)
         pages = [held("page%d" % t, [P, T], F32) for t in range(2)]
         nc.vector.memset(pages[0][:].bitcast(I32), 0)
         nc.vector.memset(pages[1][:, 0 : T // 2].bitcast(I32), 0)
         nc.gpsimd.memset(pages[1][:, T // 2 - 8 : T], 0.0)
-        warm_in = placed("warm_in", [P, 9], F32, pages_at + page_bytes - 32, align=32)
+        warm_in = placed("warm_in", [P, 9], F32, wa_codes_at - 32, align=32)
         warm_out = held("warm_out", [P, 9], F32)
         nc.vector.memset(warm_in[:], 0.0)
         nc.scalar.activation(warm_out[:], warm_in[:], ACT.Sigmoid)
-        for t in range(2, PACK):
-            pages.append(placed("page%d" % t, [P, T], F32, pages_at + (t - 2) * page_bytes))
-            nc.gpsimd.memset(pages[t][:], 0.0)
+        pages.append(placed("page2", [P, T], F32, page2_at))
+        nc.gpsimd.memset(pages[2][:], 0.0)
+        pages.append(pages[0])
 
         wc_rows = wc.rearrange("(a p i) n -> a p i n", p=P, i=PACK)
         wc_grouped = placed("wc_grouped", [P, PASSES, N * PACK], BF16, grouped_at)
@@ -99,24 +97,24 @@ def tile_list_rgg_reluP_kernel(
             raw = held(name, [P, PACK, n1 - n0], F32)
             nc.sync.dma_start(raw[:], wc_rows[a][:, :, n0:n1])
             nc.scalar.copy(
-                wc_grouped[:, a, :].rearrange("p (t m i) -> p m t i", t=PACK, i=PACK)[:, n0 // PACK : n1 // PACK],
-                raw[:].rearrange("p i (m t) -> p m t i", t=PACK),
+                wc_grouped[:, a, :].rearrange("p (t m i) -> p m i t", t=PACK, i=PACK)[:, n0 // PACK : n1 // PACK],
+                raw[:].rearrange("p i (m t) -> p m i t", t=PACK),
             )
 
         nc.sync.dma_start(lists[SOURCE][:], offs)
+        wa_raw = held("wa_raw", [P, PASSES, 2 * N], U8)
+        nc.sync.dma_start(wa_raw[:].bitcast(I32), wa_words.rearrange("a p b -> p a b").bitcast(I32))
         for r in range(SCALE_ROWS):
             nc.sync.dma_start(tab_s[r:P:PASS_GAP, :].bitcast(I32), scale_rows(tab_scales, r))
         nc.sync.dma_start(lists[TARGET][:], offs2)
         tab_w = held("tab_w", [P, T], I32)
         nc.sync.dma_start(tab_w[:], tab_words[0].rearrange("p t b -> p (t b)").bitcast(I32))
-        wa_raw = placed("wa_raw", [P, PASSES, 2 * N], U8, parted1_at - 2 * N)
-        nc.sync.dma_start(wa_raw[:].bitcast(I32), wa_words.rearrange("a p b -> p a b").bitcast(I32))
-        wb_raw = placed("wb_raw", [P, PASSES, N], I32, wc_codes_at)
-        nc.sync.dma_start(wb_raw[:], wb_words.rearrange("a p n b -> p a (n b)").bitcast(I32))
-        load_weight_scales(0, SCALE_ROWS)
         load_and_round_wc(0, 0, N // 2, "wc_raw0")
+        wb_raw = held("wb_raw", [P, PASSES, N], I32)
+        nc.sync.dma_start(wb_raw[:], wb_words.rearrange("a p n b -> p a (n b)").bitcast(I32))
+        load_weight_scales(0, 5)
         load_and_round_wc(0, N // 2, N, "wc_raw1")
-        load_weight_scales(SCALE_ROWS, 2 * SCALE_ROWS)
+        load_weight_scales(5, 8)
         load_and_round_wc(1, 0, N // 2, "wc_raw2")
         load_and_round_wc(1, N // 2, N, "wc_raw_last")
 
@@ -139,31 +137,33 @@ def tile_list_rgg_reluP_kernel(
             lift_second_pass(second, both)
             picked_s[h] = (both, second)
 
-        def part_words(h, offset):
-            parted[h] = placed("parted%d" % h, [P, 2, PASSES, 2 * HALF], U8, offset)
-            nc.vector.tensor_copy(
-                parted[h][:].bitcast(U16),
-                words[:, :, half(h)].bitcast(U16).rearrange("p w (j a) -> p w a j", a=PASSES),
-            )
+        def part_words(tile, picked):
+            nc.vector.tensor_copy(tile.bitcast(U16), picked.bitcast(U16).rearrange("p w (j a) -> p w a j", a=PASSES))
 
         pick_scales(0, held("picked_s0", [P, 2 * HALF], U8))
-        words = placed("picked_w", [P, 2, J], I32, words_at)
-        for which in (SOURCE, TARGET):
+        words = held("picked_w", [P, 2, J], I32)
+        for which in (TARGET, SOURCE):
             nc.vector.tensor_copy(words[:, which, :].bitcast(U32), tab_w[:].bitcast(U32).indirect(lists[which][:]))
-        gain = held("gain", [P, J], F32)
-        nc.sync.dma_start(gain[:], wgo)
 
+        wa_codes = placed("wa_codes", [P, PASSES, 2 * N], U8, wa_codes_at)
+        deal_columns(nc.gpsimd, wa_codes[:].bitcast(U16), wa_raw[:].bitcast(U16), 2)
+        wb_codes = held("wb_codes", [P, PASSES, N], I32)
+        deal_columns(nc.gpsimd, wb_codes[:], wb_raw[:], 4)
         w_s = held("w_s", [P, 2, N], U8)
-        deal_columns(w_s[:], w_s_raw[:], 1)
+        deal_columns(nc.vector, w_s[:], w_s_raw, 1)
         w_s_second = held("w_s_second", [P, 2, N], U8)
         lift_second_pass(w_s_second, w_s)
         w_planes = (w_s, w_s_second)
-        part_words(0, parted0_at)
-        wa_codes = placed("wa_codes", [P, PASSES, 2 * N], U8, wa_codes_at)
-        deal_columns(wa_codes[:].bitcast(U16), wa_raw[:].bitcast(U16), 2)
-        wb_codes = placed("wb_codes", [P, PASSES, N], I32, wb_codes_at)
-        deal_columns(wb_codes[:], wb_raw[:], 4)
-        part_words(1, parted1_at)
+        gain = held("gain", [P, J], F32)
+        nc.sync.dma_start(gain[:], wgo)
+        for which in (TARGET, SOURCE):
+            tile = placed("parted0_%d" % which, [P, 1, PASSES, 2 * HALF], U8, parted0_at + which * 4 * HALF)
+            part_words(tile[:], words[:, which : which + 1, half(0)])
+            parted[0, which] = tile[:, 0]
+        tile = placed("parted1", [P, 2, PASSES, 2 * HALF], U8, parted0_at + operand_bytes)
+        part_words(tile[:], words[:, :, half(1)])
+        for which in (SOURCE, TARGET):
+            parted[1, which] = tile[:, which]
         wc_codes = placed("wc_codes", [P, PASSES, N], U32, wc_codes_at)
         wc_s = held("wc_s", [P, PASSES, N], U8)
         nc.vector.quantize_mx(
@@ -171,12 +171,12 @@ def tile_list_rgg_reluP_kernel(
             scales=wc_s[:].rearrange("p a n -> p (a n)"),
             in_=wc_grouped[:].rearrange("p a n -> p (a n)"),
         )
-        pick_scales(1, placed("picked_s1", [P, 2 * HALF], U8, grouped_at - HALF))
+        pick_scales(1, placed("picked_s1", [P, 2 * HALF], U8, grouped_at))
 
         messages = [held("message%d" % t, [P, J], F32) for t in range(PACK)]
 
         def table_operand(which, h, a):
-            return parted[h][:, which, a, :].bitcast(FP4X4), picked_s[h][a][:, slot(which)]
+            return parted[h, which][:, a, :].bitcast(FP4X4), picked_s[h][a][:, slot(which)]
 
         def bank(index, count=1):
             return psum.tile([P, count * HALF], F32, name="bank%d_%d" % (index, count), offset=index * 4 * HALF)[:, 0:HALF]
@@ -240,9 +240,8 @@ def tile_list_rgg_reluP_kernel(
             empty(LAST, h)
         for t, h in ((1, 0), (0, 1), (1, 1), (2, 0), (2, 1)):
             place(t, half(h), list_half(TARGET, h))
-        place(LAST, slice(0, J), lists[TARGET][:])
         out_rows = out_0.rearrange("(p t) c -> p t c", t=PACK)
-        for t in range(PACK):
+        for t in range(LAST):
             nc.sync.dma_start(out_rows[:, t, :], pages[t][:])
 
         low_pair = placed("low_pair", [P, T, 2], BF16, wc_codes_at)
@@ -258,6 +257,8 @@ def tile_list_rgg_reluP_kernel(
 
         for t in range(2):
             nc.scalar.copy(low_pair[:, :, t], pages[t][:])
+        place(LAST, slice(0, J), lists[TARGET][:])
+        nc.sync.dma_start(out_rows[:, LAST, :], pages[LAST][:])
         low_words = low_pair[:].rearrange("p c e -> p (c e)").bitcast(U32)
         for view, cols in pieces(0, T):
             both_words = view.rearrange("p c t -> p (c t)").bitcast(U32).rearrange("p (c u) -> p c u", u=2)
@@ -272,12 +273,13 @@ def tile_list_rgg_reluP_kernel(
         for view, cols in pieces(VECTOR_COLUMNS, T):
             nc.scalar.copy(view[:, :, LAST], pages[LAST][:, cols])
 
-        y_s = held("y_s", [P, T], U8)
+        y_s = held("y_s", [P, HALF], U8)
         out_words = out_1[0].rearrange("p t b -> p (t b)").bitcast(I32)
         for c, (c0, c1) in enumerate(QUANTISED):
             y_codes = held("y_codes%d" % c, [P, c1 - c0], I32)
-            nc.vector.quantize_mx(out=y_codes[:].bitcast(FP8X4), scales=y_s[:, c0:c1], in_=rounded[c][:].rearrange("p c t -> p (c t)"))
+            nc.vector.quantize_mx(out=y_codes[:].bitcast(FP8X4), scales=y_s[SCALE_ROWS * (c0 // HALF) : P, c0 % HALF : c0 % HALF + c1 - c0], in_=rounded[c][:].rearrange("p c t -> p (c t)"))
             nc.sync.dma_start(out_words[:, c0:c1], y_codes[:])
         for q in range(P // QUADRANT):
-            rows = y_s[QUADRANT * q : QUADRANT * q + SCALE_ROWS, :]
-            (nc.scalar, nc.sync)[q % 2].dma_start(out_2[0, SCALE_ROWS * q : SCALE_ROWS * (q + 1), :].bitcast(I32), rows.bitcast(I32))
+            rows = y_s[QUADRANT * q : QUADRANT * q + SCALE_ROWS * (T // HALF), :]
+            stored = out_2[0, SCALE_ROWS * q : SCALE_ROWS * (q + 1), :].rearrange("r (c n) -> c r n", n=HALF)
+            (nc.scalar, nc.sync)[q % 2].dma_start(stored.bitcast(I32), rows.bitcast(I32))

@@ -64,19 +64,20 @@ def tile_list_rgg_reluP_kernel(
         operand_bytes = 4 * PASSES * N
         grouped_at, page2_at = page_bytes, 2 * page_bytes
         wa_codes_at = page2_at + page_bytes
-        parted0_at = wa_codes_at + operand_bytes
+        gain_at = wa_codes_at + operand_bytes
+        parted0_at = gain_at + 4 * J
         wc_codes_at = parted0_at + 2 * operand_bytes
 
         def placed(name, shape, dtype, offset, align=64):
             return overlay.tile(shape, dtype, name=name, offset=offset, align_bytes=align)
 
-        w_s_raw = placed("w_s_raw", [P, 6, N], U8, parted0_at + operand_bytes // 2 - N)[:, 0:2, :]
+        w_s_raw = placed("w_s_raw", [P, 10, N], U8, parted0_at - N)[:, 0:2, :]
         nc.vector.memset(tab_s[:].bitcast(I32), 0)
         nc.vector.memset(w_s_raw.rearrange("p w n -> p (w n)").bitcast(I32), 0)
         pages = [held("page%d" % t, [P, T], F32) for t in range(2)]
         nc.vector.memset(pages[0][:].bitcast(I32), 0)
-        nc.vector.memset(pages[1][:, 0 : T // 2].bitcast(I32), 0)
-        nc.gpsimd.memset(pages[1][:, T // 2 - 8 : T], 0.0)
+        nc.vector.memset(pages[1][:, 0 : 3 * T // 4].bitcast(I32), 0)
+        nc.gpsimd.memset(pages[1][:, 3 * T // 4 - 8 : T], 0.0)
         warm_in = placed("warm_in", [P, 9], F32, wa_codes_at - 32, align=32)
         warm_out = held("warm_out", [P, 9], F32)
         nc.vector.memset(warm_in[:], 0.0)
@@ -154,7 +155,7 @@ def tile_list_rgg_reluP_kernel(
         w_s_second = held("w_s_second", [P, 2, N], U8)
         lift_second_pass(w_s_second, w_s)
         w_planes = (w_s, w_s_second)
-        gain = held("gain", [P, J], F32)
+        gain = placed("gain", [P, J], F32, gain_at)
         nc.sync.dma_start(gain[:], wgo)
         for which in (TARGET, SOURCE):
             tile = placed("parted0_%d" % which, [P, 1, PASSES, 2 * HALF], U8, parted0_at + which * 4 * HALF)
@@ -197,8 +198,10 @@ def tile_list_rgg_reluP_kernel(
                 wc_cols = wc_codes[:, a, m].bitcast(FP8X4)
                 nc.tensor.matmul_mx(ms, wc_cols, wc_s[:, a, m], v, v_s, start=(a == 0), stop=(a == PASSES - 1))
 
-            if h == 0:
+            if (t, h) == (0, 0):
                 steps = (gate_pass, 0), (gate_pass, 1), (message_pass, 0), (message_pass, 1)
+            elif h == 0:
+                steps = (message_pass, 0), (message_pass, 1), (gate_pass, 0), (gate_pass, 1)
             else:
                 steps = (gate_pass, 0), (message_pass, 0), (message_pass, 1), (gate_pass, 1)
             for step, a in steps:
@@ -210,11 +213,8 @@ def tile_list_rgg_reluP_kernel(
         def empty(t, h):
             za, ms = bank(banks.pop(0)), bank(banks.pop(0))
             multiply(t, h, za, ms)
-            if h == 0:
-                nc.scalar.activation(etas[t][:, half(h)], za, ACT.Sigmoid)
             nc.scalar.activation(positives[t][:, half(h)], ms, ACT.Relu)
-            if h == 1:
-                nc.scalar.activation(etas[t][:, half(h)], za, ACT.Sigmoid)
+            nc.scalar.activation(etas[t][:, half(h)], za, ACT.Sigmoid)
 
         def place(t, cols, offsets):
             weighted = held("weighted", [P, cols.stop - cols.start], F32)

@@ -27,7 +27,8 @@ LINE = 16
 HALF = 512
 HALVES = J // HALF
 QUANTISED = ((0, 512), (512, 1024), (1024, 1536), (1536, 1792), (1792, 2048))
-VECTOR_COLUMNS = 768
+VECTOR_CLEARS = 768
+VECTOR_COLUMNS = 960
 SOURCE, TARGET = 0, 1
 WA, WB = 0, 1
 LAST = PACK - 1
@@ -62,22 +63,35 @@ def tile_list_rgg_reluP_kernel(
         tab_s = held("tab_s", [P, T], U8)
         page_bytes = 4 * T
         operand_bytes = 4 * PASSES * N
-        grouped_at, page2_at = page_bytes, 2 * page_bytes
+        piece_bytes = 4 * PACK * (N // 2)
+        grouped_at, page2_at = 0, page_bytes
         wa_codes_at = page2_at + page_bytes
-        gain_at = wa_codes_at + operand_bytes
-        parted0_at = gain_at + 4 * J
-        wc_codes_at = parted0_at + 2 * operand_bytes
+        wc_raw2_at = wa_codes_at + operand_bytes // 2
+        wc_raw_last_at = wc_raw2_at + piece_bytes
+        page1_at = wc_raw_last_at + piece_bytes
+        wc_codes_at = page1_at + page_bytes
 
         def placed(name, shape, dtype, offset, align=64):
             return overlay.tile(shape, dtype, name=name, offset=offset, align_bytes=align)
 
-        w_s_raw = placed("w_s_raw", [P, 10, N], U8, parted0_at - N)[:, 0:2, :]
+        w_s_raw = placed("w_s_raw", [P, page1_at - wa_codes_at + 128], U8, wa_codes_at - 64)[:, 0 : 2 * N]
+        rows_at = P - QUADRANT
         nc.vector.memset(tab_s[:].bitcast(I32), 0)
-        nc.vector.memset(w_s_raw.rearrange("p w n -> p (w n)").bitcast(I32), 0)
-        pages = [held("page%d" % t, [P, T], F32) for t in range(2)]
+        nc.vector.memset(w_s_raw[0:rows_at].bitcast(I32), 0)
+        pages = [held("page0", [P, T], F32)]
         nc.vector.memset(pages[0][:].bitcast(I32), 0)
-        nc.vector.memset(pages[1][:, 0 : 3 * T // 4].bitcast(I32), 0)
-        nc.gpsimd.memset(pages[1][:, 3 * T // 4 - 8 : T], 0.0)
+
+        nc.sync.dma_start(lists[SOURCE][:], offs)
+        for w, scales in enumerate((wa_scales, wb_scales)):
+            nc.sync.dma_start(
+                w_s_raw[rows_at:P, w * N : (w + 1) * N].bitcast(I32), scales.rearrange("a q n -> (a q) n").bitcast(I32)
+            )
+        w_s = held("w_s", [P, 2, N], U8)
+        deal_columns(nc.vector, w_s[:], w_s_raw.rearrange("p (w n) -> p w n", w=2), 1)
+
+        pages.append(placed("page1", [P, T], F32, page1_at))
+        nc.vector.memset(pages[1][:, 0:VECTOR_CLEARS].bitcast(I32), 0)
+        nc.gpsimd.memset(pages[1][:, VECTOR_CLEARS - 8 : T], 0.0)
         warm_in = placed("warm_in", [P, 9], F32, wa_codes_at - 32, align=32)
         warm_out = held("warm_out", [P, 9], F32)
         nc.vector.memset(warm_in[:], 0.0)
@@ -88,21 +102,25 @@ def tile_list_rgg_reluP_kernel(
 
         wc_rows = wc.rearrange("(a p i) n -> a p i n", p=P, i=PACK)
         wc_grouped = placed("wc_grouped", [P, PASSES, N * PACK], BF16, grouped_at)
+        w_planes = [held("w_plane%d" % a, [P, 2 * N], U8) for a in range(PASSES)]
 
-        def load_weight_scales(first, last):
+        def spread_weight_scales(first, last):
             for index in range(first, last):
-                w, r = divmod(index, SCALE_ROWS)
-                nc.sync.dma_start(w_s_raw[r:P:PASS_GAP, w, :].bitcast(I32), scale_rows((wa_scales, wb_scales)[w], r))
+                a, q = divmod(index, P // QUADRANT)
+                row = rows_at + PASS_GAP * a + SCALE_ROWS * q
+                nc.sync.dma_start(
+                    w_planes[a][QUADRANT * q : QUADRANT * q + SCALE_ROWS].bitcast(I32),
+                    w_s[row : row + SCALE_ROWS].rearrange("p w n -> p (w n)").bitcast(I32),
+                )
 
-        def load_and_round_wc(a, n0, n1, name):
-            raw = held(name, [P, PACK, n1 - n0], F32)
+        def load_and_round_wc(a, n0, n1, raw):
             nc.sync.dma_start(raw[:], wc_rows[a][:, :, n0:n1])
             nc.scalar.copy(
                 wc_grouped[:, a, :].rearrange("p (t m i) -> p m i t", t=PACK, i=PACK)[:, n0 // PACK : n1 // PACK],
                 raw[:].rearrange("p i (m t) -> p m i t", t=PACK),
             )
 
-        nc.sync.dma_start(lists[SOURCE][:], offs)
+        piece = [P, PACK, N // 2]
         wa_raw = held("wa_raw", [P, PASSES, 2 * N], U8)
         nc.sync.dma_start(wa_raw[:].bitcast(I32), wa_words.rearrange("a p b -> p a b").bitcast(I32))
         for r in range(SCALE_ROWS):
@@ -110,14 +128,15 @@ def tile_list_rgg_reluP_kernel(
         nc.sync.dma_start(lists[TARGET][:], offs2)
         tab_w = held("tab_w", [P, T], I32)
         nc.sync.dma_start(tab_w[:], tab_words[0].rearrange("p t b -> p (t b)").bitcast(I32))
-        load_and_round_wc(0, 0, N // 2, "wc_raw0")
         wb_raw = held("wb_raw", [P, PASSES, N], I32)
         nc.sync.dma_start(wb_raw[:], wb_words.rearrange("a p n b -> p a (n b)").bitcast(I32))
-        load_weight_scales(0, 5)
-        load_and_round_wc(0, N // 2, N, "wc_raw1")
-        load_weight_scales(5, 8)
-        load_and_round_wc(1, 0, N // 2, "wc_raw2")
-        load_and_round_wc(1, N // 2, N, "wc_raw_last")
+        load_and_round_wc(0, 0, N // 2, held("wc_raw0", piece, F32))
+        load_and_round_wc(0, N // 2, N, held("wc_raw1", piece, F32))
+        spread_weight_scales(0, 4)
+        load_and_round_wc(1, 0, N // 2, placed("wc_raw2", piece, F32, wc_raw2_at))
+        spread_weight_scales(4, 5)
+        load_and_round_wc(1, N // 2, N, placed("wc_raw_last", piece, F32, wc_raw_last_at))
+        spread_weight_scales(5, 8)
 
         picked_s = {}
         parted = {}
@@ -150,18 +169,13 @@ def tile_list_rgg_reluP_kernel(
         deal_columns(nc.gpsimd, wa_codes[:].bitcast(U16), wa_raw[:].bitcast(U16), 2)
         wb_codes = held("wb_codes", [P, PASSES, N], I32)
         deal_columns(nc.gpsimd, wb_codes[:], wb_raw[:], 4)
-        w_s = held("w_s", [P, 2, N], U8)
-        deal_columns(nc.vector, w_s[:], w_s_raw, 1)
-        w_s_second = held("w_s_second", [P, 2, N], U8)
-        lift_second_pass(w_s_second, w_s)
-        w_planes = (w_s, w_s_second)
-        gain = placed("gain", [P, J], F32, gain_at)
+        gain = held("gain", [P, J], F32, tag="wc_raw0")
         nc.sync.dma_start(gain[:], wgo)
         for which in (TARGET, SOURCE):
-            tile = placed("parted0_%d" % which, [P, 1, PASSES, 2 * HALF], U8, parted0_at + which * 4 * HALF)
+            tile = held("parted0_%d" % which, [P, 1, PASSES, 2 * HALF], U8)
             part_words(tile[:], words[:, which : which + 1, half(0)])
             parted[0, which] = tile[:, 0]
-        tile = placed("parted1", [P, 2, PASSES, 2 * HALF], U8, parted0_at + operand_bytes)
+        tile = held("parted1", [P, 2, PASSES, 2 * HALF], U8)
         part_words(tile[:], words[:, :, half(1)])
         for which in (SOURCE, TARGET):
             parted[1, which] = tile[:, which]
@@ -172,7 +186,7 @@ def tile_list_rgg_reluP_kernel(
             scales=wc_s[:].rearrange("p a n -> p (a n)"),
             in_=wc_grouped[:].rearrange("p a n -> p (a n)"),
         )
-        pick_scales(1, placed("picked_s1", [P, 2 * HALF], U8, grouped_at))
+        pick_scales(1, placed("picked_s1", [P, 2 * HALF], U8, wc_raw_last_at + 4 * HALF))
 
         messages = [held("message%d" % t, [P, J], F32) for t in range(PACK)]
 
@@ -188,10 +202,10 @@ def tile_list_rgg_reluP_kernel(
             def gate_pass(a):
                 v, v_s = table_operand(TARGET, h, a)
                 wa_cols = wa_codes[:, a, 2 * t * P : 2 * (t + 1) * P].bitcast(FP4X4)
-                nc.tensor.matmul_mx(za, wa_cols, w_planes[a][:, WA, m], v, v_s, start=(a == 0), stop=False)
+                nc.tensor.matmul_mx(za, wa_cols, w_planes[a][:, WA * N + t * P : WA * N + (t + 1) * P], v, v_s, start=(a == 0), stop=False)
                 v, v_s = table_operand(SOURCE, h, a)
                 wb_cols = wb_codes[:, a, m].bitcast(FP8X4)
-                nc.tensor.matmul_mx(za, wb_cols, w_planes[a][:, WB, m], v, v_s, start=False, stop=(a == PASSES - 1))
+                nc.tensor.matmul_mx(za, wb_cols, w_planes[a][:, WB * N + t * P : WB * N + (t + 1) * P], v, v_s, start=False, stop=(a == PASSES - 1))
 
             def message_pass(a):
                 v, v_s = table_operand(SOURCE, h, a)
@@ -225,7 +239,7 @@ def tile_list_rgg_reluP_kernel(
         za, ms = bank(0, 7), bank(7)
         banks = [b % 7 for b in range(14)]
         multiply(0, 0, za, ms)
-        eta = held("first_eta", [P, HALF], F32, tag="wc_raw_last")
+        eta = placed("first_eta", [P, HALF], F32, wc_raw_last_at)
         nc.scalar.activation(eta[:], za, ACT.Sigmoid)
         gated = placed("first_gated", [P, HALF], F32, grouped_at + 2 * HALF)
         nc.gpsimd.tensor_tensor(gated[:], eta[:], gain[:, half(0)], ALU.mult)
@@ -245,14 +259,17 @@ def tile_list_rgg_reluP_kernel(
             nc.sync.dma_start(out_rows[:, t, :], pages[t][:])
 
         low_pair = placed("low_pair", [P, T, 2], BF16, wc_codes_at)
-        rounded = [held("rounded%d" % c, [P, c1 - c0, PACK], BF16) for c, (c0, c1) in enumerate(QUANTISED)]
+        rounded = held("rounded", [P, T * PACK], BF16)
+
+        def columns(first, last):
+            return rounded[:, first * PACK : last * PACK].rearrange("p (c t) -> p c t", t=PACK), slice(first, last)
 
         def pieces(first, last):
             found = []
-            for c, (c0, c1) in enumerate(QUANTISED):
+            for c0, c1 in QUANTISED:
                 lo, hi = max(first, c0), min(last, c1)
                 if lo < hi:
-                    found.append((rounded[c][:, lo - c0 : hi - c0, :], slice(lo, hi)))
+                    found.append(columns(lo, hi))
             return found
 
         for t in range(2):
@@ -260,26 +277,26 @@ def tile_list_rgg_reluP_kernel(
         place(LAST, slice(0, J), lists[TARGET][:])
         nc.sync.dma_start(out_rows[:, LAST, :], pages[LAST][:])
         low_words = low_pair[:].rearrange("p c e -> p (c e)").bitcast(U32)
-        for view, cols in pieces(0, T):
+        for view, cols in [columns(0, VECTOR_COLUMNS), columns(VECTOR_COLUMNS, T)]:
             both_words = view.rearrange("p c t -> p (c t)").bitcast(U32).rearrange("p (c u) -> p c u", u=2)
             nc.scalar.copy(both_words, low_words[:, cols].unsqueeze(2).to_broadcast([P, cols.stop - cols.start, 2]))
-        for view, cols in pieces(0, VECTOR_COLUMNS):
+        for view, cols in [columns(0, VECTOR_COLUMNS)]:
             twice = pages[2][:, cols].unsqueeze(2).to_broadcast([P, cols.stop - cols.start, 2])
             nc.gpsimd.tensor_scalar(view[:, :, 2:PACK], twice, 1.0, -0.0, ALU.mult, ALU.add)
-        for view, cols in pieces(VECTOR_COLUMNS, T):
+        for view, cols in [columns(VECTOR_COLUMNS, T)]:
             nc.scalar.copy(view[:, :, 2], pages[2][:, cols])
         for view, cols in pieces(0, VECTOR_COLUMNS):
             nc.vector.tensor_copy(view[:, :, LAST], pages[LAST][:, cols])
         for view, cols in pieces(VECTOR_COLUMNS, T):
             nc.scalar.copy(view[:, :, LAST], pages[LAST][:, cols])
 
-        y_s = held("y_s", [P, HALF], U8)
+        y_s = held("y_s", [P, T // 2], U8)
         out_words = out_1[0].rearrange("p t b -> p (t b)").bitcast(I32)
         for c, (c0, c1) in enumerate(QUANTISED):
             y_codes = held("y_codes%d" % c, [P, c1 - c0], I32)
-            nc.vector.quantize_mx(out=y_codes[:].bitcast(FP8X4), scales=y_s[SCALE_ROWS * (c0 // HALF) : P, c0 % HALF : c0 % HALF + c1 - c0], in_=rounded[c][:].rearrange("p c t -> p (c t)"))
+            nc.vector.quantize_mx(out=y_codes[:].bitcast(FP8X4), scales=y_s[SCALE_ROWS * (c0 // J) : P, c0 % J : c0 % J + c1 - c0], in_=rounded[:, c0 * PACK : c1 * PACK])
             nc.sync.dma_start(out_words[:, c0:c1], y_codes[:])
         for q in range(P // QUADRANT):
-            rows = y_s[QUADRANT * q : QUADRANT * q + SCALE_ROWS * (T // HALF), :]
-            stored = out_2[0, SCALE_ROWS * q : SCALE_ROWS * (q + 1), :].rearrange("r (c n) -> c r n", n=HALF)
+            rows = y_s[QUADRANT * q : QUADRANT * q + SCALE_ROWS * 2, :]
+            stored = out_2[0, SCALE_ROWS * q : SCALE_ROWS * (q + 1), :].rearrange("r (c n) -> c r n", n=J)
             (nc.scalar, nc.sync)[q % 2].dma_start(stored.bitcast(I32), rows.bitcast(I32))

@@ -27,7 +27,7 @@ LINE = 16
 HALF = 512
 HALVES = J // HALF
 QUANTISED = ((0, 512), (512, 1024), (1024, 1536), (1536, 1792), (1792, 2048))
-VECTOR_CLEARS = 768
+VECTOR_CLEARS = 1024
 VECTOR_COLUMNS = 960
 SOURCE, TARGET = 0, 1
 WA, WB = 0, 1
@@ -49,8 +49,11 @@ def tile_list_rgg_reluP_kernel(
         def scale_rows(scales, r):
             return scales.rearrange("a (q r) n -> r q a n", r=SCALE_ROWS)[r].bitcast(I32)
 
-        def lift_second_pass(second, both):
-            nc.sync.dma_start(second[0 : P - PASS_GAP].bitcast(I32), both[PASS_GAP:P].bitcast(I32))
+        def lift_second_pass(second, both, pieces):
+            for first, count in pieces:
+                nc.sync.dma_start(
+                    second[first : first + count].bitcast(I32), both[first + PASS_GAP : first + PASS_GAP + count].bitcast(I32)
+                )
 
         def deal_columns(engine, dealt, raw, element_bytes):
             i = LINE // element_bytes
@@ -66,20 +69,21 @@ def tile_list_rgg_reluP_kernel(
         piece_bytes = 4 * PACK * (N // 2)
         grouped_at, page2_at = 0, page_bytes
         wa_codes_at = page2_at + page_bytes
-        wc_raw2_at = wa_codes_at + operand_bytes // 2
+        wc_raw1_at = wa_codes_at + operand_bytes // 2
+        wc_raw2_at = wc_raw1_at + piece_bytes
         wc_raw_last_at = wc_raw2_at + piece_bytes
-        page1_at = wc_raw_last_at + piece_bytes
-        wc_codes_at = page1_at + page_bytes
+        wc_codes_at = wc_raw_last_at + piece_bytes
 
         def placed(name, shape, dtype, offset, align=64):
             return overlay.tile(shape, dtype, name=name, offset=offset, align_bytes=align)
 
-        w_s_raw = placed("w_s_raw", [P, page1_at - wa_codes_at + 128], U8, wa_codes_at - 64)[:, 0 : 2 * N]
+        w_s_raw = placed("w_s_raw", [P, wc_codes_at - wa_codes_at], U8, wa_codes_at - 64)[:, 0 : 2 * N]
         rows_at = P - QUADRANT
         nc.vector.memset(tab_s[:].bitcast(I32), 0)
         nc.vector.memset(w_s_raw[0:rows_at].bitcast(I32), 0)
-        pages = [held("page0", [P, T], F32)]
+        pages = [held("page%d" % t, [P, T], F32) for t in range(2)]
         nc.vector.memset(pages[0][:].bitcast(I32), 0)
+        nc.vector.memset(pages[1][:, 0:VECTOR_CLEARS].bitcast(I32), 0)
 
         nc.sync.dma_start(lists[SOURCE][:], offs)
         for w, scales in enumerate((wa_scales, wb_scales)):
@@ -89,16 +93,9 @@ def tile_list_rgg_reluP_kernel(
         w_s = held("w_s", [P, 2, N], U8)
         deal_columns(nc.vector, w_s[:], w_s_raw.rearrange("p (w n) -> p w n", w=2), 1)
 
-        pages.append(placed("page1", [P, T], F32, page1_at))
-        nc.vector.memset(pages[1][:, 0:VECTOR_CLEARS].bitcast(I32), 0)
         nc.gpsimd.memset(pages[1][:, VECTOR_CLEARS - 8 : T], 0.0)
-        warm_in = placed("warm_in", [P, 9], F32, wa_codes_at - 32, align=32)
-        warm_out = held("warm_out", [P, 9], F32)
-        nc.vector.memset(warm_in[:], 0.0)
-        nc.scalar.activation(warm_out[:], warm_in[:], ACT.Sigmoid)
-        pages.append(placed("page2", [P, T], F32, page2_at))
-        nc.gpsimd.memset(pages[2][:], 0.0)
-        pages.append(pages[0])
+        warm_out = held("warm_out", [P, 8], F32)
+        nc.scalar.activation(warm_out[:], pages[0][:, 0:8], ACT.Sigmoid)
 
         wc_rows = wc.rearrange("(a p i) n -> a p i n", p=P, i=PACK)
         wc_grouped = placed("wc_grouped", [P, PASSES, N * PACK], BF16, grouped_at)
@@ -123,6 +120,11 @@ def tile_list_rgg_reluP_kernel(
         piece = [P, PACK, N // 2]
         wa_raw = held("wa_raw", [P, PASSES, 2 * N], U8)
         nc.sync.dma_start(wa_raw[:].bitcast(I32), wa_words.rearrange("a p b -> p a b").bitcast(I32))
+        wa_codes = placed("wa_codes", [P, PASSES, 2 * N], U8, wa_codes_at)
+        deal_columns(nc.gpsimd, wa_codes[:].bitcast(U16), wa_raw[:].bitcast(U16), 2)
+        pages.append(placed("page2", [P, T], F32, page2_at))
+        nc.gpsimd.memset(pages[2][:], 0.0)
+        pages.append(pages[0])
         for r in range(SCALE_ROWS):
             nc.sync.dma_start(tab_s[r:P:PASS_GAP, :].bitcast(I32), scale_rows(tab_scales, r))
         nc.sync.dma_start(lists[TARGET][:], offs2)
@@ -131,12 +133,11 @@ def tile_list_rgg_reluP_kernel(
         wb_raw = held("wb_raw", [P, PASSES, N], I32)
         nc.sync.dma_start(wb_raw[:], wb_words.rearrange("a p n b -> p a (n b)").bitcast(I32))
         load_and_round_wc(0, 0, N // 2, held("wc_raw0", piece, F32))
-        load_and_round_wc(0, N // 2, N, held("wc_raw1", piece, F32))
-        spread_weight_scales(0, 4)
+        spread_weight_scales(0, 5)
+        load_and_round_wc(0, N // 2, N, placed("wc_raw1", piece, F32, wc_raw1_at))
         load_and_round_wc(1, 0, N // 2, placed("wc_raw2", piece, F32, wc_raw2_at))
-        spread_weight_scales(4, 5)
-        load_and_round_wc(1, N // 2, N, placed("wc_raw_last", piece, F32, wc_raw_last_at))
         spread_weight_scales(5, 8)
+        load_and_round_wc(1, N // 2, N, placed("wc_raw_last", piece, F32, wc_raw_last_at))
 
         picked_s = {}
         parted = {}
@@ -154,7 +155,7 @@ def tile_list_rgg_reluP_kernel(
             for which in (SOURCE, TARGET):
                 nc.vector.tensor_copy(both[:, slot(which)], tab_s[:].indirect(list_half(which, h)))
             second = held("picked_s_second%d" % h, [P, 2 * HALF], U8)
-            lift_second_pass(second, both)
+            lift_second_pass(second, both, ((0, P - PASS_GAP),) if h == 0 else ((0, 64), (64, 32), (96, 16)))
             picked_s[h] = (both, second)
 
         def part_words(tile, picked):
@@ -165,11 +166,9 @@ def tile_list_rgg_reluP_kernel(
         for which in (TARGET, SOURCE):
             nc.vector.tensor_copy(words[:, which, :].bitcast(U32), tab_w[:].bitcast(U32).indirect(lists[which][:]))
 
-        wa_codes = placed("wa_codes", [P, PASSES, 2 * N], U8, wa_codes_at)
-        deal_columns(nc.gpsimd, wa_codes[:].bitcast(U16), wa_raw[:].bitcast(U16), 2)
         wb_codes = held("wb_codes", [P, PASSES, N], I32)
         deal_columns(nc.gpsimd, wb_codes[:], wb_raw[:], 4)
-        gain = held("gain", [P, J], F32, tag="wc_raw0")
+        gain = placed("gain", [P, J], F32, wc_raw1_at)
         nc.sync.dma_start(gain[:], wgo)
         for which in (TARGET, SOURCE):
             tile = held("parted0_%d" % which, [P, 1, PASSES, 2 * HALF], U8)
@@ -225,7 +224,7 @@ def tile_list_rgg_reluP_kernel(
         positives = [held("positive%d" % t, [P, J], F32) for t in range(PACK)]
 
         def empty(t, h):
-            za, ms = bank(banks.pop(0)), bank(banks.pop(0))
+            za, ms = bank(*banks.pop(0)), bank(banks.pop(0))
             multiply(t, h, za, ms)
             nc.scalar.activation(positives[t][:, half(h)], ms, ACT.Relu)
             nc.scalar.activation(etas[t][:, half(h)], za, ACT.Sigmoid)
@@ -237,7 +236,7 @@ def tile_list_rgg_reluP_kernel(
             nc.vector.tensor_copy(pages[t][:].indirect(offsets), messages[t][:, cols])
 
         za, ms = bank(0, 7), bank(7)
-        banks = [b % 7 for b in range(14)]
+        banks = [(0, 1), 1, (2, 5), 7, (0, 1), 1, (3, 1), 4, (5, 1), 6, (2, 1), 7, (0, 1), 1]
         multiply(0, 0, za, ms)
         eta = placed("first_eta", [P, HALF], F32, wc_raw_last_at)
         nc.scalar.activation(eta[:], za, ACT.Sigmoid)
@@ -246,12 +245,8 @@ def tile_list_rgg_reluP_kernel(
         nc.vector.scalar_tensor_tensor(messages[0][:, half(0)], ms, 0.0, gated[:], ALU.max, ALU.mult)
         nc.vector.tensor_copy(pages[0][:].indirect(list_half(TARGET, 0)), messages[0][:, half(0)])
 
-        for t in range(1, LAST):
-            empty(t, 0)
-        for t in range(LAST):
-            empty(t, 1)
-        for h in range(HALVES):
-            empty(LAST, h)
+        for t, h in ((1, 0), (0, 1), (1, 1), (2, 0), (2, 1), (LAST, 0), (LAST, 1)):
+            empty(t, h)
         for t, h in ((1, 0), (0, 1), (1, 1), (2, 0), (2, 1)):
             place(t, half(h), list_half(TARGET, h))
         out_rows = out_0.rearrange("(p t) c -> p t c", t=PACK)

@@ -28,6 +28,7 @@ HALF = 512
 HALVES = J // HALF
 QUANTISED = ((0, 512), (512, 1024), (1024, 1536), (1536, 1792), (1792, 2048))
 VECTOR_CLEARS = 1024
+GPSIMD_FROM = 1792
 VECTOR_COLUMNS = 960
 SOURCE, TARGET = 0, 1
 WA, WB = 0, 1
@@ -180,11 +181,8 @@ def tile_list_rgg_reluP_kernel(
             parted[1, which] = tile[:, which]
         wc_codes = placed("wc_codes", [P, PASSES, N], U32, wc_codes_at)
         wc_s = held("wc_s", [P, PASSES, N], U8)
-        nc.vector.quantize_mx(
-            out=wc_codes[:].rearrange("p a n -> p (a n)").bitcast(FP8X4),
-            scales=wc_s[:].rearrange("p a n -> p (a n)"),
-            in_=wc_grouped[:].rearrange("p a n -> p (a n)"),
-        )
+        for a in range(PASSES):
+            nc.vector.quantize_mx(out=wc_codes[:, a, :].bitcast(FP8X4), scales=wc_s[:, a, :], in_=wc_grouped[:, a, :])
         pick_scales(1, placed("picked_s1", [P, 2 * HALF], U8, wc_raw_last_at + 4 * HALF))
 
         messages = [held("message%d" % t, [P, J], F32) for t in range(PACK)]
@@ -206,13 +204,15 @@ def tile_list_rgg_reluP_kernel(
                 wb_cols = wb_codes[:, a, m].bitcast(FP8X4)
                 nc.tensor.matmul_mx(za, wb_cols, w_planes[a][:, WB * N + t * P : WB * N + (t + 1) * P], v, v_s, start=False, stop=(a == PASSES - 1))
 
+            opening = 1 if (t, h) == (0, 0) else 0
+
             def message_pass(a):
                 v, v_s = table_operand(SOURCE, h, a)
                 wc_cols = wc_codes[:, a, m].bitcast(FP8X4)
-                nc.tensor.matmul_mx(ms, wc_cols, wc_s[:, a, m], v, v_s, start=(a == 0), stop=(a == PASSES - 1))
+                nc.tensor.matmul_mx(ms, wc_cols, wc_s[:, a, m], v, v_s, start=(a == opening), stop=(a != opening))
 
             if (t, h) == (0, 0):
-                steps = (gate_pass, 0), (gate_pass, 1), (message_pass, 0), (message_pass, 1)
+                steps = (gate_pass, 0), (gate_pass, 1), (message_pass, 1), (message_pass, 0)
             elif h == 0:
                 steps = (message_pass, 0), (message_pass, 1), (gate_pass, 0), (gate_pass, 1)
             else:
@@ -229,9 +229,12 @@ def tile_list_rgg_reluP_kernel(
             nc.scalar.activation(positives[t][:, half(h)], ms, ACT.Relu)
             nc.scalar.activation(etas[t][:, half(h)], za, ACT.Sigmoid)
 
-        def place(t, cols, offsets):
-            weighted = held("weighted", [P, cols.stop - cols.start], F32)
+        def weigh(t, cols, tag):
+            weighted = held("weighted", [P, cols.stop - cols.start], F32, tag=tag)
             nc.gpsimd.tensor_tensor(weighted[:], positives[t][:, cols], gain[:, cols], ALU.mult)
+            return weighted
+
+        def place(t, cols, offsets, weighted):
             nc.gpsimd.tensor_tensor(messages[t][:, cols], weighted[:], etas[t][:, cols], ALU.mult)
             nc.vector.tensor_copy(pages[t][:].indirect(offsets), messages[t][:, cols])
 
@@ -247,8 +250,14 @@ def tile_list_rgg_reluP_kernel(
 
         for t, h in ((1, 0), (0, 1), (1, 1), (2, 0), (2, 1), (LAST, 0), (LAST, 1)):
             empty(t, h)
-        for t, h in ((1, 0), (0, 1), (1, 1), (2, 0), (2, 1)):
-            place(t, half(h), list_half(TARGET, h))
+        for t, h in ((1, 0), (0, 1)):
+            place(t, half(h), list_half(TARGET, h), weigh(t, half(h), "even"))
+        ahead = weigh(1, half(1), "even")
+        units = [(1, half(1)), (2, half(0)), (2, half(1)), (LAST, slice(0, J))]
+        for u in range(len(units) - 1):
+            weighted, ahead = ahead, weigh(*units[u + 1], ("odd", "even")[u % 2])
+            t, cols = units[u]
+            place(t, cols, list_half(TARGET, cols.start // HALF), weighted)
         out_rows = out_0.rearrange("(p t) c -> p t c", t=PACK)
         for t in range(LAST):
             nc.sync.dma_start(out_rows[:, t, :], pages[t][:])
@@ -269,16 +278,16 @@ def tile_list_rgg_reluP_kernel(
 
         for t in range(2):
             nc.scalar.copy(low_pair[:, :, t], pages[t][:])
-        place(LAST, slice(0, J), lists[TARGET][:])
+        place(LAST, slice(0, J), lists[TARGET][:], ahead)
         nc.sync.dma_start(out_rows[:, LAST, :], pages[LAST][:])
         low_words = low_pair[:].rearrange("p c e -> p (c e)").bitcast(U32)
         for view, cols in [columns(0, VECTOR_COLUMNS), columns(VECTOR_COLUMNS, T)]:
             both_words = view.rearrange("p c t -> p (c t)").bitcast(U32).rearrange("p (c u) -> p c u", u=2)
             nc.scalar.copy(both_words, low_words[:, cols].unsqueeze(2).to_broadcast([P, cols.stop - cols.start, 2]))
-        for view, cols in [columns(0, VECTOR_COLUMNS)]:
+        for view, cols in [columns(0, VECTOR_COLUMNS), columns(GPSIMD_FROM, T)]:
             twice = pages[2][:, cols].unsqueeze(2).to_broadcast([P, cols.stop - cols.start, 2])
             nc.gpsimd.tensor_scalar(view[:, :, 2:PACK], twice, 1.0, -0.0, ALU.mult, ALU.add)
-        for view, cols in [columns(VECTOR_COLUMNS, T)]:
+        for view, cols in [columns(VECTOR_COLUMNS, GPSIMD_FROM)]:
             nc.scalar.copy(view[:, :, 2], pages[2][:, cols])
         for view, cols in pieces(0, VECTOR_COLUMNS):
             nc.vector.tensor_copy(view[:, :, LAST], pages[LAST][:, cols])

@@ -28,7 +28,8 @@ HALF = 512
 HALVES = J // HALF
 QUANTISED = ((0, 512), (512, 1024), (1024, 1536), (1536, 1792), (1792, 2048))
 VECTOR_CLEARS = 1024
-GPSIMD_FROM = 1792
+PAIRED = 512
+WOVEN = ((0, 1024), (1024, 1536), (1536, 2048))
 VECTOR_COLUMNS = 960
 SOURCE, TARGET = 0, 1
 WA, WB = 0, 1
@@ -229,13 +230,18 @@ def tile_list_rgg_reluP_kernel(
             nc.scalar.activation(positives[t][:, half(h)], ms, ACT.Relu)
             nc.scalar.activation(etas[t][:, half(h)], za, ACT.Sigmoid)
 
+        pairs = placed("pairs", [P, 2 * T * 2], BF16, wc_codes_at)
+
         def weigh(t, cols, tag):
-            weighted = held("weighted", [P, cols.stop - cols.start], F32, tag=tag)
-            nc.gpsimd.tensor_tensor(weighted[:], positives[t][:, cols], gain[:, cols], ALU.mult)
+            if t == LAST:
+                weighted = pairs[:, 2 * T + 3 * PAIRED : 2 * T + 3 * PAIRED + 2 * J].bitcast(F32)
+            else:
+                weighted = held("weighted", [P, cols.stop - cols.start], F32, tag=tag)[:]
+            nc.gpsimd.tensor_tensor(weighted, positives[t][:, cols], gain[:, cols], ALU.mult)
             return weighted
 
         def place(t, cols, offsets, weighted):
-            nc.gpsimd.tensor_tensor(messages[t][:, cols], weighted[:], etas[t][:, cols], ALU.mult)
+            nc.gpsimd.tensor_tensor(messages[t][:, cols], weighted, etas[t][:, cols], ALU.mult)
             nc.vector.tensor_copy(pages[t][:].indirect(offsets), messages[t][:, cols])
 
         za, ms = bank(0, 7), bank(7)
@@ -262,7 +268,7 @@ def tile_list_rgg_reluP_kernel(
         for t in range(LAST):
             nc.sync.dma_start(out_rows[:, t, :], pages[t][:])
 
-        low_pair = placed("low_pair", [P, T, 2], BF16, wc_codes_at)
+        low_pair, high_pair = [pairs[:, u * T * 2 : (u + 1) * T * 2].rearrange("p (c e) -> p c e", e=2) for u in range(2)]
         rounded = held("rounded", [P, T * PACK], BF16)
 
         def columns(first, last):
@@ -280,15 +286,18 @@ def tile_list_rgg_reluP_kernel(
             nc.scalar.copy(low_pair[:, :, t], pages[t][:])
         place(LAST, slice(0, J), lists[TARGET][:], ahead)
         nc.sync.dma_start(out_rows[:, LAST, :], pages[LAST][:])
-        low_words = low_pair[:].rearrange("p c e -> p (c e)").bitcast(U32)
-        for view, cols in [columns(0, VECTOR_COLUMNS), columns(VECTOR_COLUMNS, T)]:
+        pair_words = pairs[:].bitcast(U32).rearrange("p (u c) -> p c u", u=2)
+        for first in range(0, T, PAIRED):
+            cols = slice(first, first + PAIRED)
+            twice = pages[2][:, cols].unsqueeze(2).to_broadcast([P, PAIRED, 2])
+            if first == 0:
+                nc.scalar.copy(high_pair[:, cols], twice)
+            else:
+                nc.gpsimd.tensor_scalar(high_pair[:, cols], twice, 1.0, -0.0, ALU.mult, ALU.add)
+        for first, last in WOVEN:
+            view, cols = columns(first, last)
             both_words = view.rearrange("p c t -> p (c t)").bitcast(U32).rearrange("p (c u) -> p c u", u=2)
-            nc.scalar.copy(both_words, low_words[:, cols].unsqueeze(2).to_broadcast([P, cols.stop - cols.start, 2]))
-        for view, cols in [columns(0, VECTOR_COLUMNS), columns(GPSIMD_FROM, T)]:
-            twice = pages[2][:, cols].unsqueeze(2).to_broadcast([P, cols.stop - cols.start, 2])
-            nc.gpsimd.tensor_scalar(view[:, :, 2:PACK], twice, 1.0, -0.0, ALU.mult, ALU.add)
-        for view, cols in [columns(VECTOR_COLUMNS, GPSIMD_FROM)]:
-            nc.scalar.copy(view[:, :, 2], pages[2][:, cols])
+            nc.scalar.copy(both_words, pair_words[:, cols])
         for view, cols in pieces(0, VECTOR_COLUMNS):
             nc.vector.tensor_copy(view[:, :, LAST], pages[LAST][:, cols])
         for view, cols in pieces(VECTOR_COLUMNS, T):

@@ -26,7 +26,9 @@ PER_COLUMN = 16
 LINE = 16
 HALF = 512
 HALVES = J // HALF
-QUANTISED = ((0, 512), (512, 1024), (1024, 1536), (1536, 1792), (1792, 2048))
+ROUNDED = ((0, 512), (512, 1024), (1024, 1536), (1536, 1792), (1792, 2048))
+QUANTISED = 256
+STORED = 512
 VECTOR_CLEARS = 1024
 PAIRED = 512
 WOVEN = ((0, 1024), (1024, 1536), (1536, 2048))
@@ -259,11 +261,11 @@ def tile_list_rgg_reluP_kernel(
         for t, h in ((1, 0), (0, 1)):
             place(t, half(h), list_half(TARGET, h), weigh(t, half(h), "even"))
         ahead = weigh(1, half(1), "even")
-        units = [(1, half(1)), (2, half(0)), (2, half(1)), (LAST, slice(0, J))]
-        for u in range(len(units) - 1):
-            weighted, ahead = ahead, weigh(*units[u + 1], ("odd", "even")[u % 2])
-            t, cols = units[u]
-            place(t, cols, list_half(TARGET, cols.start // HALF), weighted)
+        place(1, half(1), list_half(TARGET, 1), ahead)
+        whole = slice(0, J)
+        weighted = weigh(2, whole, "even")
+        ahead = weigh(LAST, whole, None)
+        place(2, whole, lists[TARGET][:], weighted)
         out_rows = out_0.rearrange("(p t) c -> p t c", t=PACK)
         for t in range(LAST):
             nc.sync.dma_start(out_rows[:, t, :], pages[t][:])
@@ -276,7 +278,7 @@ def tile_list_rgg_reluP_kernel(
 
         def pieces(first, last):
             found = []
-            for c0, c1 in QUANTISED:
+            for c0, c1 in ROUNDED:
                 lo, hi = max(first, c0), min(last, c1)
                 if lo < hi:
                     found.append(columns(lo, hi))
@@ -303,13 +305,18 @@ def tile_list_rgg_reluP_kernel(
         for view, cols in pieces(VECTOR_COLUMNS, T):
             nc.scalar.copy(view[:, :, LAST], pages[LAST][:, cols])
 
-        y_s = held("y_s", [P, T // 2], U8)
+        y_s = held("y_s", [P, STORED], U8)
         out_words = out_1[0].rearrange("p t b -> p (t b)").bitcast(I32)
-        for c, (c0, c1) in enumerate(QUANTISED):
-            y_codes = held("y_codes%d" % c, [P, c1 - c0], I32)
-            nc.vector.quantize_mx(out=y_codes[:].bitcast(FP8X4), scales=y_s[SCALE_ROWS * (c0 // J) : P, c0 % J : c0 % J + c1 - c0], in_=rounded[:, c0 * PACK : c1 * PACK])
-            nc.sync.dma_start(out_words[:, c0:c1], y_codes[:])
+        for c in range(T // STORED):
+            y_codes = held("y_codes%d" % c, [P, STORED], I32)
+            for first in range(0, STORED, QUANTISED):
+                cols = slice(first, first + QUANTISED)
+                c0 = c * STORED + first
+                nc.vector.quantize_mx(
+                    out=y_codes[:, cols].bitcast(FP8X4), scales=y_s[SCALE_ROWS * c : P, cols], in_=rounded[:, c0 * PACK : (c0 + QUANTISED) * PACK]
+                )
+            nc.sync.dma_start(out_words[:, c * STORED : (c + 1) * STORED], y_codes[:])
         for q in range(P // QUADRANT):
-            rows = y_s[QUADRANT * q : QUADRANT * q + SCALE_ROWS * 2, :]
-            stored = out_2[0, SCALE_ROWS * q : SCALE_ROWS * (q + 1), :].rearrange("r (c n) -> c r n", n=J)
+            rows = y_s[QUADRANT * q : QUADRANT * q + SCALE_ROWS * (T // STORED), :]
+            stored = out_2[0, SCALE_ROWS * q : SCALE_ROWS * (q + 1), :].rearrange("r (c n) -> c r n", n=STORED)
             (nc.scalar, nc.sync)[q % 2].dma_start(stored.bitcast(I32), rows.bitcast(I32))

@@ -196,59 +196,52 @@ def tile_list_rgg_reluP_kernel(
         def bank(index, count=1):
             return psum.tile([P, count * HALF], F32, name="bank%d_%d" % (index, count), offset=index * 4 * HALF)[:, 0:HALF]
 
-        def multiply(t, h, za, ms):
+        def gate_pass(t, h, a, za):
+            v, v_s = table_operand(TARGET, h, a)
+            wa_cols = wa_codes[:, a, 2 * t * P : 2 * (t + 1) * P].bitcast(FP4X4)
+            nc.tensor.matmul_mx(za, wa_cols, w_planes[a][:, WA * N + t * P : WA * N + (t + 1) * P], v, v_s, start=(a == 0), stop=False)
+            v, v_s = table_operand(SOURCE, h, a)
+            wb_cols = wb_codes[:, a, t * P : (t + 1) * P].bitcast(FP8X4)
+            nc.tensor.matmul_mx(za, wb_cols, w_planes[a][:, WB * N + t * P : WB * N + (t + 1) * P], v, v_s, start=False, stop=(a == PASSES - 1))
+
+        def message_pass(t, h, a, ms, opening=0):
             m = slice(t * P, (t + 1) * P)
-
-            def gate_pass(a):
-                v, v_s = table_operand(TARGET, h, a)
-                wa_cols = wa_codes[:, a, 2 * t * P : 2 * (t + 1) * P].bitcast(FP4X4)
-                nc.tensor.matmul_mx(za, wa_cols, w_planes[a][:, WA * N + t * P : WA * N + (t + 1) * P], v, v_s, start=(a == 0), stop=False)
-                v, v_s = table_operand(SOURCE, h, a)
-                wb_cols = wb_codes[:, a, m].bitcast(FP8X4)
-                nc.tensor.matmul_mx(za, wb_cols, w_planes[a][:, WB * N + t * P : WB * N + (t + 1) * P], v, v_s, start=False, stop=(a == PASSES - 1))
-
-            opening = 1 if (t, h) == (0, 0) else 0
-
-            def message_pass(a):
-                v, v_s = table_operand(SOURCE, h, a)
-                wc_cols = wc_codes[:, a, m].bitcast(FP8X4)
-                nc.tensor.matmul_mx(ms, wc_cols, wc_s[:, a, m], v, v_s, start=(a == opening), stop=(a != opening))
-
-            if (t, h) == (0, 0):
-                steps = (gate_pass, 0), (gate_pass, 1), (message_pass, 1), (message_pass, 0)
-            elif h == 0:
-                steps = (message_pass, 0), (message_pass, 1), (gate_pass, 0), (gate_pass, 1)
-            else:
-                steps = (gate_pass, 0), (message_pass, 0), (message_pass, 1), (gate_pass, 1)
-            for step, a in steps:
-                step(a)
+            v, v_s = table_operand(SOURCE, h, a)
+            nc.tensor.matmul_mx(ms, wc_codes[:, a, m].bitcast(FP8X4), wc_s[:, a, m], v, v_s, start=(a == opening), stop=(a != opening))
 
         etas = [held("eta%d" % t, [P, J], F32) for t in range(PACK)]
         positives = [held("positive%d" % t, [P, J], F32) for t in range(PACK)]
 
-        def empty(t, h):
-            za, ms = bank(*banks.pop(0)), bank(banks.pop(0))
-            multiply(t, h, za, ms)
-            nc.scalar.activation(positives[t][:, half(h)], ms, ACT.Relu)
-            nc.scalar.activation(etas[t][:, half(h)], za, ACT.Sigmoid)
+        def positive_part(t, ms):
+            for a in range(PASSES):
+                message_pass(t, 0, a, ms)
+            nc.scalar.activation(positives[t][:, half(0)], ms, ACT.Relu)
 
-        pairs = placed("pairs", [P, 2 * T * 2], BF16, wc_codes_at)
+        def gate(t, za):
+            for a in range(PASSES):
+                gate_pass(t, 0, a, za)
+            nc.scalar.activation(etas[t][:, half(0)], za, ACT.Sigmoid)
 
-        def weigh(t, cols, tag):
-            if t == LAST:
-                weighted = pairs[:, 2 * T + 3 * PAIRED : 2 * T + 3 * PAIRED + 2 * J].bitcast(F32)
-            else:
-                weighted = held("weighted", [P, cols.stop - cols.start], F32, tag=tag)[:]
+        def second_half(t, za, ms):
+            gate_pass(t, 1, 0, za)
+            message_pass(t, 1, 0, ms)
+            message_pass(t, 1, 1, ms)
+            gate_pass(t, 1, 1, za)
+            nc.scalar.activation(positives[t][:, half(1)], ms, ACT.Relu)
+            nc.scalar.activation(etas[t][:, half(1)], za, ACT.Sigmoid)
+
+        def weigh(t, cols, weighted):
             nc.gpsimd.tensor_tensor(weighted, positives[t][:, cols], gain[:, cols], ALU.mult)
-            return weighted
 
         def place(t, cols, offsets, weighted):
             nc.gpsimd.tensor_tensor(messages[t][:, cols], weighted, etas[t][:, cols], ALU.mult)
             nc.vector.tensor_copy(pages[t][:].indirect(offsets), messages[t][:, cols])
 
         za, ms = bank(0, 7), bank(7)
-        banks = [(0, 1), 1, (2, 5), 7, (0, 1), 1, (3, 1), 4, (5, 1), 6, (2, 1), 7, (0, 1), 1]
-        multiply(0, 0, za, ms)
+        for a in range(PASSES):
+            gate_pass(0, 0, a, za)
+        for a in (1, 0):
+            message_pass(0, 0, a, ms, 1)
         eta = placed("first_eta", [P, HALF], F32, wc_raw_last_at)
         nc.scalar.activation(eta[:], za, ACT.Sigmoid)
         gated = placed("first_gated", [P, HALF], F32, grouped_at + 2 * HALF)
@@ -256,16 +249,30 @@ def tile_list_rgg_reluP_kernel(
         nc.vector.scalar_tensor_tensor(messages[0][:, half(0)], ms, 0.0, gated[:], ALU.max, ALU.mult)
         nc.vector.tensor_copy(pages[0][:].indirect(list_half(TARGET, 0)), messages[0][:, half(0)])
 
-        for t, h in ((1, 0), (0, 1), (1, 1), (2, 0), (2, 1), (LAST, 0), (LAST, 1)):
-            empty(t, h)
-        for t, h in ((1, 0), (0, 1)):
-            place(t, half(h), list_half(TARGET, h), weigh(t, half(h), "even"))
-        ahead = weigh(1, half(1), "even")
-        place(1, half(1), list_half(TARGET, 1), ahead)
+        positive_part(1, bank(1))
+        gate(1, bank(0))
+        positive_part(2, bank(0))
+        second_half(0, bank(2, 5), bank(7))
+        second_half(1, bank(0), bank(1))
+        gate(2, bank(3))
+        second_half(2, bank(5), bank(6))
+        positive_part(LAST, bank(7))
+        gate(LAST, bank(2))
+        second_half(LAST, bank(0), bank(1))
+
+        weighted = held("weighted", [P, J], F32)
+        weigh(1, half(0), weighted[:, half(1)])
+        place(1, half(0), list_half(TARGET, 0), weighted[:, half(1)])
+        weigh(2, half(0), weighted[:, half(0)])
+        for t in range(2):
+            weigh(t, half(1), weighted[:, half(1)])
+            place(t, half(1), list_half(TARGET, 1), weighted[:, half(1)])
+        weigh(2, half(1), weighted[:, half(1)])
         whole = slice(0, J)
-        weighted = weigh(2, whole, "even")
-        ahead = weigh(LAST, whole, None)
-        place(2, whole, lists[TARGET][:], weighted)
+        pairs = placed("pairs", [P, 2 * T * 2], BF16, wc_codes_at)
+        ahead = pairs[:, 2 * T + 3 * PAIRED : 2 * T + 3 * PAIRED + 2 * J].bitcast(F32)
+        weigh(LAST, whole, ahead)
+        place(2, whole, lists[TARGET][:], weighted[:])
         out_rows = out_0.rearrange("(p t) c -> p t c", t=PACK)
         for t in range(LAST):
             nc.sync.dma_start(out_rows[:, t, :], pages[t][:])

@@ -29,7 +29,7 @@ HALVES = J // HALF
 ROUNDED = ((0, 512), (512, 1024), (1024, 1536), (1536, 1792), (1792, 2048))
 QUANTISED = 256
 STORED = 512
-VECTOR_CLEARS = 1024
+VECTOR_CLEARS = 512
 PAIRED = 512
 WOVEN = ((0, 1024), (1024, 1536), (1536, 2048))
 VECTOR_COLUMNS = 960
@@ -59,9 +59,9 @@ def tile_list_rgg_reluP_kernel(
                     second[first : first + count].bitcast(I32), both[first + PASS_GAP : first + PASS_GAP + count].bitcast(I32)
                 )
 
-        def deal_columns(engine, dealt, raw, element_bytes):
+        def deal_columns(copy, dealt, raw, element_bytes):
             i = LINE // element_bytes
-            engine.tensor_copy(
+            copy(
                 dealt.rearrange("p a (t o i) -> p a o t i", t=PACK, i=i),
                 raw.rearrange("p a (o i t) -> p a o t i", t=PACK, i=i),
             )
@@ -73,7 +73,8 @@ def tile_list_rgg_reluP_kernel(
         piece_bytes = 4 * PACK * (N // 2)
         grouped_at, page2_at = 0, page_bytes
         wa_codes_at = page2_at + page_bytes
-        wc_raw1_at = wa_codes_at + operand_bytes // 2
+        wc_raw0_at = wa_codes_at + operand_bytes // 2
+        wc_raw1_at = wc_raw0_at + piece_bytes
         wc_raw2_at = wc_raw1_at + piece_bytes
         wc_raw_last_at = wc_raw2_at + piece_bytes
         wc_codes_at = wc_raw_last_at + piece_bytes
@@ -95,7 +96,7 @@ def tile_list_rgg_reluP_kernel(
                 w_s_raw[rows_at:P, w * N : (w + 1) * N].bitcast(I32), scales.rearrange("a q n -> (a q) n").bitcast(I32)
             )
         w_s = held("w_s", [P, 2, N], U8)
-        deal_columns(nc.vector, w_s[:], w_s_raw.rearrange("p (w n) -> p w n", w=2), 1)
+        deal_columns(nc.vector.tensor_copy, w_s[:], w_s_raw.rearrange("p (w n) -> p w n", w=2), 1)
 
         nc.gpsimd.memset(pages[1][:, VECTOR_CLEARS - 8 : T], 0.0)
         warm_out = held("warm_out", [P, 8], F32)
@@ -125,7 +126,7 @@ def tile_list_rgg_reluP_kernel(
         wa_raw = held("wa_raw", [P, PASSES, 2 * N], U8)
         nc.sync.dma_start(wa_raw[:].bitcast(I32), wa_words.rearrange("a p b -> p a b").bitcast(I32))
         wa_codes = placed("wa_codes", [P, PASSES, 2 * N], U8, wa_codes_at)
-        deal_columns(nc.gpsimd, wa_codes[:].bitcast(U16), wa_raw[:].bitcast(U16), 2)
+        deal_columns(nc.scalar.copy, wa_codes[:].bitcast(U16), wa_raw[:].bitcast(U16), 2)
         pages.append(placed("page2", [P, T], F32, page2_at))
         nc.gpsimd.memset(pages[2][:], 0.0)
         pages.append(pages[0])
@@ -136,12 +137,13 @@ def tile_list_rgg_reluP_kernel(
         nc.sync.dma_start(tab_w[:], tab_words[0].rearrange("p t b -> p (t b)").bitcast(I32))
         wb_raw = held("wb_raw", [P, PASSES, N], I32)
         nc.sync.dma_start(wb_raw[:], wb_words.rearrange("a p n b -> p a (n b)").bitcast(I32))
-        load_and_round_wc(0, 0, N // 2, held("wc_raw0", piece, F32))
-        spread_weight_scales(0, 5)
+        spread_weight_scales(0, 3)
+        load_and_round_wc(0, 0, N // 2, placed("wc_raw0", piece, F32, wc_raw0_at))
+        spread_weight_scales(3, 5)
         load_and_round_wc(0, N // 2, N, placed("wc_raw1", piece, F32, wc_raw1_at))
         load_and_round_wc(1, 0, N // 2, placed("wc_raw2", piece, F32, wc_raw2_at))
-        spread_weight_scales(5, 8)
         load_and_round_wc(1, N // 2, N, placed("wc_raw_last", piece, F32, wc_raw_last_at))
+        spread_weight_scales(5, 8)
 
         picked_s = {}
         parted = {}
@@ -171,7 +173,7 @@ def tile_list_rgg_reluP_kernel(
             nc.vector.tensor_copy(words[:, which, :].bitcast(U32), tab_w[:].bitcast(U32).indirect(lists[which][:]))
 
         wb_codes = held("wb_codes", [P, PASSES, N], I32)
-        deal_columns(nc.gpsimd, wb_codes[:], wb_raw[:], 4)
+        deal_columns(nc.gpsimd.tensor_copy, wb_codes[:], wb_raw[:], 4)
         gain = placed("gain", [P, J], F32, wc_raw1_at)
         nc.sync.dma_start(gain[:], wgo)
         for which in (TARGET, SOURCE):

@@ -29,7 +29,6 @@ HALVES = J // HALF
 ROUNDED = ((0, 512), (512, 1024), (1024, 1536), (1536, 1792), (1792, 2048))
 QUANTISED = 256
 STORED = 512
-VECTOR_CLEARS = 512
 PAIRED = 512
 WOVEN = ((0, 1024), (1024, 1536), (1536, 2048))
 VECTOR_COLUMNS = 960
@@ -71,34 +70,43 @@ def tile_list_rgg_reluP_kernel(
         page_bytes = 4 * T
         operand_bytes = 4 * PASSES * N
         piece_bytes = 4 * PACK * (N // 2)
-        grouped_at, page2_at = 0, page_bytes
-        wa_codes_at = page2_at + page_bytes
-        wc_raw0_at = wa_codes_at + operand_bytes // 2
+        grouped_at, page1_at = 0, page_bytes
+        page2_at = page1_at + page_bytes
+        wc_raw0_at = page2_at + page_bytes
         wc_raw1_at = wc_raw0_at + piece_bytes
         wc_raw2_at = wc_raw1_at + piece_bytes
-        wc_raw_last_at = wc_raw2_at + piece_bytes
-        wc_codes_at = wc_raw_last_at + piece_bytes
+        wb_raw_at = wc_raw2_at + piece_bytes
+        wc_raw_last_at = wb_raw_at + operand_bytes
+        wc_codes_at = wc_raw_last_at + LAST * 4 * HALF
+        wa_raw_at = wc_codes_at + 2 * page_bytes
 
         def placed(name, shape, dtype, offset, align=64):
             return overlay.tile(shape, dtype, name=name, offset=offset, align_bytes=align)
 
-        w_s_raw = placed("w_s_raw", [P, wc_codes_at - wa_codes_at], U8, wa_codes_at - 64)[:, 0 : 2 * N]
+        w_s_raw = placed("w_s_raw", [P, wb_raw_at - page1_at], U8, page1_at)[:, 0 : 2 * N]
         rows_at = P - QUADRANT
         nc.vector.memset(tab_s[:].bitcast(I32), 0)
         nc.vector.memset(w_s_raw[0:rows_at].bitcast(I32), 0)
-        pages = [held("page%d" % t, [P, T], F32) for t in range(2)]
+        pages = [held("page0", [P, T], F32)]
         nc.vector.memset(pages[0][:].bitcast(I32), 0)
-        nc.vector.memset(pages[1][:, 0:VECTOR_CLEARS].bitcast(I32), 0)
 
         nc.sync.dma_start(lists[SOURCE][:], offs)
         for w, scales in enumerate((wa_scales, wb_scales)):
             nc.sync.dma_start(
                 w_s_raw[rows_at:P, w * N : (w + 1) * N].bitcast(I32), scales.rearrange("a q n -> (a q) n").bitcast(I32)
             )
+        for r in range(SCALE_ROWS):
+            nc.sync.dma_start(tab_s[r:P:PASS_GAP, :].bitcast(I32), scale_rows(tab_scales, r))
+        tab_w = held("tab_w", [P, T], I32)
+        nc.sync.dma_start(tab_w[:], tab_words[0].rearrange("p t b -> p (t b)").bitcast(I32))
+        nc.sync.dma_start(lists[TARGET][:], offs2)
         w_s = held("w_s", [P, 2, N], U8)
         deal_columns(nc.vector.tensor_copy, w_s[:], w_s_raw.rearrange("p (w n) -> p w n", w=2), 1)
 
-        nc.gpsimd.memset(pages[1][:, VECTOR_CLEARS - 8 : T], 0.0)
+        for t, offset in ((1, page1_at), (2, page2_at)):
+            pages.append(placed("page%d" % t, [P, T], F32, offset))
+            nc.gpsimd.memset(pages[t][:], 0.0)
+        pages.append(pages[0])
         warm_out = held("warm_out", [P, 8], F32)
         nc.scalar.activation(warm_out[:], pages[0][:, 0:8], ACT.Sigmoid)
 
@@ -123,27 +131,19 @@ def tile_list_rgg_reluP_kernel(
             )
 
         piece = [P, PACK, N // 2]
-        wa_raw = held("wa_raw", [P, PASSES, 2 * N], U8)
+        wb_raw = placed("wb_raw", [P, PASSES * N + LINE], I32, wb_raw_at)[:, 0 : PASSES * N].rearrange("p (a n) -> p a n", a=PASSES)
+        nc.sync.dma_start(wb_raw, wb_words.rearrange("a p n b -> p a (n b)").bitcast(I32))
+        wb_codes = held("wb_codes", [P, PASSES, N], U32)
+        deal_columns(nc.scalar.copy, wb_codes[:], wb_raw.bitcast(U32), 4)
+        wa_raw = placed("wa_raw", [P, PASSES, 2 * N], U8, wa_raw_at)
         nc.sync.dma_start(wa_raw[:].bitcast(I32), wa_words.rearrange("a p b -> p a b").bitcast(I32))
-        wa_codes = placed("wa_codes", [P, PASSES, 2 * N], U8, wa_codes_at)
+        wa_codes = held("wa_codes", [P, PASSES, 2 * N], U8)
         deal_columns(nc.scalar.copy, wa_codes[:].bitcast(U16), wa_raw[:].bitcast(U16), 2)
-        pages.append(placed("page2", [P, T], F32, page2_at))
-        nc.gpsimd.memset(pages[2][:], 0.0)
-        pages.append(pages[0])
-        for r in range(SCALE_ROWS):
-            nc.sync.dma_start(tab_s[r:P:PASS_GAP, :].bitcast(I32), scale_rows(tab_scales, r))
-        nc.sync.dma_start(lists[TARGET][:], offs2)
-        tab_w = held("tab_w", [P, T], I32)
-        nc.sync.dma_start(tab_w[:], tab_words[0].rearrange("p t b -> p (t b)").bitcast(I32))
-        wb_raw = held("wb_raw", [P, PASSES, N], I32)
-        nc.sync.dma_start(wb_raw[:], wb_words.rearrange("a p n b -> p a (n b)").bitcast(I32))
-        spread_weight_scales(0, 3)
         load_and_round_wc(0, 0, N // 2, placed("wc_raw0", piece, F32, wc_raw0_at))
-        spread_weight_scales(3, 5)
+        spread_weight_scales(0, 4)
         load_and_round_wc(0, N // 2, N, placed("wc_raw1", piece, F32, wc_raw1_at))
+        spread_weight_scales(4, 8)
         load_and_round_wc(1, 0, N // 2, placed("wc_raw2", piece, F32, wc_raw2_at))
-        load_and_round_wc(1, N // 2, N, placed("wc_raw_last", piece, F32, wc_raw_last_at))
-        spread_weight_scales(5, 8)
 
         picked_s = {}
         parted = {}
@@ -151,133 +151,135 @@ def tile_list_rgg_reluP_kernel(
         def half(h):
             return slice(h * HALF, (h + 1) * HALF)
 
-        def slot(which):
-            return slice(which * HALF, (which + 1) * HALF)
-
         def list_half(which, h):
             return lists[which][:, h * HALF // PER_COLUMN : (h + 1) * HALF // PER_COLUMN]
 
-        def pick_scales(h, both):
-            for which in (SOURCE, TARGET):
-                nc.vector.tensor_copy(both[:, slot(which)], tab_s[:].indirect(list_half(which, h)))
-            second = held("picked_s_second%d" % h, [P, 2 * HALF], U8)
-            lift_second_pass(second, both, ((0, P - PASS_GAP),) if h == 0 else ((0, 64), (64, 32), (96, 16)))
-            picked_s[h] = (both, second)
+        def pick_scales(name, both, runs, pieces):
+            second = held(name, [P, len(runs) * HALF], U8)
+            for index, (which, h) in enumerate(runs):
+                nc.vector.tensor_copy(both[:, half(index)], tab_s[:].indirect(list_half(which, h)))
+                picked_s[which, h] = (both[:, half(index)], second[:, half(index)])
+            lift_second_pass(second, both, pieces)
 
         def part_words(tile, picked):
             nc.vector.tensor_copy(tile.bitcast(U16), picked.bitcast(U16).rearrange("p w (j a) -> p w a j", a=PASSES))
 
-        pick_scales(0, held("picked_s0", [P, 2 * HALF], U8))
-        words = held("picked_w", [P, 2, J], I32)
-        for which in (TARGET, SOURCE):
-            nc.vector.tensor_copy(words[:, which, :].bitcast(U32), tab_w[:].bitcast(U32).indirect(lists[which][:]))
+        early = ((SOURCE, 0), (SOURCE, 1), (TARGET, 0))
+        pick_scales("early_second", held("early_both", [P, len(early) * HALF], U8), early, ((0, P - PASS_GAP),))
+        load_and_round_wc(1, N // 2, N, placed("wc_raw_last", piece, F32, wc_raw_last_at))
 
-        wb_codes = held("wb_codes", [P, PASSES, N], I32)
-        deal_columns(nc.gpsimd.tensor_copy, wb_codes[:], wb_raw[:], 4)
+        def pick_words(h, words):
+            for which in (SOURCE, TARGET):
+                nc.vector.tensor_copy(words[:, which, :].bitcast(U32), tab_w[:].bitcast(U32).indirect(list_half(which, h)))
+            return words
+
+        words = pick_words(0, held("picked_w0", [P, 2, HALF], I32))
+
         gain = placed("gain", [P, J], F32, wc_raw1_at)
         nc.sync.dma_start(gain[:], wgo)
-        for which in (TARGET, SOURCE):
-            tile = held("parted0_%d" % which, [P, 1, PASSES, 2 * HALF], U8)
-            part_words(tile[:], words[:, which : which + 1, half(0)])
+        for which in (SOURCE, TARGET):
+            tile = placed("parted0_%d" % which, [P, 1, PASSES, 2 * HALF], U8, wb_raw_at + which * operand_bytes // 2)
+            part_words(tile[:], words[:, which : which + 1])
             parted[0, which] = tile[:, 0]
         tile = held("parted1", [P, 2, PASSES, 2 * HALF], U8)
-        part_words(tile[:], words[:, :, half(1)])
+        part_words(tile[:], pick_words(1, placed("picked_w1", [P, 2, HALF], I32, wa_raw_at))[:])
         for which in (SOURCE, TARGET):
             parted[1, which] = tile[:, which]
         wc_codes = placed("wc_codes", [P, PASSES, N], U32, wc_codes_at)
         wc_s = held("wc_s", [P, PASSES, N], U8)
         for a in range(PASSES):
             nc.vector.quantize_mx(out=wc_codes[:, a, :].bitcast(FP8X4), scales=wc_s[:, a, :], in_=wc_grouped[:, a, :])
-        pick_scales(1, placed("picked_s1", [P, 2 * HALF], U8, wc_raw_last_at + 4 * HALF))
+        late_both = placed("late_both", [P, HALF], U8, grouped_at)
+        pick_scales("late_second", late_both, ((TARGET, 1),), ((0, 64), (64, 32), (96, 16)))
 
         messages = [held("message%d" % t, [P, J], F32) for t in range(PACK)]
 
         def table_operand(which, h, a):
-            return parted[h, which][:, a, :].bitcast(FP4X4), picked_s[h][a][:, slot(which)]
+            return parted[h, which][:, a, :].bitcast(FP4X4), picked_s[which, h][a]
 
         def bank(index, count=1):
             return psum.tile([P, count * HALF], F32, name="bank%d_%d" % (index, count), offset=index * 4 * HALF)[:, 0:HALF]
 
-        def gate_pass(t, h, a, za):
-            v, v_s = table_operand(TARGET, h, a)
-            wa_cols = wa_codes[:, a, 2 * t * P : 2 * (t + 1) * P].bitcast(FP4X4)
-            nc.tensor.matmul_mx(za, wa_cols, w_planes[a][:, WA * N + t * P : WA * N + (t + 1) * P], v, v_s, start=(a == 0), stop=False)
+        def source_pass(t, h, a, za):
             v, v_s = table_operand(SOURCE, h, a)
             wb_cols = wb_codes[:, a, t * P : (t + 1) * P].bitcast(FP8X4)
-            nc.tensor.matmul_mx(za, wb_cols, w_planes[a][:, WB * N + t * P : WB * N + (t + 1) * P], v, v_s, start=False, stop=(a == PASSES - 1))
+            nc.tensor.matmul_mx(za, wb_cols, w_planes[a][:, WB * N + t * P : WB * N + (t + 1) * P], v, v_s, start=(a == 0), stop=False)
 
-        def message_pass(t, h, a, ms, opening=0):
+        def target_pass(t, h, a, za):
+            v, v_s = table_operand(TARGET, h, a)
+            wa_cols = wa_codes[:, a, 2 * t * P : 2 * (t + 1) * P].bitcast(FP4X4)
+            nc.tensor.matmul_mx(za, wa_cols, w_planes[a][:, WA * N + t * P : WA * N + (t + 1) * P], v, v_s, start=False, stop=(a == PASSES - 1))
+
+        def gate_pass(t, h, a, za):
+            source_pass(t, h, a, za)
+            target_pass(t, h, a, za)
+
+        def message_pass(t, h, a, ms):
             m = slice(t * P, (t + 1) * P)
             v, v_s = table_operand(SOURCE, h, a)
-            nc.tensor.matmul_mx(ms, wc_codes[:, a, m].bitcast(FP8X4), wc_s[:, a, m], v, v_s, start=(a == opening), stop=(a != opening))
+            nc.tensor.matmul_mx(ms, wc_codes[:, a, m].bitcast(FP8X4), wc_s[:, a, m], v, v_s, start=(a == PASSES - 1), stop=(a == 0))
 
-        etas = [held("eta%d" % t, [P, J], F32) for t in range(PACK)]
+        first_etas = placed("first_etas", [P, LAST * HALF], F32, wc_raw_last_at)
+        etas = {(t, 1): held("eta%d" % t, [P, HALF], F32)[:] for t in range(LAST)}
+        for t in range(LAST):
+            etas[t, 0] = first_etas[:, t * HALF : (t + 1) * HALF]
+        last_eta = held("last_eta", [P, J], F32)
+        for h in range(2):
+            etas[LAST, h] = last_eta[:, half(h)]
         positives = [held("positive%d" % t, [P, J], F32) for t in range(PACK)]
-
-        def positive_part(t, ms):
-            for a in range(PASSES):
-                message_pass(t, 0, a, ms)
-            nc.scalar.activation(positives[t][:, half(0)], ms, ACT.Relu)
 
         def gate(t, za):
             for a in range(PASSES):
                 gate_pass(t, 0, a, za)
-            nc.scalar.activation(etas[t][:, half(0)], za, ACT.Sigmoid)
+            nc.scalar.activation(etas[t, 0], za, ACT.Sigmoid)
+
+        def positive_part(t, h, ms):
+            for a in reversed(range(PASSES)):
+                message_pass(t, h, a, ms)
+            nc.scalar.activation(positives[t][:, half(h)], ms, ACT.Relu)
 
         def second_half(t, za, ms):
-            gate_pass(t, 1, 0, za)
-            message_pass(t, 1, 0, ms)
-            message_pass(t, 1, 1, ms)
-            gate_pass(t, 1, 1, za)
-            nc.scalar.activation(positives[t][:, half(1)], ms, ACT.Relu)
-            nc.scalar.activation(etas[t][:, half(1)], za, ACT.Sigmoid)
+            positive_part(t, 1, ms)
+            for a in range(PASSES):
+                source_pass(t, 1, a, za)
+            for a in range(PASSES):
+                target_pass(t, 1, a, za)
+            nc.scalar.activation(etas[t, 1], za, ACT.Sigmoid)
 
-        def weigh(t, cols, weighted):
-            nc.gpsimd.tensor_tensor(weighted, positives[t][:, cols], gain[:, cols], ALU.mult)
+        for t in range(LAST):
+            gate(t, bank(t))
+        ms = bank(3)
+        for a in reversed(range(PASSES)):
+            message_pass(0, 0, a, ms)
+        positive_part(1, 0, bank(4))
+        positive_part(2, 0, bank(5))
+        second_half(0, bank(0), bank(7))
 
-        def place(t, cols, offsets, weighted):
-            nc.gpsimd.tensor_tensor(messages[t][:, cols], weighted, etas[t][:, cols], ALU.mult)
-            nc.vector.tensor_copy(pages[t][:].indirect(offsets), messages[t][:, cols])
-
-        za, ms = bank(0, 7), bank(7)
-        for a in range(PASSES):
-            gate_pass(0, 0, a, za)
-        for a in (1, 0):
-            message_pass(0, 0, a, ms, 1)
-        eta = placed("first_eta", [P, HALF], F32, wc_raw_last_at)
-        nc.scalar.activation(eta[:], za, ACT.Sigmoid)
-        gated = placed("first_gated", [P, HALF], F32, grouped_at + 2 * HALF)
-        nc.gpsimd.tensor_tensor(gated[:], eta[:], gain[:, half(0)], ALU.mult)
-        nc.vector.scalar_tensor_tensor(messages[0][:, half(0)], ms, 0.0, gated[:], ALU.max, ALU.mult)
+        gated = placed("first_gated", [P, LAST * HALF], F32, grouped_at + 2 * HALF)
+        nc.gpsimd.tensor_tensor(gated[:, half(0)], etas[0, 0], gain[:, half(0)], ALU.mult)
+        nc.vector.scalar_tensor_tensor(messages[0][:, half(0)], ms, 0.0, gated[:, half(0)], ALU.max, ALU.mult)
         nc.vector.tensor_copy(pages[0][:].indirect(list_half(TARGET, 0)), messages[0][:, half(0)])
 
-        positive_part(1, bank(1))
-        gate(1, bank(0))
-        positive_part(2, bank(0))
-        second_half(0, bank(2, 5), bank(7))
-        second_half(1, bank(0), bank(1))
-        gate(2, bank(3))
-        second_half(2, bank(5), bank(6))
-        positive_part(LAST, bank(7))
-        gate(LAST, bank(2))
-        second_half(LAST, bank(0), bank(1))
+        gate(LAST, bank(1))
+        positive_part(LAST, 0, bank(2))
+        second_half(1, bank(3), bank(4))
+        second_half(2, bank(1), bank(2))
+        second_half(LAST, bank(0), bank(7))
 
-        weighted = held("weighted", [P, J], F32)
-        weigh(1, half(0), weighted[:, half(1)])
-        place(1, half(0), list_half(TARGET, 0), weighted[:, half(1)])
-        weigh(2, half(0), weighted[:, half(0)])
-        for t in range(2):
-            weigh(t, half(1), weighted[:, half(1)])
-            place(t, half(1), list_half(TARGET, 1), weighted[:, half(1)])
-        weigh(2, half(1), weighted[:, half(1)])
-        whole = slice(0, J)
+        def place(t, cols, offsets, weighted, first, second):
+            nc.gpsimd.tensor_tensor(weighted, first, gain[:, cols], ALU.mult)
+            nc.gpsimd.tensor_tensor(messages[t][:, cols], weighted, second, ALU.mult)
+            nc.vector.tensor_copy(pages[t][:].indirect(offsets), messages[t][:, cols])
+
+        out_rows = out_0.rearrange("(p t) c -> p t c", t=PACK)
+        weighted = placed("weighted", [P, J], F32, wc_codes_at + operand_bytes)
+        place(1, half(0), list_half(TARGET, 0), gated[:, half(1)], etas[1, 0], positives[1][:, half(0)])
+        place(2, half(0), list_half(TARGET, 0), gated[:, half(2)], etas[2, 0], positives[2][:, half(0)])
+        for t in range(LAST):
+            place(t, half(1), list_half(TARGET, 1), weighted[:, half(t % 2)], positives[t][:, half(1)], etas[t, 1])
+            nc.sync.dma_start(out_rows[:, t, :], pages[t][:])
         pairs = placed("pairs", [P, 2 * T * 2], BF16, wc_codes_at)
         ahead = pairs[:, 2 * T + 3 * PAIRED : 2 * T + 3 * PAIRED + 2 * J].bitcast(F32)
-        weigh(LAST, whole, ahead)
-        place(2, whole, lists[TARGET][:], weighted[:])
-        out_rows = out_0.rearrange("(p t) c -> p t c", t=PACK)
-        for t in range(LAST):
-            nc.sync.dma_start(out_rows[:, t, :], pages[t][:])
 
         low_pair, high_pair = [pairs[:, u * T * 2 : (u + 1) * T * 2].rearrange("p (c e) -> p c e", e=2) for u in range(2)]
         rounded = held("rounded", [P, T * PACK], BF16)
@@ -295,7 +297,7 @@ def tile_list_rgg_reluP_kernel(
 
         for t in range(2):
             nc.scalar.copy(low_pair[:, :, t], pages[t][:])
-        place(LAST, slice(0, J), lists[TARGET][:], ahead)
+        place(LAST, slice(0, J), lists[TARGET][:], ahead, positives[LAST][:], last_eta[:])
         nc.sync.dma_start(out_rows[:, LAST, :], pages[LAST][:])
         pair_words = pairs[:].bitcast(U32).rearrange("p (u c) -> p c u", u=2)
         for first in range(0, T, PAIRED):

@@ -272,7 +272,7 @@ def tile_list_rgg_reluP_kernel(
             nc.vector.tensor_copy(pages[t][:].indirect(offsets), messages[t][:, cols])
 
         out_rows = out_0.rearrange("(p t) c -> p t c", t=PACK)
-        weighted = placed("weighted", [P, J], F32, wc_codes_at + operand_bytes)
+        weighted = held("weighted", [P, J], F32)
         place(1, half(0), list_half(TARGET, 0), gated[:, half(1)], etas[1, 0], positives[1][:, half(0)])
         place(2, half(0), list_half(TARGET, 0), gated[:, half(2)], etas[2, 0], positives[2][:, half(0)])
         for t in range(LAST):

@@ -226,7 +226,13 @@ def tile_list_rgg_reluP_kernel(
         last_eta = held("last_eta", [P, J], F32)
         for h in range(2):
             etas[LAST, h] = last_eta[:, half(h)]
-        positives = [held("positive%d" % t, [P, J], F32) for t in range(PACK)]
+        late_positives = held("late_positives", [P, LAST * HALF], F32)
+        last_positive = held("last_positive", [P, J], F32)
+        positives = {(t, 0): held("positive%d" % t, [P, HALF], F32)[:] for t in range(1, LAST)}
+        for t in range(LAST):
+            positives[t, 1] = late_positives[:, half(t)]
+        for h in range(2):
+            positives[LAST, h] = last_positive[:, half(h)]
 
         def gate(t, za):
             for a in range(PASSES):
@@ -236,7 +242,7 @@ def tile_list_rgg_reluP_kernel(
         def positive_part(t, h, ms):
             for a in reversed(range(PASSES)):
                 message_pass(t, h, a, ms)
-            nc.scalar.activation(positives[t][:, half(h)], ms, ACT.Relu)
+            nc.scalar.activation(positives[t, h], ms, ACT.Relu)
 
         def second_half(t, za, ms):
             positive_part(t, 1, ms)
@@ -266,17 +272,32 @@ def tile_list_rgg_reluP_kernel(
         second_half(2, bank(1), bank(2))
         second_half(LAST, bank(0), bank(7))
 
-        def place(t, cols, offsets, weighted, first, second):
-            nc.gpsimd.tensor_tensor(weighted, first, gain[:, cols], ALU.mult)
-            nc.gpsimd.tensor_tensor(messages[t][:, cols], weighted, second, ALU.mult)
+        def weigh(weighted, values, cols):
+            nc.gpsimd.tensor_tensor(weighted, values, gain[:, cols], ALU.mult)
+
+        def weigh_two(weighted, values, h):
+            shape = [P, 2, HALF]
+            nc.gpsimd.tensor_tensor(
+                weighted.rearrange("p (u j) -> p u j", u=2),
+                values.rearrange("p (u j) -> p u j", u=2),
+                gain[:, half(h)].unsqueeze(1).to_broadcast(shape),
+                ALU.mult,
+            )
+
+        def place(t, cols, offsets, weighted, other):
+            nc.gpsimd.tensor_tensor(messages[t][:, cols], weighted, other, ALU.mult)
             nc.vector.tensor_copy(pages[t][:].indirect(offsets), messages[t][:, cols])
 
         out_rows = out_0.rearrange("(p t) c -> p t c", t=PACK)
+        weigh_two(gated[:, HALF:], first_etas[:, HALF:], 0)
+        for t in range(1, LAST):
+            place(t, half(0), list_half(TARGET, 0), gated[:, half(t)], positives[t, 0])
         weighted = held("weighted", [P, J], F32)
-        place(1, half(0), list_half(TARGET, 0), gated[:, half(1)], etas[1, 0], positives[1][:, half(0)])
-        place(2, half(0), list_half(TARGET, 0), gated[:, half(2)], etas[2, 0], positives[2][:, half(0)])
+        weigh_two(weighted[:], late_positives[:, 0:J], 1)
         for t in range(LAST):
-            place(t, half(1), list_half(TARGET, 1), weighted[:, half(t % 2)], positives[t][:, half(1)], etas[t, 1])
+            if t == 2:
+                weigh(weighted[:, half(0)], positives[t, 1], half(1))
+            place(t, half(1), list_half(TARGET, 1), weighted[:, half(t % 2)], etas[t, 1])
             nc.sync.dma_start(out_rows[:, t, :], pages[t][:])
         pairs = placed("pairs", [P, 2 * T * 2], BF16, wc_codes_at)
         ahead = pairs[:, 2 * T + 3 * PAIRED : 2 * T + 3 * PAIRED + 2 * J].bitcast(F32)
@@ -297,7 +318,8 @@ def tile_list_rgg_reluP_kernel(
 
         for t in range(2):
             nc.scalar.copy(low_pair[:, :, t], pages[t][:])
-        place(LAST, slice(0, J), lists[TARGET][:], ahead, positives[LAST][:], last_eta[:])
+        weigh(ahead, last_positive[:], slice(0, J))
+        place(LAST, slice(0, J), lists[TARGET][:], ahead, last_eta[:])
         nc.sync.dma_start(out_rows[:, LAST, :], pages[LAST][:])
         pair_words = pairs[:].bitcast(U32).rearrange("p (u c) -> p c u", u=2)
         for first in range(0, T, PAIRED):

@@ -75,15 +75,15 @@ def tile_list_rgg_reluP_kernel(
         wc_raw0_at = page2_at + page_bytes
         wc_raw1_at = wc_raw0_at + piece_bytes
         wc_raw2_at = wc_raw1_at + piece_bytes
-        wb_raw_at = wc_raw2_at + piece_bytes
-        wc_raw_last_at = wb_raw_at + operand_bytes
-        wc_codes_at = wc_raw_last_at + LAST * 4 * HALF
-        wa_raw_at = wc_codes_at + 2 * page_bytes
+        wa_raw_at = wc_raw2_at + piece_bytes
+        wc_raw_last_at = wa_raw_at + operand_bytes
+        wc_codes_at = wc_raw_last_at + PACK * 4 * HALF
+        wb_raw_at = wc_codes_at + 2 * page_bytes
 
         def placed(name, shape, dtype, offset, align=64):
             return overlay.tile(shape, dtype, name=name, offset=offset, align_bytes=align)
 
-        w_s_raw = placed("w_s_raw", [P, wb_raw_at - page1_at], U8, page1_at)[:, 0 : 2 * N]
+        w_s_raw = placed("w_s_raw", [P, wa_raw_at - page1_at], U8, page1_at)[:, 0 : 2 * N]
         rows_at = P - QUADRANT
         nc.vector.memset(tab_s[:].bitcast(I32), 0)
         nc.vector.memset(w_s_raw[0:rows_at].bitcast(I32), 0)
@@ -131,14 +131,14 @@ def tile_list_rgg_reluP_kernel(
             )
 
         piece = [P, PACK, N // 2]
-        wb_raw = placed("wb_raw", [P, PASSES * N + LINE], I32, wb_raw_at)[:, 0 : PASSES * N].rearrange("p (a n) -> p a n", a=PASSES)
-        nc.sync.dma_start(wb_raw, wb_words.rearrange("a p n b -> p a (n b)").bitcast(I32))
-        wb_codes = held("wb_codes", [P, PASSES, N], U32)
-        deal_columns(nc.scalar.copy, wb_codes[:], wb_raw.bitcast(U32), 4)
-        wa_raw = placed("wa_raw", [P, PASSES, 2 * N], U8, wa_raw_at)
-        nc.sync.dma_start(wa_raw[:].bitcast(I32), wa_words.rearrange("a p b -> p a b").bitcast(I32))
+        wa_raw = placed("wa_raw", [P, operand_bytes + 64], U8, wa_raw_at)[:, 0 : PASSES * 2 * N].rearrange("p (a b) -> p a b", a=PASSES)
+        nc.sync.dma_start(wa_raw.bitcast(I32), wa_words.rearrange("a p b -> p a b").bitcast(I32))
         wa_codes = held("wa_codes", [P, PASSES, 2 * N], U8)
-        deal_columns(nc.scalar.copy, wa_codes[:].bitcast(U16), wa_raw[:].bitcast(U16), 2)
+        deal_columns(nc.scalar.copy, wa_codes[:].bitcast(U16), wa_raw.bitcast(U16), 2)
+        wb_raw = placed("wb_raw", [P, PASSES, N], I32, wb_raw_at)
+        nc.sync.dma_start(wb_raw[:], wb_words.rearrange("a p n b -> p a (n b)").bitcast(I32))
+        wb_codes = held("wb_codes", [P, PASSES, N], U32)
+        deal_columns(nc.scalar.copy, wb_codes[:], wb_raw[:].bitcast(U32), 4)
         load_and_round_wc(0, 0, N // 2, placed("wc_raw0", piece, F32, wc_raw0_at))
         spread_weight_scales(0, 4)
         load_and_round_wc(0, N // 2, N, placed("wc_raw1", piece, F32, wc_raw1_at))
@@ -178,11 +178,11 @@ def tile_list_rgg_reluP_kernel(
         gain = placed("gain", [P, J], F32, wc_raw1_at)
         nc.sync.dma_start(gain[:], wgo)
         for which in (SOURCE, TARGET):
-            tile = placed("parted0_%d" % which, [P, 1, PASSES, 2 * HALF], U8, wb_raw_at + which * operand_bytes // 2)
+            tile = placed("parted0_%d" % which, [P, 1, PASSES, 2 * HALF], U8, wa_raw_at + which * operand_bytes // 2)
             part_words(tile[:], words[:, which : which + 1])
             parted[0, which] = tile[:, 0]
         tile = held("parted1", [P, 2, PASSES, 2 * HALF], U8)
-        part_words(tile[:], pick_words(1, placed("picked_w1", [P, 2, HALF], I32, wa_raw_at))[:])
+        part_words(tile[:], pick_words(1, placed("picked_w1", [P, 2, HALF], I32, wb_raw_at))[:])
         for which in (SOURCE, TARGET):
             parted[1, which] = tile[:, which]
         wc_codes = placed("wc_codes", [P, PASSES, N], U32, wc_codes_at)
@@ -219,20 +219,19 @@ def tile_list_rgg_reluP_kernel(
             v, v_s = table_operand(SOURCE, h, a)
             nc.tensor.matmul_mx(ms, wc_codes[:, a, m].bitcast(FP8X4), wc_s[:, a, m], v, v_s, start=(a == PASSES - 1), stop=(a == 0))
 
-        first_etas = placed("first_etas", [P, LAST * HALF], F32, wc_raw_last_at)
-        etas = {(t, 1): held("eta%d" % t, [P, HALF], F32)[:] for t in range(LAST)}
-        for t in range(LAST):
-            etas[t, 0] = first_etas[:, t * HALF : (t + 1) * HALF]
-        last_eta = held("last_eta", [P, J], F32)
-        for h in range(2):
-            etas[LAST, h] = last_eta[:, half(h)]
-        late_positives = held("late_positives", [P, LAST * HALF], F32)
-        last_positive = held("last_positive", [P, J], F32)
-        positives = {(t, 0): held("positive%d" % t, [P, HALF], F32)[:] for t in range(1, LAST)}
-        for t in range(LAST):
+        first_etas = placed("first_etas", [P, PACK * HALF], F32, wc_raw_last_at)
+        late_positives = held("late_positives", [P, J], F32)
+        etas, positives = {}, {(1, 0): held("positive1", [P, HALF], F32)[:]}
+        for t in range(2):
+            etas[t, 0] = first_etas[:, half(t)]
+            etas[t, 1] = held("eta%d" % t, [P, HALF], F32)[:]
             positives[t, 1] = late_positives[:, half(t)]
-        for h in range(2):
-            positives[LAST, h] = last_positive[:, half(h)]
+        whole_etas = {2: first_etas[:, J:], LAST: held("last_eta", [P, J], F32)[:]}
+        whole_positives = {t: held("positive%d" % t, [P, J], F32)[:] for t in (2, LAST)}
+        for t in (2, LAST):
+            for h in range(2):
+                etas[t, h] = whole_etas[t][:, half(h)]
+                positives[t, h] = whole_positives[t][:, half(h)]
 
         def gate(t, za):
             for a in range(PASSES):
@@ -261,16 +260,16 @@ def tile_list_rgg_reluP_kernel(
         positive_part(2, 0, bank(5))
         second_half(0, bank(0), bank(7))
 
-        gated = placed("first_gated", [P, LAST * HALF], F32, grouped_at + 2 * HALF)
+        gated = placed("first_gated", [P, J], F32, grouped_at + 2 * HALF)
         nc.gpsimd.tensor_tensor(gated[:, half(0)], etas[0, 0], gain[:, half(0)], ALU.mult)
         nc.vector.scalar_tensor_tensor(messages[0][:, half(0)], ms, 0.0, gated[:, half(0)], ALU.max, ALU.mult)
         nc.vector.tensor_copy(pages[0][:].indirect(list_half(TARGET, 0)), messages[0][:, half(0)])
 
-        gate(LAST, bank(1))
-        positive_part(LAST, 0, bank(2))
         second_half(1, bank(3), bank(4))
-        second_half(2, bank(1), bank(2))
-        second_half(LAST, bank(0), bank(7))
+        second_half(2, bank(1), bank(5))
+        gate(LAST, bank(2))
+        positive_part(LAST, 0, bank(7))
+        second_half(LAST, bank(0), bank(4))
 
         def weigh(weighted, values, cols):
             nc.gpsimd.tensor_tensor(weighted, values, gain[:, cols], ALU.mult)
@@ -289,16 +288,18 @@ def tile_list_rgg_reluP_kernel(
             nc.vector.tensor_copy(pages[t][:].indirect(offsets), messages[t][:, cols])
 
         out_rows = out_0.rearrange("(p t) c -> p t c", t=PACK)
-        weigh_two(gated[:, HALF:], first_etas[:, HALF:], 0)
-        for t in range(1, LAST):
-            place(t, half(0), list_half(TARGET, 0), gated[:, half(t)], positives[t, 0])
+        weigh(gated[:, half(1)], etas[1, 0], half(0))
+        place(1, half(0), list_half(TARGET, 0), gated[:, half(1)], positives[1, 0])
         weighted = held("weighted", [P, J], F32)
-        weigh_two(weighted[:], late_positives[:, 0:J], 1)
-        for t in range(LAST):
-            if t == 2:
-                weigh(weighted[:, half(0)], positives[t, 1], half(1))
-            place(t, half(1), list_half(TARGET, 1), weighted[:, half(t % 2)], etas[t, 1])
+        weigh_two(weighted[:], late_positives[:], 1)
+        for t in range(2):
+            place(t, half(1), list_half(TARGET, 1), weighted[:, half(t)], etas[t, 1])
             nc.sync.dma_start(out_rows[:, t, :], pages[t][:])
+        whole = slice(0, J)
+        page2_weighted = placed("page2_weighted", [P, J], F32, grouped_at + 2 * HALF)
+        weigh(page2_weighted[:], whole_positives[2], whole)
+        place(2, whole, lists[TARGET][:], page2_weighted[:], whole_etas[2])
+        nc.sync.dma_start(out_rows[:, 2, :], pages[2][:])
         pairs = placed("pairs", [P, 2 * T * 2], BF16, wc_codes_at)
         ahead = pairs[:, 2 * T + 3 * PAIRED : 2 * T + 3 * PAIRED + 2 * J].bitcast(F32)
 
@@ -318,8 +319,8 @@ def tile_list_rgg_reluP_kernel(
 
         for t in range(2):
             nc.scalar.copy(low_pair[:, :, t], pages[t][:])
-        weigh(ahead, last_positive[:], slice(0, J))
-        place(LAST, slice(0, J), lists[TARGET][:], ahead, last_eta[:])
+        weigh(ahead, whole_positives[LAST], whole)
+        place(LAST, whole, lists[TARGET][:], ahead, whole_etas[LAST])
         nc.sync.dma_start(out_rows[:, LAST, :], pages[LAST][:])
         pair_words = pairs[:].bitcast(U32).rearrange("p (u c) -> p c u", u=2)
         for first in range(0, T, PAIRED):

@@ -77,7 +77,8 @@ def tile_list_rgg_reluP_kernel(
         wc_raw2_at = wc_raw1_at + piece_bytes
         wa_raw_at = wc_raw2_at + piece_bytes
         wc_raw_last_at = wa_raw_at + operand_bytes
-        wc_codes_at = wc_raw_last_at + PACK * 4 * HALF
+        late_at = wc_raw_last_at + PACK * 4 * HALF
+        wc_codes_at = late_at + HALF
         wb_raw_at = wc_codes_at + 2 * page_bytes
 
         def placed(name, shape, dtype, offset, align=64):
@@ -90,11 +91,11 @@ def tile_list_rgg_reluP_kernel(
         pages = [held("page0", [P, T], F32)]
         nc.vector.memset(pages[0][:].bitcast(I32), 0)
 
-        nc.sync.dma_start(lists[SOURCE][:], offs)
         for w, scales in enumerate((wa_scales, wb_scales)):
             nc.sync.dma_start(
                 w_s_raw[rows_at:P, w * N : (w + 1) * N].bitcast(I32), scales.rearrange("a q n -> (a q) n").bitcast(I32)
             )
+        nc.sync.dma_start(lists[SOURCE][:], offs)
         for r in range(SCALE_ROWS):
             nc.sync.dma_start(tab_s[r:P:PASS_GAP, :].bitcast(I32), scale_rows(tab_scales, r))
         tab_w = held("tab_w", [P, T], I32)
@@ -166,7 +167,8 @@ def tile_list_rgg_reluP_kernel(
 
         early = ((SOURCE, 0), (SOURCE, 1), (TARGET, 0))
         pick_scales("early_second", held("early_both", [P, len(early) * HALF], U8), early, ((0, P - PASS_GAP),))
-        load_and_round_wc(1, N // 2, N, placed("wc_raw_last", piece, F32, wc_raw_last_at))
+        last_piece = placed("wc_raw_last", [P, (wc_codes_at - wc_raw_last_at) // 4], F32, wc_raw_last_at)
+        load_and_round_wc(1, N // 2, N, last_piece[:, 0 : piece_bytes // 4].rearrange("p (i n) -> p i n", i=PACK))
 
         def pick_words(h, words):
             for which in (SOURCE, TARGET):
@@ -181,15 +183,16 @@ def tile_list_rgg_reluP_kernel(
             tile = placed("parted0_%d" % which, [P, 1, PASSES, 2 * HALF], U8, wa_raw_at + which * operand_bytes // 2)
             part_words(tile[:], words[:, which : which + 1])
             parted[0, which] = tile[:, 0]
-        tile = held("parted1", [P, 2, PASSES, 2 * HALF], U8)
-        part_words(tile[:], pick_words(1, placed("picked_w1", [P, 2, HALF], I32, wb_raw_at))[:])
+        words = pick_words(1, placed("picked_w1", [P, 2, HALF], I32, wb_raw_at))
         for which in (SOURCE, TARGET):
-            parted[1, which] = tile[:, which]
+            tile = held("parted1_%d" % which, [P, 1, PASSES, 2 * HALF], U8)
+            part_words(tile[:], words[:, which : which + 1])
+            parted[1, which] = tile[:, 0]
         wc_codes = placed("wc_codes", [P, PASSES, N], U32, wc_codes_at)
         wc_s = held("wc_s", [P, PASSES, N], U8)
         for a in range(PASSES):
             nc.vector.quantize_mx(out=wc_codes[:, a, :].bitcast(FP8X4), scales=wc_s[:, a, :], in_=wc_grouped[:, a, :])
-        late_both = placed("late_both", [P, HALF], U8, grouped_at)
+        late_both = placed("late_both", [P, HALF], U8, late_at)
         pick_scales("late_second", late_both, ((TARGET, 1),), ((0, 64), (64, 32), (96, 16)))
 
         messages = [held("message%d" % t, [P, J], F32) for t in range(PACK)]

@@ -75,10 +75,10 @@ def tile_list_rgg_reluP_kernel(
         wc_raw0_at = page2_at + page_bytes
         wc_raw1_at = wc_raw0_at + piece_bytes
         wc_raw2_at = wc_raw1_at + piece_bytes
-        wa_raw_at = wc_raw2_at + piece_bytes
-        wc_raw_last_at = wa_raw_at + operand_bytes
+        wc_raw_last_at = wc_raw2_at + piece_bytes
         late_at = wc_raw_last_at + PACK * 4 * HALF
-        wc_codes_at = late_at + HALF
+        wa_raw_at = late_at + HALF
+        wc_codes_at = wa_raw_at + operand_bytes
         wb_raw_at = wc_codes_at + 2 * page_bytes
 
         def placed(name, shape, dtype, offset, align=64):
@@ -132,7 +132,7 @@ def tile_list_rgg_reluP_kernel(
             )
 
         piece = [P, PACK, N // 2]
-        wa_raw = placed("wa_raw", [P, operand_bytes + 64], U8, wa_raw_at)[:, 0 : PASSES * 2 * N].rearrange("p (a b) -> p a b", a=PASSES)
+        wa_raw = placed("wa_raw", [P, operand_bytes], U8, wa_raw_at)[:, 0 : PASSES * 2 * N].rearrange("p (a b) -> p a b", a=PASSES)
         nc.sync.dma_start(wa_raw.bitcast(I32), wa_words.rearrange("a p b -> p a b").bitcast(I32))
         wa_codes = held("wa_codes", [P, PASSES, 2 * N], U8)
         deal_columns(nc.scalar.copy, wa_codes[:].bitcast(U16), wa_raw.bitcast(U16), 2)
@@ -143,14 +143,19 @@ def tile_list_rgg_reluP_kernel(
         load_and_round_wc(0, 0, N // 2, placed("wc_raw0", piece, F32, wc_raw0_at))
         spread_weight_scales(0, 4)
         load_and_round_wc(0, N // 2, N, placed("wc_raw1", piece, F32, wc_raw1_at))
-        spread_weight_scales(4, 8)
         load_and_round_wc(1, 0, N // 2, placed("wc_raw2", piece, F32, wc_raw2_at))
+        last_piece = placed("wc_raw_last", [P, (wa_raw_at - wc_raw_last_at) // 4], F32, wc_raw_last_at)
+        load_and_round_wc(1, N // 2, N, last_piece[:, 0 : piece_bytes // 4].rearrange("p (i n) -> p i n", i=PACK))
+        spread_weight_scales(4, 8)
 
         picked_s = {}
         parted = {}
 
         def half(h):
             return slice(h * HALF, (h + 1) * HALF)
+
+        def quarter(c):
+            return slice(c * HALF // 2, (c + 1) * HALF // 2)
 
         def list_half(which, h):
             return lists[which][:, h * HALF // PER_COLUMN : (h + 1) * HALF // PER_COLUMN]
@@ -167,8 +172,6 @@ def tile_list_rgg_reluP_kernel(
 
         early = ((SOURCE, 0), (SOURCE, 1), (TARGET, 0))
         pick_scales("early_second", held("early_both", [P, len(early) * HALF], U8), early, ((0, P - PASS_GAP),))
-        last_piece = placed("wc_raw_last", [P, (wc_codes_at - wc_raw_last_at) // 4], F32, wc_raw_last_at)
-        load_and_round_wc(1, N // 2, N, last_piece[:, 0 : piece_bytes // 4].rearrange("p (i n) -> p i n", i=PACK))
 
         def pick_words(h, words):
             for which in (SOURCE, TARGET):
@@ -177,7 +180,7 @@ def tile_list_rgg_reluP_kernel(
 
         words = pick_words(0, held("picked_w0", [P, 2, HALF], I32))
 
-        gain = placed("gain", [P, J], F32, wc_raw1_at)
+        gain = placed("gain", [P, J], F32, wc_raw0_at)
         nc.sync.dma_start(gain[:], wgo)
         for which in (SOURCE, TARGET):
             tile = placed("parted0_%d" % which, [P, 1, PASSES, 2 * HALF], U8, wa_raw_at + which * operand_bytes // 2)
@@ -197,29 +200,29 @@ def tile_list_rgg_reluP_kernel(
 
         messages = [held("message%d" % t, [P, J], F32) for t in range(PACK)]
 
-        def table_operand(which, h, a):
-            return parted[h, which][:, a, :].bitcast(FP4X4), picked_s[which, h][a]
+        def table_operand(which, h, a, cols):
+            return parted[h, which][:, a, 2 * cols.start : 2 * cols.stop].bitcast(FP4X4), picked_s[which, h][a][:, cols]
 
         def bank(index, count=1):
             return psum.tile([P, count * HALF], F32, name="bank%d_%d" % (index, count), offset=index * 4 * HALF)[:, 0:HALF]
 
-        def source_pass(t, h, a, za):
-            v, v_s = table_operand(SOURCE, h, a)
+        def source_pass(t, h, a, za, cols=half(0)):
+            v, v_s = table_operand(SOURCE, h, a, cols)
             wb_cols = wb_codes[:, a, t * P : (t + 1) * P].bitcast(FP8X4)
             nc.tensor.matmul_mx(za, wb_cols, w_planes[a][:, WB * N + t * P : WB * N + (t + 1) * P], v, v_s, start=(a == 0), stop=False)
 
-        def target_pass(t, h, a, za):
-            v, v_s = table_operand(TARGET, h, a)
+        def target_pass(t, h, a, za, cols=half(0)):
+            v, v_s = table_operand(TARGET, h, a, cols)
             wa_cols = wa_codes[:, a, 2 * t * P : 2 * (t + 1) * P].bitcast(FP4X4)
             nc.tensor.matmul_mx(za, wa_cols, w_planes[a][:, WA * N + t * P : WA * N + (t + 1) * P], v, v_s, start=False, stop=(a == PASSES - 1))
 
-        def gate_pass(t, h, a, za):
-            source_pass(t, h, a, za)
-            target_pass(t, h, a, za)
+        def gate_pass(t, h, a, za, cols=half(0)):
+            source_pass(t, h, a, za, cols)
+            target_pass(t, h, a, za, cols)
 
         def message_pass(t, h, a, ms):
             m = slice(t * P, (t + 1) * P)
-            v, v_s = table_operand(SOURCE, h, a)
+            v, v_s = table_operand(SOURCE, h, a, half(0))
             nc.tensor.matmul_mx(ms, wc_codes[:, a, m].bitcast(FP8X4), wc_s[:, a, m], v, v_s, start=(a == PASSES - 1), stop=(a == 0))
 
         first_etas = placed("first_etas", [P, PACK * HALF], F32, wc_raw_last_at)
@@ -246,33 +249,46 @@ def tile_list_rgg_reluP_kernel(
                 message_pass(t, h, a, ms)
             nc.scalar.activation(positives[t, h], ms, ACT.Relu)
 
-        def second_half(t, za, ms):
-            positive_part(t, 1, ms)
+        def second_gate(t, za):
             for a in range(PASSES):
                 source_pass(t, 1, a, za)
             for a in range(PASSES):
                 target_pass(t, 1, a, za)
             nc.scalar.activation(etas[t, 1], za, ACT.Sigmoid)
 
-        for t in range(LAST):
-            gate(t, bank(t))
-        ms = bank(3)
+        def second_half(t, za, ms):
+            positive_part(t, 1, ms)
+            second_gate(t, za)
+
+        for c in range(2):
+            za = bank(c)[:, quarter(0)]
+            for a in range(PASSES):
+                gate_pass(0, 0, a, za, quarter(c))
+            nc.scalar.activation(etas[0, 0][:, quarter(c)], za, ACT.Sigmoid)
+        gate(1, bank(2, 5))
+        ms = bank(7)
         for a in reversed(range(PASSES)):
             message_pass(0, 0, a, ms)
-        positive_part(1, 0, bank(4))
-        positive_part(2, 0, bank(5))
-        second_half(0, bank(0), bank(7))
 
         gated = placed("first_gated", [P, J], F32, grouped_at + 2 * HALF)
-        nc.gpsimd.tensor_tensor(gated[:, half(0)], etas[0, 0], gain[:, half(0)], ALU.mult)
-        nc.vector.scalar_tensor_tensor(messages[0][:, half(0)], ms, 0.0, gated[:, half(0)], ALU.max, ALU.mult)
+        for c in range(2):
+            cols = quarter(c)
+            nc.gpsimd.tensor_tensor(gated[:, cols], etas[0, 0][:, cols], gain[:, cols], ALU.mult)
+            nc.vector.scalar_tensor_tensor(messages[0][:, cols], ms[:, cols], 0.0, gated[:, cols], ALU.max, ALU.mult)
         nc.vector.tensor_copy(pages[0][:].indirect(list_half(TARGET, 0)), messages[0][:, half(0)])
 
-        second_half(1, bank(3), bank(4))
-        second_half(2, bank(1), bank(5))
-        gate(LAST, bank(2))
-        positive_part(LAST, 0, bank(7))
-        second_half(LAST, bank(0), bank(4))
+        positive_part(1, 0, bank(0, 3))
+        positive_part(0, 1, bank(3, 4))
+        positive_part(1, 1, bank(0))
+        second_gate(0, bank(1))
+        positive_part(2, 0, bank(2))
+        second_gate(1, bank(3))
+        positive_part(2, 1, bank(4))
+        gate(2, bank(5))
+        second_gate(2, bank(0))
+        gate(LAST, bank(7))
+        positive_part(LAST, 0, bank(6))
+        second_half(LAST, bank(2), bank(4))
 
         def weigh(weighted, values, cols):
             nc.gpsimd.tensor_tensor(weighted, values, gain[:, cols], ALU.mult)

from contextlib import ExitStack

import concourse.mybir as mybir

K, N, T, J = 1024, 512, 2048, 1024
FLOPS = 3 * 2 * K * N * J

F32 = mybir.dt.float32
BF16 = mybir.dt.bfloat16
I32 = mybir.dt.int32
U32 = mybir.dt.uint32
U16 = mybir.dt.uint16
U8 = mybir.dt.uint8
FP8X4 = mybir.dt.float8_e4m3fn_x4
FP4X4 = mybir.dt.float4_e2m1fn_x4
ALU = mybir.AluOpType
ACT = mybir.ActivationFunctionType

P = 128
PACK = 4
PASSES = K // (P * PACK)
QUADRANT = 32
SCALE_ROWS = 4
PASS_GAP = 16
PER_COLUMN = 16
LINE = 16
HALF = 512
HALVES = J // HALF
ROUNDED = ((0, 512), (512, 1024), (1024, 1536), (1536, 1792), (1792, 2048))
QUANTISED = 256
STORED = 512
PAIRED = 512
WOVEN = ((0, 1024), (1024, 1536), (1536, 2048))
VECTOR_COLUMNS = 960
SOURCE, TARGET = 0, 1
WA, WB = 0, 1
LAST = PACK - 1


def tile_list_rgg_reluP_kernel(
    tc, tab_words, tab_scales, wa_words, wa_scales, wb_words, wb_scales, wc, wgo, offs, offs2, out_0, out_1, out_2
):
    nc = tc.nc
    with ExitStack() as ctx:
        keep = ctx.enter_context(tc.tile_pool(name="keep", bufs=1))
        overlay = ctx.enter_context(tc.tile_pool(name="overlay", bufs=1))
        psum = ctx.enter_context(tc.psum_pool(name="psum", bufs=1))

        def held(name, shape, dtype, tag=None):
            return keep.tile(shape, dtype, name=name, tag=tag or name, align_bytes=64)

        def scale_rows(scales, r):
            return scales.rearrange("a (q r) n -> r q a n", r=SCALE_ROWS)[r].bitcast(I32)

        def lift_second_pass(second, both, pieces):
            for first, count in pieces:
                nc.sync.dma_start(
                    second[first : first + count].bitcast(I32), both[first + PASS_GAP : first + PASS_GAP + count].bitcast(I32)
                )

        def deal_columns(copy, dealt, raw, element_bytes):
            i = LINE // element_bytes
            copy(
                dealt.rearrange("p a (t o i) -> p a o t i", t=PACK, i=i),
                raw.rearrange("p a (o i t) -> p a o t i", t=PACK, i=i),
            )

        lists = [keep.tile([P, J // PER_COLUMN], U16, name=name) for name in ("source_list", "target_list")]
        tab_s = held("tab_s", [P, T], U8)
        page_bytes = 4 * T
        operand_bytes = 4 * PASSES * N
        piece_bytes = 4 * PACK * (N // 2)
        grouped_at, page1_at = 0, page_bytes
        page2_at = page1_at + page_bytes
        wc_raw0_at = page2_at + page_bytes
        wc_raw1_at = wc_raw0_at + piece_bytes
        wc_raw2_at = wc_raw1_at + piece_bytes
        wc_raw_last_at = wc_raw2_at + piece_bytes
        late_at = wc_raw_last_at + PACK * 4 * HALF
        wa_raw_at = late_at + HALF
        wc_codes_at = wa_raw_at + operand_bytes
        wb_raw_at = wc_codes_at + 2 * page_bytes

        def placed(name, shape, dtype, offset, align=64):
            return overlay.tile(shape, dtype, name=name, offset=offset, align_bytes=align)

        w_s_raw = placed("w_s_raw", [P, wa_raw_at - page1_at], U8, page1_at)[:, 0 : 2 * N]
        rows_at = P - QUADRANT
        nc.vector.memset(tab_s[:].bitcast(I32), 0)
        nc.vector.memset(w_s_raw[0:rows_at].bitcast(I32), 0)
        pages = [held("page0", [P, T], F32)]
        nc.vector.memset(pages[0][:].bitcast(I32), 0)

        for w, scales in enumerate((wa_scales, wb_scales)):
            nc.sync.dma_start(
                w_s_raw[rows_at:P, w * N : (w + 1) * N].bitcast(I32), scales.rearrange("a q n -> (a q) n").bitcast(I32)
            )
        nc.sync.dma_start(lists[SOURCE][:], offs)
        for r in range(SCALE_ROWS):
            nc.sync.dma_start(tab_s[r:P:PASS_GAP, :].bitcast(I32), scale_rows(tab_scales, r))
        tab_w = held("tab_w", [P, T], I32)
        nc.sync.dma_start(tab_w[:], tab_words[0].rearrange("p t b -> p (t b)").bitcast(I32))
        nc.sync.dma_start(lists[TARGET][:], offs2)
        w_s = held("w_s", [P, 2, N], U8)
        deal_columns(nc.vector.tensor_copy, w_s[:], w_s_raw.rearrange("p (w n) -> p w n", w=2), 1)

        for t, offset in ((1, page1_at), (2, page2_at)):
            pages.append(placed("page%d" % t, [P, T], F32, offset))
            nc.gpsimd.memset(pages[t][:], 0.0)
        pages.append(pages[0])
        warm_out = held("warm_out", [P, 8], F32)
        nc.scalar.activation(warm_out[:], pages[0][:, 0:8], ACT.Sigmoid)

        wc_rows = wc.rearrange("(a p i) n -> a p i n", p=P, i=PACK)
        wc_grouped = placed("wc_grouped", [P, PASSES, N * PACK], BF16, grouped_at)
        w_planes = [held("w_plane%d" % a, [P, 2 * N], U8) for a in range(PASSES)]

        def spread_weight_scales(first, last):
            for index in range(first, last):
                a, q = divmod(index, P // QUADRANT)
                row = rows_at + PASS_GAP * a + SCALE_ROWS * q
                nc.sync.dma_start(
                    w_planes[a][QUADRANT * q : QUADRANT * q + SCALE_ROWS].bitcast(I32),
                    w_s[row : row + SCALE_ROWS].rearrange("p w n -> p (w n)").bitcast(I32),
                )

        def load_and_round_wc(a, n0, n1, raw):
            nc.sync.dma_start(raw[:], wc_rows[a][:, :, n0:n1])
            nc.scalar.copy(
                wc_grouped[:, a, :].rearrange("p (t m i) -> p m i t", t=PACK, i=PACK)[:, n0 // PACK : n1 // PACK],
                raw[:].rearrange("p i (m t) -> p m i t", t=PACK),
            )

        piece = [P, PACK, N // 2]
        wa_raw = placed("wa_raw", [P, operand_bytes], U8, wa_raw_at)[:, 0 : PASSES * 2 * N].rearrange("p (a b) -> p a b", a=PASSES)
        nc.sync.dma_start(wa_raw.bitcast(I32), wa_words.rearrange("a p b -> p a b").bitcast(I32))
        wa_codes = held("wa_codes", [P, PASSES, 2 * N], U8)
        deal_columns(nc.scalar.copy, wa_codes[:].bitcast(U16), wa_raw.bitcast(U16), 2)
        wb_raw = placed("wb_raw", [P, PASSES, N], I32, wb_raw_at)
        nc.sync.dma_start(wb_raw[:], wb_words.rearrange("a p n b -> p a (n b)").bitcast(I32))
        wb_codes = held("wb_codes", [P, PASSES, N], U32)
        deal_columns(nc.scalar.copy, wb_codes[:], wb_raw[:].bitcast(U32), 4)
        load_and_round_wc(0, 0, N // 2, placed("wc_raw0", piece, F32, wc_raw0_at))
        spread_weight_scales(0, 4)
        load_and_round_wc(0, N // 2, N, placed("wc_raw1", piece, F32, wc_raw1_at))
        load_and_round_wc(1, 0, N // 2, placed("wc_raw2", piece, F32, wc_raw2_at))
        last_piece = placed("wc_raw_last", [P, (wa_raw_at - wc_raw_last_at) // 4], F32, wc_raw_last_at)
        load_and_round_wc(1, N // 2, N, last_piece[:, 0 : piece_bytes // 4].rearrange("p (i n) -> p i n", i=PACK))
        spread_weight_scales(4, 8)

        picked_s = {}
        parted = {}

        def half(h):
            return slice(h * HALF, (h + 1) * HALF)

        def quarter(c):
            return slice(c * HALF // 2, (c + 1) * HALF // 2)

        def list_half(which, h):
            return lists[which][:, h * HALF // PER_COLUMN : (h + 1) * HALF // PER_COLUMN]

        def pick_scales(name, both, runs, pieces):
            second = held(name, [P, len(runs) * HALF], U8)
            for index, (which, h) in enumerate(runs):
                nc.vector.tensor_copy(both[:, half(index)], tab_s[:].indirect(list_half(which, h)))
                picked_s[which, h] = (both[:, half(index)], second[:, half(index)])
            lift_second_pass(second, both, pieces)

        def part_words(tile, picked):
            nc.vector.tensor_copy(tile.bitcast(U16), picked.bitcast(U16).rearrange("p w (j a) -> p w a j", a=PASSES))

        early = ((SOURCE, 0), (SOURCE, 1), (TARGET, 0))
        pick_scales("early_second", held("early_both", [P, len(early) * HALF], U8), early, ((0, P - PASS_GAP),))

        def pick_words(h, words):
            for which in (SOURCE, TARGET):
                nc.vector.tensor_copy(words[:, which, :].bitcast(U32), tab_w[:].bitcast(U32).indirect(list_half(which, h)))
            return words

        words = pick_words(0, held("picked_w0", [P, 2, HALF], I32))

        gain = placed("gain", [P, J], F32, wc_raw0_at)
        nc.sync.dma_start(gain[:], wgo)
        for which in (SOURCE, TARGET):
            tile = placed("parted0_%d" % which, [P, 1, PASSES, 2 * HALF], U8, wa_raw_at + which * operand_bytes // 2)
            part_words(tile[:], words[:, which : which + 1])
            parted[0, which] = tile[:, 0]
        words = pick_words(1, placed("picked_w1", [P, 2, HALF], I32, wb_raw_at))
        for which in (SOURCE, TARGET):
            tile = held("parted1_%d" % which, [P, 1, PASSES, 2 * HALF], U8)
            part_words(tile[:], words[:, which : which + 1])
            parted[1, which] = tile[:, 0]
        wc_codes = placed("wc_codes", [P, PASSES, N], U32, wc_codes_at)
        wc_s = held("wc_s", [P, PASSES, N], U8)
        for a in range(PASSES):
            nc.vector.quantize_mx(out=wc_codes[:, a, :].bitcast(FP8X4), scales=wc_s[:, a, :], in_=wc_grouped[:, a, :])
        late_both = placed("late_both", [P, HALF], U8, late_at)
        pick_scales("late_second", late_both, ((TARGET, 1),), ((0, 64), (64, 32), (96, 16)))

        messages = [held("message%d" % t, [P, J], F32) for t in range(PACK)]

        def table_operand(which, h, a, cols):
            return parted[h, which][:, a, 2 * cols.start : 2 * cols.stop].bitcast(FP4X4), picked_s[which, h][a][:, cols]

        def bank(index, count=1):
            return psum.tile([P, count * HALF], F32, name="bank%d_%d" % (index, count), offset=index * 4 * HALF)[:, 0:HALF]

        def source_pass(t, h, a, za, cols=half(0)):
            v, v_s = table_operand(SOURCE, h, a, cols)
            wb_cols = wb_codes[:, a, t * P : (t + 1) * P].bitcast(FP8X4)
            nc.tensor.matmul_mx(za, wb_cols, w_planes[a][:, WB * N + t * P : WB * N + (t + 1) * P], v, v_s, start=(a == 0), stop=False)

        def target_pass(t, h, a, za, cols=half(0)):
            v, v_s = table_operand(TARGET, h, a, cols)
            wa_cols = wa_codes[:, a, 2 * t * P : 2 * (t + 1) * P].bitcast(FP4X4)
            nc.tensor.matmul_mx(za, wa_cols, w_planes[a][:, WA * N + t * P : WA * N + (t + 1) * P], v, v_s, start=False, stop=(a == PASSES - 1))

        def gate_pass(t, h, a, za, cols=half(0)):
            source_pass(t, h, a, za, cols)
            target_pass(t, h, a, za, cols)

        def message_pass(t, h, a, ms):
            m = slice(t * P, (t + 1) * P)
            v, v_s = table_operand(SOURCE, h, a, half(0))
            nc.tensor.matmul_mx(ms, wc_codes[:, a, m].bitcast(FP8X4), wc_s[:, a, m], v, v_s, start=(a == PASSES - 1), stop=(a == 0))

        first_etas = placed("first_etas", [P, PACK * HALF], F32, wc_raw_last_at)
        late_positives = held("late_positives", [P, J], F32)
        etas, positives = {}, {(1, 0): held("positive1", [P, HALF], F32)[:]}
        for t in range(2):
            etas[t, 0] = first_etas[:, half(t)]
            etas[t, 1] = held("eta%d" % t, [P, HALF], F32)[:]
            positives[t, 1] = late_positives[:, half(t)]
        whole_etas = {2: first_etas[:, J:], LAST: held("last_eta", [P, J], F32)[:]}
        whole_positives = {t: held("positive%d" % t, [P, J], F32)[:] for t in (2, LAST)}
        for t in (2, LAST):
            for h in range(2):
                etas[t, h] = whole_etas[t][:, half(h)]
                positives[t, h] = whole_positives[t][:, half(h)]

        def gate(t, za):
            for a in range(PASSES):
                gate_pass(t, 0, a, za)
            nc.scalar.activation(etas[t, 0], za, ACT.Sigmoid)

        def positive_part(t, h, ms):
            for a in reversed(range(PASSES)):
                message_pass(t, h, a, ms)
            nc.scalar.activation(positives[t, h], ms, ACT.Relu)

        def second_gate(t, za):
            for a in range(PASSES):
                source_pass(t, 1, a, za)
            for a in range(PASSES):
                target_pass(t, 1, a, za)
            nc.scalar.activation(etas[t, 1], za, ACT.Sigmoid)

        def second_half(t, za, ms):
            positive_part(t, 1, ms)
            second_gate(t, za)

        for c in range(2):
            za = bank(c)[:, quarter(0)]
            for a in range(PASSES):
                gate_pass(0, 0, a, za, quarter(c))
            nc.scalar.activation(etas[0, 0][:, quarter(c)], za, ACT.Sigmoid)
        gate(1, bank(2, 5))
        ms = bank(7)
        for a in reversed(range(PASSES)):
            message_pass(0, 0, a, ms)

        gated = placed("first_gated", [P, J], F32, grouped_at + 2 * HALF)
        for c in range(2):
            cols = quarter(c)
            nc.gpsimd.tensor_tensor(gated[:, cols], etas[0, 0][:, cols], gain[:, cols], ALU.mult)
            nc.vector.scalar_tensor_tensor(messages[0][:, cols], ms[:, cols], 0.0, gated[:, cols], ALU.max, ALU.mult)
        nc.vector.tensor_copy(pages[0][:].indirect(list_half(TARGET, 0)), messages[0][:, half(0)])

        positive_part(1, 0, bank(0, 3))
        positive_part(0, 1, bank(3, 4))
        positive_part(1, 1, bank(0))
        second_gate(0, bank(1))
        positive_part(2, 0, bank(2))
        second_gate(1, bank(3))
        positive_part(2, 1, bank(4))
        gate(2, bank(5))
        second_gate(2, bank(0))
        gate(LAST, bank(7))
        positive_part(LAST, 0, bank(6))
        second_half(LAST, bank(2), bank(4))

        def weigh(weighted, values, cols):
            nc.gpsimd.tensor_tensor(weighted, values, gain[:, cols], ALU.mult)

        def weigh_two(weighted, values, h):
            shape = [P, 2, HALF]
            nc.gpsimd.tensor_tensor(
                weighted.rearrange("p (u j) -> p u j", u=2),
                values.rearrange("p (u j) -> p u j", u=2),
                gain[:, half(h)].unsqueeze(1).to_broadcast(shape),
                ALU.mult,
            )

        def place(t, cols, offsets, weighted, other):
            nc.gpsimd.tensor_tensor(messages[t][:, cols], weighted, other, ALU.mult)
            nc.vector.tensor_copy(pages[t][:].indirect(offsets), messages[t][:, cols])

        out_rows = out_0.rearrange("(p t) c -> p t c", t=PACK)
        weigh(gated[:, half(1)], etas[1, 0], half(0))
        place(1, half(0), list_half(TARGET, 0), gated[:, half(1)], positives[1, 0])
        weighted = held("weighted", [P, J], F32)
        weigh_two(weighted[:], late_positives[:], 1)
        for t in range(2):
            place(t, half(1), list_half(TARGET, 1), weighted[:, half(t)], etas[t, 1])
            nc.sync.dma_start(out_rows[:, t, :], pages[t][:])
        whole = slice(0, J)
        page2_weighted = placed("page2_weighted", [P, J], F32, grouped_at + 2 * HALF)
        weigh(page2_weighted[:], whole_positives[2], whole)
        place(2, whole, lists[TARGET][:], page2_weighted[:], whole_etas[2])
        nc.sync.dma_start(out_rows[:, 2, :], pages[2][:])
        pairs = placed("pairs", [P, 2 * T * 2], BF16, wc_codes_at)
        ahead = pairs[:, 2 * T + 3 * PAIRED : 2 * T + 3 * PAIRED + 2 * J].bitcast(F32)

        low_pair, high_pair = [pairs[:, u * T * 2 : (u + 1) * T * 2].rearrange("p (c e) -> p c e", e=2) for u in range(2)]
        rounded = held("rounded", [P, T * PACK], BF16)

        def columns(first, last):
            return rounded[:, first * PACK : last * PACK].rearrange("p (c t) -> p c t", t=PACK), slice(first, last)

        def pieces(first, last):
            found = []
            for c0, c1 in ROUNDED:
                lo, hi = max(first, c0), min(last, c1)
                if lo < hi:
                    found.append(columns(lo, hi))
            return found

        for t in range(2):
            nc.scalar.copy(low_pair[:, :, t], pages[t][:])
        weigh(ahead, whole_positives[LAST], whole)
        place(LAST, whole, lists[TARGET][:], ahead, whole_etas[LAST])
        nc.sync.dma_start(out_rows[:, LAST, :], pages[LAST][:])
        pair_words = pairs[:].bitcast(U32).rearrange("p (u c) -> p c u", u=2)
        for first in range(0, T, PAIRED):
            cols = slice(first, first + PAIRED)
            twice = pages[2][:, cols].unsqueeze(2).to_broadcast([P, PAIRED, 2])
            if first == 0:
                nc.scalar.copy(high_pair[:, cols], twice)
            else:
                nc.gpsimd.tensor_scalar(high_pair[:, cols], twice, 1.0, -0.0, ALU.mult, ALU.add)
        for first, last in WOVEN:
            view, cols = columns(first, last)
            both_words = view.rearrange("p c t -> p (c t)").bitcast(U32).rearrange("p (c u) -> p c u", u=2)
            nc.scalar.copy(both_words, pair_words[:, cols])
        for view, cols in pieces(0, VECTOR_COLUMNS):
            nc.vector.tensor_copy(view[:, :, LAST], pages[LAST][:, cols])
        for view, cols in pieces(VECTOR_COLUMNS, T):
            nc.scalar.copy(view[:, :, LAST], pages[LAST][:, cols])

        y_s = held("y_s", [P, STORED], U8)
        out_words = out_1[0].rearrange("p t b -> p (t b)").bitcast(I32)
        for c in range(T // STORED):
            y_codes = held("y_codes%d" % c, [P, STORED], I32)
            for first in range(0, STORED, QUANTISED):
                cols = slice(first, first + QUANTISED)
                c0 = c * STORED + first
                nc.vector.quantize_mx(
                    out=y_codes[:, cols].bitcast(FP8X4), scales=y_s[SCALE_ROWS * c : P, cols], in_=rounded[:, c0 * PACK : (c0 + QUANTISED) * PACK]
                )
            nc.sync.dma_start(out_words[:, c * STORED : (c + 1) * STORED], y_codes[:])
        for q in range(P // QUADRANT):
            rows = y_s[QUADRANT * q : QUADRANT * q + SCALE_ROWS * (T // STORED), :]
            stored = out_2[0, SCALE_ROWS * q : SCALE_ROWS * (q + 1), :].rearrange("r (c n) -> c r n", n=STORED)
            (nc.scalar, nc.sync)[q % 2].dma_start(stored.bitcast(I32), rows.bitcast(I32))
